import numpy as np
import ml_dtypes


def mxq(x, axis, fmt="e4m3"):
    dtype, down = {"e4m3": (ml_dtypes.float8_e4m3fn, 7), "e5m2": (ml_dtypes.float8_e5m2, 14)}[fmt]
    v = np.moveaxis(np.asarray(x, np.float32).astype(ml_dtypes.bfloat16).astype(np.float64), axis, -1)
    blocks = v.reshape(v.shape[:-1] + (-1, 32))
    amax = np.abs(blocks).max(-1, keepdims=True)
    byte = np.maximum(np.where(amax > 0, np.frexp(amax)[1] - 1 + 127, 0) - down, 1)
    scale = np.exp2(byte - 127.0)
    codes = (blocks / scale).astype(np.float32).astype(dtype).astype(np.float64)
    return np.moveaxis((codes * scale).reshape(v.shape), -1, axis)


WIDE = False


def mx_kscale(k):
    if not WIDE:
        return np.ones(k)
    levels = np.array([10, -10, 5, -5, 0])
    if k % 512:
        return np.exp2(np.random.permutation(np.resize(levels, k // 32))).repeat(32)
    a = np.empty((k // 512, 16))
    for p in range(k // 512):
        a[p, :8] = np.random.permutation(np.resize(levels, 8))
        for g in range(8):
            far = levels[np.abs(levels - a[p, g]) >= 10]
            a[p, g + 8] = far[np.random.randint(len(far))]
    return np.exp2(a.ravel()).repeat(32)


def f64(x):
    return np.asarray(x).astype(np.float64)


def striped(idx):
    return np.tile(idx.reshape(-1, 16).T, (8, 1)).astype(np.uint16)


def unstriped(offs):
    return offs[:16].T.reshape(-1).astype(np.int64)


E2M1 = np.array([0.0, 0.5, 1.0, 1.5, 2.0, 3.0, 4.0, 6.0, -0.0, -0.5, -1.0, -1.5, -2.0, -3.0, -4.0, -6.0])


def pack_weight(w, fmt):
    k, n = w.shape
    w = f64(np.asarray(w, np.float32).astype(ml_dtypes.bfloat16)).reshape(k // 32, 32, n)
    amax = np.abs(w).max(1)
    if fmt == "e4m3":
        byte = np.frexp(amax)[1] - 1 + 127 - 7
    else:
        mant, ex = np.frexp(amax / 6.0)
        byte = np.where(mant > 0.5, ex, ex - 1) + 127
    byte = np.clip(np.where(amax > 0, byte, 1), 1, 254)
    scaled = (w * np.exp2(127.0 - byte)[:, None, :]).reshape(k, n).astype(np.float32)
    by_word = np.ascontiguousarray(scaled.reshape(k // 512, 128, 4, n).transpose(0, 1, 3, 2))
    if fmt == "e4m3":
        words = by_word.astype(ml_dtypes.float8_e4m3fn).view(np.uint8)
    else:
        c = by_word.astype(ml_dtypes.float4_e2m1fn).view(np.uint8) & 0xF
        words = (c[..., 0::2] | (c[..., 1::2] << 4)).reshape(k // 512, 128, 2 * n)
    return np.ascontiguousarray(words), np.ascontiguousarray(byte.astype(np.uint8).reshape(k // 512, 16, n))


def unpack_weight(words, scales, fmt):
    g, _, n = scales.shape
    words = np.ascontiguousarray(words).reshape(g, 128, n, -1)
    if fmt == "e4m3":
        vals = words.view(ml_dtypes.float8_e4m3fn).astype(np.float64)
    else:
        nib = np.empty((g, 128, n, 4), np.uint8)
        nib[..., 0::2] = words & 0xF
        nib[..., 1::2] = words >> 4
        vals = E2M1[nib]
    vals = vals * np.repeat(np.exp2(scales.astype(np.float64) - 127.0), 8, axis=1)[..., None]
    return vals.transpose(0, 1, 3, 2).reshape(g * 512, n)


def gelu(v):
    return 0.5 * v * (1.0 + np.tanh(np.sqrt(2.0 / np.pi) * (v + 0.044715 * v**3)))


def bf(x):
    return np.asarray(x, np.float32).astype(ml_dtypes.bfloat16)

def planes(Y):
    n, m = Y.shape
    b = f64(bf(Y)).reshape(n // 32, 32, m)
    amax = np.abs(b).max(1)
    byte = np.clip(np.where(amax > 0, np.frexp(amax)[1] - 1 + 127 - 7, 1), 1, 254)
    codes = (b * np.exp2(127.0 - byte)[:, None, :]).reshape(n, m).astype(np.float32).astype(ml_dtypes.float8_e4m3fn).view(np.uint8)
    words = codes.reshape(n // 512, 128, 4, m).transpose(0, 1, 3, 2)
    return np.ascontiguousarray(words), np.ascontiguousarray(byte.astype(np.uint8).reshape(n // 512, 16, m))


K, T, S, P, H, N = 1024, 4096, 1024, 512, 1024, 1024

def setup_inputs():
    n = np.random.standard_normal
    s = mx_kscale(K)[:, None]
    u = mx_kscale(H)[:, None]
    tab_words, tab_scales = pack_weight(n((K, T)) * s, "e4m3")
    w1 = n((K, H)) * 2.0 / np.sqrt(K) / s
    g = np.exp(0.3 * n(H)) * u[:, 0]
    w2_words, w2_scales = pack_weight(n((H, N)) * np.exp(0.8 * n(N)) / np.sqrt(H) / u, "e2m1")
    return {
        "tab_words": tab_words, "tab_scales": tab_scales,
        "offs": striped(np.random.permutation(T)[:S]),
        "w1": w1.astype(np.float32),
        "pos1": striped(np.random.permutation(S)[:P]),
        "pos2": striped(np.random.permutation(S)[:P]),
        "g": g.astype(np.float32),
        "w2_words": w2_words, "w2_scales": w2_scales,
    }

def reference(tab_words, tab_scales, offs, w1, pos1, pos2, g, w2_words, w2_scales):
    v = unpack_weight(tab_words, tab_scales, "e4m3")[:, unstriped(offs)]
    w2 = unpack_weight(w2_words, w2_scales, "e2m1")
    h = 1.0 / (1.0 + np.exp(-(mxq(f64(w1), 0, "e4m3").T @ v)))
    a = h[:, unstriped(pos1)]
    b = h[:, unstriped(pos2)]
    z = (a + b - a * b) * f64(g)[:, None]
    y = w2.T @ mxq(z, 0, "e4m3")
    words, scales = planes(y)
    return y, words, scales

@@ -1,0 +1,273 @@
+from contextlib import ExitStack
+
+import concourse.mybir as mybir
+
+K, T, S, G, H, N = 1024, 4096, 1024, 512, 1024, 1024
+FLOPS = 2 * K * H * S + 2 * H * N * G
+
+F32 = mybir.dt.float32
+BF16 = mybir.dt.bfloat16
+I32 = mybir.dt.int32
+U32 = mybir.dt.uint32
+U16 = mybir.dt.uint16
+U8 = mybir.dt.uint8
+FP8X4 = mybir.dt.float8_e4m3fn_x4
+FP4X4 = mybir.dt.float4_e2m1fn_x4
+ALU = mybir.AluOpType
+ACT = mybir.ActivationFunctionType
+
+P = 128
+PACK = 4
+PASS = P * PACK
+BANK = 512
+LANES = 16
+Y_COLS = 128
+GATE_CHUNKS = (128, 128, 128, 128)
+W1_PIECES = 4
+
+
+def tile_list_fault_tree_risk_kernel(
+    tc, tab_words, tab_scales, offs, w1, pos1, pos2, g, w2_words, w2_scales, out_0, out_1, out_2
+):
+    nc = tc.nc
+    with ExitStack() as ctx:
+        keep = ctx.enter_context(tc.tile_pool(name="keep", bufs=1))
+        psum = ctx.enter_context(tc.psum_pool(name="psum", bufs=8))
+
+        def held(name, shape, dtype):
+            return keep.tile(shape, dtype, name=name, align_bytes=64)
+
+        idx = keep.tile([P, S // LANES], U16, name="idx")
+        p1 = keep.tile([P, G // LANES], U16, name="p1")
+        p2 = keep.tile([P, G // LANES], U16, name="p2")
+        table = [held(f"table{a}", [P, T], U32) for a in range(2)]
+        table_scales = held("table_scales", [P, T], U8)
+        w1_raw = {(a, b): held(f"w1_raw{a}{b}", [P, PACK, PASS], F32) for a in range(2) for b in range(2)}
+        w2_raw = held("w2_raw", [P, 2, 2 * N], U8)
+        w2_scales_raw = held("w2_scales_raw", [P, 2, N], U8)
+        severity = held("severity", [P, 2, PACK], F32)
+
+        def load_w1(a, b):
+            rows = w1[a * PASS : (a + 1) * PASS, b * PASS : (b + 1) * PASS]
+            nc.sync.dma_start(w1_raw[a, b][:], rows.rearrange("(p j) c -> p j c", j=PACK))
+
+        def load_table(a):
+            nc.sync.dma_start(table[a][:].bitcast(I32), tab_words[a].rearrange("p n i -> p (n i)").bitcast(I32))
+
+        nc.vector.memset(table_scales[:].bitcast(I32), 0)
+        nc.vector.memset(w2_scales_raw[:].rearrange("p a c -> p (a c)").bitcast(I32), 0)
+
+        nc.sync.dma_start(idx[:], offs)
+        load_w1(0, 0)
+        for q in range(4):
+            nc.sync.dma_start(
+                table_scales[32 * q : 32 * q + 8, :].bitcast(I32), tab_scales[:, 4 * q : 4 * q + 4, :].bitcast(I32)
+            )
+        load_w1(1, 0)
+        load_table(0)
+        for q in range(4):
+            nc.sync.dma_start(
+                w2_scales_raw[32 * q : 32 * q + 4, :, :].bitcast(I32),
+                w2_scales[:, 4 * q : 4 * q + 4, :].rearrange("a r c -> r a c").bitcast(I32),
+            )
+        nc.sync.dma_start(w2_raw[:].bitcast(I32), w2_words.rearrange("a p c -> p a c").bitcast(I32))
+        load_table(1)
+        nc.sync.dma_start(p1[:], pos1)
+        nc.sync.dma_start(p2[:], pos2)
+        nc.sync.dma_start(severity[:], g.rearrange("(b p t) -> p b t", b=2, t=PACK))
+        load_w1(0, 1)
+        load_w1(1, 1)
+
+        w1_bf = {key: held(f"w1_bf{key[0]}{key[1]}", [P, PACK * P * PACK], BF16) for key in w1_raw}
+        w1_codes = {key: held(f"w1_codes{key[0]}{key[1]}", [P, PASS], U32) for key in w1_raw}
+        w1_scales = {key: held(f"w1_scales{key[0]}{key[1]}", [P, PASS], U8) for key in w1_raw}
+
+        def round_w1(a, b, piece):
+            ms = slice(piece * P // W1_PIECES, (piece + 1) * P // W1_PIECES)
+            dealt = w1_bf[a, b][:].rearrange("p (t m j) -> p m j t", t=PACK, j=PACK)
+            raw = w1_raw[a, b][:].rearrange("p j (m t) -> p m j t", t=PACK)
+            nc.scalar.copy(dealt[:, ms], raw[:, ms])
+
+        def quantize_w1(a, b):
+            nc.vector.quantize_mx(out=w1_codes[a, b][:].bitcast(FP8X4), scales=w1_scales[a, b][:], in_=w1_bf[a, b][:])
+
+        for a in range(2):
+            for piece in range(W1_PIECES):
+                round_w1(a, 0, piece)
+            quantize_w1(a, 0)
+
+        picked_scales = held("picked_scales", [P, S], U8)
+        nc.vector.tensor_copy(picked_scales[:], table_scales[:].indirect(idx[:]))
+        picked = {(a, half): held(f"picked{a}{half}", [P, BANK], U32) for a in range(2) for half in range(2)}
+
+        def pick_words(a):
+            for half in range(2):
+                entries = idx[:, half * BANK // LANES : (half + 1) * BANK // LANES]
+                nc.vector.tensor_copy(picked[a, half][:], table[a][:].indirect(entries))
+
+        pick_words(0)
+
+        w2_dealt = held("w2_dealt", [P, 4, PACK, 2 * P], U8)
+        w2_scales_dealt = held("w2_scales_dealt", [P, 4, PACK, P], U8)
+        nc.vector.tensor_copy(
+            w2_dealt[:].bitcast(U16),
+            w2_raw[:].bitcast(U16).rearrange("p a (n m t) -> p (a n) t m", n=2, t=PACK),
+        )
+        nc.vector.tensor_copy(
+            w2_scales_dealt[:], w2_scales_raw[:].rearrange("p a (n m t) -> p (a n) t m", n=2, t=PACK)
+        )
+
+        pick_words(1)
+
+        h = {(b, t): held(f"h{b}{t}", [P, S], F32) for b in range(2) for t in range(PACK)}
+
+        def failure_probabilities(b, t):
+            cols = slice(t * P, (t + 1) * P)
+            for half in range(2):
+                bank = psum.tile([P, BANK], F32, name="bank")
+                for a in range(2):
+                    nc.tensor.matmul_mx(
+                        out=bank[:],
+                        lhsT=w1_codes[a, b][:, cols].bitcast(FP8X4),
+                        lhsT_scale=w1_scales[a, b][:, cols],
+                        rhs=picked[a, half][:].bitcast(FP8X4),
+                        rhs_scale=picked_scales[4 * a : P, half * BANK : (half + 1) * BANK],
+                        start=(a == 0),
+                        stop=(a == 1),
+                    )
+                nc.scalar.activation(h[b, t][:, half * BANK : (half + 1) * BANK], bank[:], ACT.Sigmoid)
+
+        first_rows = held("first_rows", [P, PACK + 1, G], F32)
+        second_rows = held("second_rows", [P, PACK + 1, G], F32)
+
+        def gate_tiles(name, width, shift):
+            return {
+                "first": first_rows[:, shift : shift + PACK, 0:width],
+                "second": second_rows[:, shift : shift + PACK, 0:width],
+                "z": held(f"z{name}", [P, width * PACK], BF16),
+                "codes": held(f"z_codes{name}", [P, width], U32),
+                "scales": held(f"z_scales{name}", [P, width], U8),
+            }
+
+        def fetch(dst, b, t, places, m0, width):
+            entries = places[:, m0 // LANES : (m0 + width) // LANES]
+            nc.vector.tensor_copy(dst[:, t, :], h[b, t][:].indirect(entries))
+
+        def weigh_first(tiles, b, t):
+            first = tiles["first"][:, t, :]
+            nc.scalar.activation(first, first, ACT.Copy, scale=severity[:, b, t : t + 1])
+
+        def cross_term(tiles, b, t):
+            second = tiles["second"][:, t, :]
+            nc.vector.scalar_tensor_tensor(
+                out=second,
+                in0=tiles["first"][:, t, :],
+                scalar=severity[:, b, t : t + 1],
+                in1=second,
+                op0=ALU.subtract,
+                op1=ALU.mult,
+            )
+
+        def join(tiles):
+            nc.vector.tensor_tensor(
+                out=tiles["z"][:].rearrange("p (c i t) -> p c t i", i=2, t=PACK),
+                in0=tiles["first"].rearrange("p t (c i) -> p c t i", i=2),
+                in1=tiles["second"].rearrange("p t (c i) -> p c t i", i=2),
+                op=ALU.subtract,
+            )
+
+        def quantize_z(tiles):
+            nc.vector.quantize_mx(out=tiles["codes"][:].bitcast(FP8X4), scales=tiles["scales"][:], in_=tiles["z"][:])
+
+        lower = gate_tiles("lower", G, 0)
+        failure_probabilities(0, 0)
+        for t in range(PACK):
+            fetch(lower["first"], 0, t, p1, 0, G)
+            if t > 0:
+                cross_term(lower, 0, t - 1)
+            fetch(lower["second"], 0, t, p2, 0, G)
+            if t + 1 < PACK:
+                failure_probabilities(0, t + 1)
+            weigh_first(lower, 0, t)
+            for piece in range(W1_PIECES // 2):
+                round_w1(t // 2, 1, (t % 2) * (W1_PIECES // 2) + piece)
+            if t % 2 == 1:
+                quantize_w1(t // 2, 1)
+        cross_term(lower, 0, PACK - 1)
+        failure_probabilities(1, PACK - 1)
+        failure_probabilities(1, 0)
+        join(lower)
+        quantize_z(lower)
+
+        y_codes = held("y_codes", [P, 2, G], U32)
+        y_scales = held("y_scales", [P, 2, G], U8)
+
+        def risk_passes(bank, n, a, codes, scales):
+            for t in range(PACK):
+                nc.tensor.matmul_mx(
+                    out=bank[:, t, :],
+                    lhsT=w2_dealt[:, 2 * a + n, t, :].bitcast(FP4X4),
+                    lhsT_scale=w2_scales_dealt[:, 2 * a + n, t, :],
+                    rhs=codes.bitcast(FP8X4),
+                    rhs_scale=scales,
+                    start=(a == 0 and t == 0),
+                    stop=(a == 1 and t == PACK - 1),
+                )
+
+        def risk_scores(upper, m0, width, last):
+            for n in range(2):
+                y = held(f"y{m0}_{n}", [P, PACK, width], F32)
+                y_bf = held(f"y_bf{m0}_{n}", [P, width, PACK], BF16)
+                for c0 in range(0, width, Y_COLS):
+                    local = slice(c0, c0 + Y_COLS)
+                    whole = slice(m0 + c0, m0 + c0 + Y_COLS)
+                    bank = psum.tile([P, PACK, Y_COLS], F32, name="bank")
+                    risk_passes(bank, n, 0, lower["codes"][:, whole], lower["scales"][:, whole])
+                    risk_passes(bank, n, 1, upper["codes"][:, local], upper["scales"][:, local])
+                    if last and n == 1:
+                        nc.vector.tensor_copy(y[:, :, local], bank[:])
+                        nc.vector.tensor_copy(
+                            y_bf[:, local, :].rearrange("p (c i) t -> p c t i", i=PACK),
+                            y[:, :, local].rearrange("p t (c i) -> p c t i", i=PACK),
+                        )
+                    else:
+                        nc.scalar.copy(y_bf[:, local, :], bank[:].rearrange("p t m -> p m t"))
+                        nc.scalar.copy(y[:, :, local], bank[:])
+                rows = out_0[n * PASS : (n + 1) * PASS, m0 : m0 + width]
+                nc.sync.dma_start(rows.rearrange("(p t) m -> p t m", t=PACK), y[:])
+                nc.vector.quantize_mx(
+                    out=y_codes[:, n, m0 : m0 + width].bitcast(FP8X4),
+                    scales=y_scales[:, n, m0 : m0 + width],
+                    in_=y_bf[:].rearrange("p m t -> p (m t)"),
+                )
+            words = out_1.rearrange("n p m t -> p n (m t)").bitcast(I32)
+            nc.sync.dma_start(words[:, :, m0 : m0 + width], y_codes[:, :, m0 : m0 + width].bitcast(I32))
+
+        m0 = 0
+        waiting = None
+        for chunk, width in enumerate(GATE_CHUNKS):
+            shift = (chunk + 1) % 2
+            upper = gate_tiles(f"upper{m0}", width, shift)
+            order = [(t - shift) % PACK for t in range(PACK)]
+            for step, t in enumerate(order):
+                fetch(upper["first"], 1, t, p1, m0, width)
+                if step > 0:
+                    cross_term(upper, 1, order[step - 1])
+                fetch(upper["second"], 1, t, p2, m0, width)
+                weigh_first(upper, 1, t)
+                if chunk == 0 and step + 2 < PACK:
+                    failure_probabilities(1, order[step + 2])
+            cross_term(upper, 1, order[-1])
+            join(upper)
+            if waiting is not None:
+                risk_scores(*waiting, False)
+            quantize_z(upper)
+            waiting = (upper, m0, width)
+            m0 = m0 + width
+        risk_scores(*waiting, True)
+
+        for q in range(4):
+            nc.sync.dma_start(
+                out_2[:, 4 * q : 4 * q + 4, :].rearrange("n r m -> r n m").bitcast(I32),
+                y_scales[32 * q : 32 * q + 4, :, :].bitcast(I32),
+            )

@@ -23,7 +23,6 @@ BANK = 512
 LANES = 16
 Y_COLS = 128
 GATE_CHUNKS = (128, 128, 128, 128)
-W1_PIECES = 4
 
 
 def tile_list_fault_tree_risk_kernel(
@@ -32,6 +31,7 @@ def tile_list_fault_tree_risk_kernel(
     nc = tc.nc
     with ExitStack() as ctx:
         keep = ctx.enter_context(tc.tile_pool(name="keep", bufs=1))
+        ring = ctx.enter_context(tc.tile_pool(name="ring", bufs=2))
         psum = ctx.enter_context(tc.psum_pool(name="psum", bufs=8))
 
         def held(name, shape, dtype):
@@ -58,46 +58,38 @@ def tile_list_fault_tree_risk_kernel(
         nc.vector.memset(w2_scales_raw[:].rearrange("p a c -> p (a c)").bitcast(I32), 0)
 
         nc.sync.dma_start(idx[:], offs)
-        load_w1(0, 0)
+        nc.sync.dma_start(severity[:], g.rearrange("(b p t) -> p b t", b=2, t=PACK))
+        nc.sync.dma_start(w2_raw[:].bitcast(I32), w2_words.rearrange("a p c -> p a c").bitcast(I32))
+        load_table(0)
         for q in range(4):
             nc.sync.dma_start(
                 table_scales[32 * q : 32 * q + 8, :].bitcast(I32), tab_scales[:, 4 * q : 4 * q + 4, :].bitcast(I32)
             )
+        load_w1(0, 0)
+        load_table(1)
+        nc.sync.dma_start(p1[:], pos1)
+        nc.sync.dma_start(p2[:], pos2)
         load_w1(1, 0)
-        load_table(0)
         for q in range(4):
             nc.sync.dma_start(
                 w2_scales_raw[32 * q : 32 * q + 4, :, :].bitcast(I32),
                 w2_scales[:, 4 * q : 4 * q + 4, :].rearrange("a r c -> r a c").bitcast(I32),
             )
-        nc.sync.dma_start(w2_raw[:].bitcast(I32), w2_words.rearrange("a p c -> p a c").bitcast(I32))
-        load_table(1)
-        nc.sync.dma_start(p1[:], pos1)
-        nc.sync.dma_start(p2[:], pos2)
-        nc.sync.dma_start(severity[:], g.rearrange("(b p t) -> p b t", b=2, t=PACK))
         load_w1(0, 1)
         load_w1(1, 1)
 
-        w1_bf = {key: held(f"w1_bf{key[0]}{key[1]}", [P, PACK * P * PACK], BF16) for key in w1_raw}
-        w1_codes = {key: held(f"w1_codes{key[0]}{key[1]}", [P, PASS], U32) for key in w1_raw}
-        w1_scales = {key: held(f"w1_scales{key[0]}{key[1]}", [P, PASS], U8) for key in w1_raw}
+        severity_rows = [held("severity_lower", [P, PACK, G], F32), held("severity_upper", [P, PACK, Y_COLS], F32)]
+        for b in range(2):
+            rows = severity_rows[b]
+            nc.vector.tensor_copy(rows[:], severity[:, b, :].unsqueeze(2).to_broadcast(list(rows.shape)))
 
-        def round_w1(a, b, piece):
-            ms = slice(piece * P // W1_PIECES, (piece + 1) * P // W1_PIECES)
-            dealt = w1_bf[a, b][:].rearrange("p (t m j) -> p m j t", t=PACK, j=PACK)
-            raw = w1_raw[a, b][:].rearrange("p j (m t) -> p m j t", t=PACK)
-            nc.scalar.copy(dealt[:, ms], raw[:, ms])
-
-        def quantize_w1(a, b):
-            nc.vector.quantize_mx(out=w1_codes[a, b][:].bitcast(FP8X4), scales=w1_scales[a, b][:], in_=w1_bf[a, b][:])
-
-        for a in range(2):
-            for piece in range(W1_PIECES):
-                round_w1(a, 0, piece)
-            quantize_w1(a, 0)
+        w2_dealt = held("w2_dealt", [P, 4, PACK, 2 * P], U8)
+        nc.vector.tensor_copy(
+            w2_dealt[:].bitcast(U16),
+            w2_raw[:].bitcast(U16).rearrange("p a (n m t) -> p (a n) t m", n=2, t=PACK),
+        )
 
         picked_scales = held("picked_scales", [P, S], U8)
-        nc.vector.tensor_copy(picked_scales[:], table_scales[:].indirect(idx[:]))
         picked = {(a, half): held(f"picked{a}{half}", [P, BANK], U32) for a in range(2) for half in range(2)}
 
         def pick_words(a):
@@ -105,19 +97,40 @@ def tile_list_fault_tree_risk_kernel(
                 entries = idx[:, half * BANK // LANES : (half + 1) * BANK // LANES]
                 nc.vector.tensor_copy(picked[a, half][:], table[a][:].indirect(entries))
 
-        pick_words(0)
+        w1_codes = {key: held(f"w1_codes{key[0]}{key[1]}", [P, PASS], U32) for key in w1_raw}
+        w1_scales = {key: held(f"w1_scales{key[0]}{key[1]}", [P, PASS], U8) for key in w1_raw}
 
-        w2_dealt = held("w2_dealt", [P, 4, PACK, 2 * P], U8)
-        w2_scales_dealt = held("w2_scales_dealt", [P, 4, PACK, P], U8)
-        nc.vector.tensor_copy(
-            w2_dealt[:].bitcast(U16),
-            w2_raw[:].bitcast(U16).rearrange("p a (n m t) -> p (a n) t m", n=2, t=PACK),
-        )
+        def round_w1(copy, rounded, a, b, ms, ts):
+            dealt = rounded[:].rearrange("p (t m j) -> p m j t", m=P, j=PACK)
+            raw = w1_raw[a, b][:].rearrange("p j (m t) -> p m j t", t=PACK)
+            copy(dealt[:, ms], raw[:, ms, :, ts])
+
+        def quantize_w1(rounded, a, b, ts):
+            cols = slice(ts.start * P, ts.stop * P)
+            nc.vector.quantize_mx(
+                out=w1_codes[a, b][:, cols].bitcast(FP8X4), scales=w1_scales[a, b][:, cols], in_=rounded[:]
+            )
+
+        every_t = slice(0, PACK)
+        t_pairs = (slice(0, 2), slice(2, 4))
+
+        pick_words(0)
+        nc.vector.tensor_copy(picked_scales[:], table_scales[:].indirect(idx[:]))
+        w1_first = held("w1_first", [P, PACK * PASS], BF16)
+        round_w1(nc.scalar.copy, w1_first, 0, 0, slice(0, P), every_t)
+        quantize_w1(w1_first, 0, 0, every_t)
+        pick_words(1)
+        w1_low = held("w1_low", [P, 2 * PASS], BF16)
+        w1_high = held("staged", [P, 2 * PASS], BF16)
+        round_w1(nc.vector.tensor_copy, w1_low, 1, 0, slice(0, P), t_pairs[0])
+        round_w1(nc.scalar.copy, w1_high, 1, 0, slice(0, P), t_pairs[1])
+        quantize_w1(w1_low, 1, 0, t_pairs[0])
+        quantize_w1(w1_high, 1, 0, t_pairs[1])
+
+        w2_scales_dealt = held("staged", [P, 4, PACK, P], U8)
         nc.vector.tensor_copy(
             w2_scales_dealt[:], w2_scales_raw[:].rearrange("p a (n m t) -> p (a n) t m", n=2, t=PACK)
         )
-
-        pick_words(1)
 
         h = {(b, t): held(f"h{b}{t}", [P, S], F32) for b in range(2) for t in range(PACK)}
 
@@ -137,65 +150,58 @@ def tile_list_fault_tree_risk_kernel(
                     )
                 nc.scalar.activation(h[b, t][:, half * BANK : (half + 1) * BANK], bank[:], ACT.Sigmoid)
 
-        first_rows = held("first_rows", [P, PACK + 1, G], F32)
-        second_rows = held("second_rows", [P, PACK + 1, G], F32)
-
-        def gate_tiles(name, width, shift):
+        def gate_tiles(pool, name, width):
             return {
-                "first": first_rows[:, shift : shift + PACK, 0:width],
-                "second": second_rows[:, shift : shift + PACK, 0:width],
+                "first": pool.tile([P, PACK, width], F32, name=f"first{width}"),
+                "rest": pool.tile([P, PACK, width], F32, name=f"rest{width}"),
+                "second": pool.tile([P, PACK, width], F32, name=f"second{width}"),
                 "z": held(f"z{name}", [P, width * PACK], BF16),
                 "codes": held(f"z_codes{name}", [P, width], U32),
                 "scales": held(f"z_scales{name}", [P, width], U8),
             }
 
-        def fetch(dst, b, t, places, m0, width):
+        def fetch_times(dst, factor, b, t, places, m0, width):
             entries = places[:, m0 // LANES : (m0 + width) // LANES]
-            nc.vector.tensor_copy(dst[:, t, :], h[b, t][:].indirect(entries))
+            nc.vector.tensor_tensor(out=dst[:, t, :], in0=h[b, t][:].indirect(entries), in1=factor[:, t, :], op=ALU.mult)
 
-        def weigh_first(tiles, b, t):
-            first = tiles["first"][:, t, :]
-            nc.scalar.activation(first, first, ACT.Copy, scale=severity[:, b, t : t + 1])
-
-        def cross_term(tiles, b, t):
-            second = tiles["second"][:, t, :]
-            nc.vector.scalar_tensor_tensor(
-                out=second,
-                in0=tiles["first"][:, t, :],
-                scalar=severity[:, b, t : t + 1],
-                in1=second,
-                op0=ALU.subtract,
-                op1=ALU.mult,
+        def remainder(tiles, b, t):
+            nc.scalar.activation(
+                tiles["rest"][:, t, :], tiles["first"][:, t, :], ACT.Identity, bias=severity[:, b, t : t + 1], scale=-1.0
             )
 
         def join(tiles):
             nc.vector.tensor_tensor(
                 out=tiles["z"][:].rearrange("p (c i t) -> p c t i", i=2, t=PACK),
-                in0=tiles["first"].rearrange("p t (c i) -> p c t i", i=2),
-                in1=tiles["second"].rearrange("p t (c i) -> p c t i", i=2),
-                op=ALU.subtract,
+                in0=tiles["first"][:].rearrange("p t (c i) -> p c t i", i=2),
+                in1=tiles["second"][:].rearrange("p t (c i) -> p c t i", i=2),
+                op=ALU.add,
             )
 
         def quantize_z(tiles):
             nc.vector.quantize_mx(out=tiles["codes"][:].bitcast(FP8X4), scales=tiles["scales"][:], in_=tiles["z"][:])
 
-        lower = gate_tiles("lower", G, 0)
+        lower = gate_tiles(keep, "lower", G)
+        quarter = P // 4
+        w1_upper = [held(f"w1_upper{a}", [P, PACK * PASS], BF16) for a in range(2)]
         failure_probabilities(0, 0)
         for t in range(PACK):
-            fetch(lower["first"], 0, t, p1, 0, G)
-            if t > 0:
-                cross_term(lower, 0, t - 1)
-            fetch(lower["second"], 0, t, p2, 0, G)
+            fetch_times(lower["first"], severity_rows[0], 0, t, p1, 0, G)
             if t + 1 < PACK:
                 failure_probabilities(0, t + 1)
-            weigh_first(lower, 0, t)
-            for piece in range(W1_PIECES // 2):
-                round_w1(t // 2, 1, (t % 2) * (W1_PIECES // 2) + piece)
-            if t % 2 == 1:
-                quantize_w1(t // 2, 1)
-        cross_term(lower, 0, PACK - 1)
-        failure_probabilities(1, PACK - 1)
-        failure_probabilities(1, 0)
+            else:
+                for piece in range(3):
+                    round_w1(nc.scalar.copy, w1_upper[0], 0, 1, slice(piece * quarter, (piece + 1) * quarter), every_t)
+                round_w1(nc.vector.tensor_copy, w1_upper[1], 1, 1, slice(quarter, P), every_t)
+            remainder(lower, 0, t)
+            if t > 0:
+                fetch_times(lower["second"], lower["rest"], 0, t - 1, p2, 0, G)
+        round_w1(nc.scalar.copy, w1_upper[0], 0, 1, slice(3 * quarter, P), every_t)
+        round_w1(nc.scalar.copy, w1_upper[1], 1, 1, slice(0, quarter), every_t)
+        fetch_times(lower["second"], lower["rest"], 0, PACK - 1, p2, 0, G)
+        for a in range(2):
+            quantize_w1(w1_upper[a], a, 1, every_t)
+        for t in range(PACK):
+            failure_probabilities(1, t)
         join(lower)
         quantize_z(lower)
 
@@ -245,19 +251,13 @@ def tile_list_fault_tree_risk_kernel(
 
         m0 = 0
         waiting = None
-        for chunk, width in enumerate(GATE_CHUNKS):
-            shift = (chunk + 1) % 2
-            upper = gate_tiles(f"upper{m0}", width, shift)
-            order = [(t - shift) % PACK for t in range(PACK)]
-            for step, t in enumerate(order):
-                fetch(upper["first"], 1, t, p1, m0, width)
-                if step > 0:
-                    cross_term(upper, 1, order[step - 1])
-                fetch(upper["second"], 1, t, p2, m0, width)
-                weigh_first(upper, 1, t)
-                if chunk == 0 and step + 2 < PACK:
-                    failure_probabilities(1, order[step + 2])
-            cross_term(upper, 1, order[-1])
+        for width in GATE_CHUNKS:
+            upper = gate_tiles(ring, f"upper{m0}", width)
+            for t in range(PACK):
+                fetch_times(upper["first"], severity_rows[1], 1, t, p1, m0, width)
+                remainder(upper, 1, t)
+            for t in range(PACK):
+                fetch_times(upper["second"], upper["rest"], 1, t, p2, m0, width)
             join(upper)
             if waiting is not None:
                 risk_scores(*waiting, False)
@@ -267,7 +267,7 @@ def tile_list_fault_tree_risk_kernel(
         risk_scores(*waiting, True)
 
         for q in range(4):
-            nc.sync.dma_start(
+            (nc.sync if q < 2 else nc.scalar).dma_start(
                 out_2[:, 4 * q : 4 * q + 4, :].rearrange("n r m -> r n m").bitcast(I32),
                 y_scales[32 * q : 32 * q + 4, :, :].bitcast(I32),
             )

@@ -22,7 +22,6 @@ PASS = P * PACK
 BANK = 512
 LANES = 16
 Y_COLS = 128
-GATE_CHUNKS = (128, 128, 128, 128)
 
 
 def tile_list_fault_tree_risk_kernel(
@@ -54,8 +53,8 @@ def tile_list_fault_tree_risk_kernel(
         def load_table(a):
             nc.sync.dma_start(table[a][:].bitcast(I32), tab_words[a].rearrange("p n i -> p (n i)").bitcast(I32))
 
-        nc.vector.memset(table_scales[:].bitcast(I32), 0)
         nc.vector.memset(w2_scales_raw[:].rearrange("p a c -> p (a c)").bitcast(I32), 0)
+        nc.vector.memset(table_scales[:].bitcast(I32), 0)
 
         nc.sync.dma_start(idx[:], offs)
         nc.sync.dma_start(severity[:], g.rearrange("(b p t) -> p b t", b=2, t=PACK))
@@ -66,15 +65,15 @@ def tile_list_fault_tree_risk_kernel(
                 table_scales[32 * q : 32 * q + 8, :].bitcast(I32), tab_scales[:, 4 * q : 4 * q + 4, :].bitcast(I32)
             )
         load_w1(0, 0)
-        load_table(1)
-        nc.sync.dma_start(p1[:], pos1)
-        nc.sync.dma_start(p2[:], pos2)
-        load_w1(1, 0)
         for q in range(4):
             nc.sync.dma_start(
                 w2_scales_raw[32 * q : 32 * q + 4, :, :].bitcast(I32),
                 w2_scales[:, 4 * q : 4 * q + 4, :].rearrange("a r c -> r a c").bitcast(I32),
             )
+        load_table(1)
+        nc.sync.dma_start(p1[:], pos1)
+        nc.sync.dma_start(p2[:], pos2)
+        load_w1(1, 0)
         load_w1(0, 1)
         load_w1(1, 1)
 
@@ -100,10 +99,10 @@ def tile_list_fault_tree_risk_kernel(
         w1_codes = {key: held(f"w1_codes{key[0]}{key[1]}", [P, PASS], U32) for key in w1_raw}
         w1_scales = {key: held(f"w1_scales{key[0]}{key[1]}", [P, PASS], U8) for key in w1_raw}
 
-        def round_w1(copy, rounded, a, b, ms, ts):
+        def round_w1(copy, rounded, into, a, b, ms, ts):
             dealt = rounded[:].rearrange("p (t m j) -> p m j t", m=P, j=PACK)
             raw = w1_raw[a, b][:].rearrange("p j (m t) -> p m j t", t=PACK)
-            copy(dealt[:, ms], raw[:, ms, :, ts])
+            copy(dealt[:, ms, :, into], raw[:, ms, :, ts])
 
         def quantize_w1(rounded, a, b, ts):
             cols = slice(ts.start * P, ts.stop * P)
@@ -112,25 +111,28 @@ def tile_list_fault_tree_risk_kernel(
             )
 
         every_t = slice(0, PACK)
+        every_m = slice(0, P)
+        m_halves = (slice(0, P // 2), slice(P // 2, P))
         t_pairs = (slice(0, 2), slice(2, 4))
 
         pick_words(0)
         nc.vector.tensor_copy(picked_scales[:], table_scales[:].indirect(idx[:]))
-        w1_first = held("w1_first", [P, PACK * PASS], BF16)
-        round_w1(nc.scalar.copy, w1_first, 0, 0, slice(0, P), every_t)
+        w1_first = held("w1_upper0", [P, PACK * PASS], BF16)
+        for ts in t_pairs:
+            round_w1(nc.scalar.copy, w1_first, ts, 0, 0, every_m, ts)
         quantize_w1(w1_first, 0, 0, every_t)
-        pick_words(1)
-        w1_low = held("w1_low", [P, 2 * PASS], BF16)
-        w1_high = held("staged", [P, 2 * PASS], BF16)
-        round_w1(nc.vector.tensor_copy, w1_low, 1, 0, slice(0, P), t_pairs[0])
-        round_w1(nc.scalar.copy, w1_high, 1, 0, slice(0, P), t_pairs[1])
-        quantize_w1(w1_low, 1, 0, t_pairs[0])
-        quantize_w1(w1_high, 1, 0, t_pairs[1])
-
-        w2_scales_dealt = held("staged", [P, 4, PACK, P], U8)
+        w2_scales_dealt = held("w2_scales_dealt", [P, 4, PACK, P], U8)
         nc.vector.tensor_copy(
             w2_scales_dealt[:], w2_scales_raw[:].rearrange("p a (n m t) -> p (a n) t m", n=2, t=PACK)
         )
+
+        pick_words(1)
+        w1_low = held("w1_low", [P, 2 * PASS], BF16)
+        w1_high = held("w1_high", [P, 2 * PASS], BF16)
+        round_w1(nc.vector.tensor_copy, w1_low, t_pairs[0], 1, 0, every_m, t_pairs[0])
+        round_w1(nc.scalar.copy, w1_high, t_pairs[0], 1, 0, every_m, t_pairs[1])
+        quantize_w1(w1_low, 1, 0, t_pairs[0])
+        quantize_w1(w1_high, 1, 0, t_pairs[1])
 
         h = {(b, t): held(f"h{b}{t}", [P, S], F32) for b in range(2) for t in range(PACK)}
 
@@ -155,6 +157,7 @@ def tile_list_fault_tree_risk_kernel(
                 "first": pool.tile([P, PACK, width], F32, name=f"first{width}"),
                 "rest": pool.tile([P, PACK, width], F32, name=f"rest{width}"),
                 "second": pool.tile([P, PACK, width], F32, name=f"second{width}"),
+                "pairs": pool.tile([P, 2, width, 2], BF16, name="w2_raw", align_bytes=64),
                 "z": held(f"z{name}", [P, width * PACK], BF16),
                 "codes": held(f"z_codes{name}", [P, width], U32),
                 "scales": held(f"z_scales{name}", [P, width], U8),
@@ -171,38 +174,50 @@ def tile_list_fault_tree_risk_kernel(
 
         def join(tiles):
             nc.vector.tensor_tensor(
-                out=tiles["z"][:].rearrange("p (c i t) -> p c t i", i=2, t=PACK),
-                in0=tiles["first"][:].rearrange("p t (c i) -> p c t i", i=2),
-                in1=tiles["second"][:].rearrange("p t (c i) -> p c t i", i=2),
+                out=tiles["pairs"][:],
+                in0=tiles["first"][:].rearrange("p (u e) m -> p u m e", e=2),
+                in1=tiles["second"][:].rearrange("p (u e) m -> p u m e", e=2),
                 op=ALU.add,
+            )
+
+        def weave(tiles):
+            words = tiles["pairs"][:].rearrange("p u m e -> p u (m e)").bitcast(F32)
+            nc.vector.tensor_copy(
+                tiles["z"][:].bitcast(F32).rearrange("p (m u) -> p m u", u=2), words.rearrange("p u m -> p m u")
             )
 
         def quantize_z(tiles):
             nc.vector.quantize_mx(out=tiles["codes"][:].bitcast(FP8X4), scales=tiles["scales"][:], in_=tiles["z"][:])
 
         lower = gate_tiles(keep, "lower", G)
-        quarter = P // 4
         w1_upper = [held(f"w1_upper{a}", [P, PACK * PASS], BF16) for a in range(2)]
+
+        def round_upper(copy, a, ms, pair):
+            round_w1(copy, w1_upper[a], t_pairs[pair], a, 1, ms, t_pairs[pair])
+
         failure_probabilities(0, 0)
+        round_upper(nc.vector.tensor_copy, 0, every_m, 0)
+        round_upper(nc.vector.tensor_copy, 0, m_halves[0], 1)
         for t in range(PACK):
             fetch_times(lower["first"], severity_rows[0], 0, t, p1, 0, G)
             if t + 1 < PACK:
                 failure_probabilities(0, t + 1)
             else:
-                for piece in range(3):
-                    round_w1(nc.scalar.copy, w1_upper[0], 0, 1, slice(piece * quarter, (piece + 1) * quarter), every_t)
-                round_w1(nc.vector.tensor_copy, w1_upper[1], 1, 1, slice(quarter, P), every_t)
+                round_upper(nc.scalar.copy, 0, m_halves[1], 1)
+                for ms in m_halves:
+                    round_upper(nc.scalar.copy, 1, ms, 0)
             remainder(lower, 0, t)
             if t > 0:
                 fetch_times(lower["second"], lower["rest"], 0, t - 1, p2, 0, G)
-        round_w1(nc.scalar.copy, w1_upper[0], 0, 1, slice(3 * quarter, P), every_t)
-        round_w1(nc.scalar.copy, w1_upper[1], 1, 1, slice(0, quarter), every_t)
+        for ms in m_halves:
+            round_upper(nc.scalar.copy, 1, ms, 1)
         fetch_times(lower["second"], lower["rest"], 0, PACK - 1, p2, 0, G)
         for a in range(2):
             quantize_w1(w1_upper[a], a, 1, every_t)
         for t in range(PACK):
             failure_probabilities(1, t)
         join(lower)
+        weave(lower)
         quantize_z(lower)
 
         y_codes = held("y_codes", [P, 2, G], U32)
@@ -249,22 +264,26 @@ def tile_list_fault_tree_risk_kernel(
             words = out_1.rearrange("n p m t -> p n (m t)").bitcast(I32)
             nc.sync.dma_start(words[:, :, m0 : m0 + width], y_codes[:, :, m0 : m0 + width].bitcast(I32))
 
-        m0 = 0
-        waiting = None
-        for width in GATE_CHUNKS:
-            upper = gate_tiles(ring, f"upper{m0}", width)
+        chunks = G // Y_COLS
+        upper = {}
+
+        def first_inputs(chunk):
+            upper[chunk] = gate_tiles(ring, f"upper{chunk}", Y_COLS)
             for t in range(PACK):
-                fetch_times(upper["first"], severity_rows[1], 1, t, p1, m0, width)
-                remainder(upper, 1, t)
+                fetch_times(upper[chunk]["first"], severity_rows[1], 1, t, p1, chunk * Y_COLS, Y_COLS)
+                remainder(upper[chunk], 1, t)
+
+        first_inputs(0)
+        first_inputs(1)
+        for chunk in range(chunks):
             for t in range(PACK):
-                fetch_times(upper["second"], upper["rest"], 1, t, p2, m0, width)
-            join(upper)
-            if waiting is not None:
-                risk_scores(*waiting, False)
-            quantize_z(upper)
-            waiting = (upper, m0, width)
-            m0 = m0 + width
-        risk_scores(*waiting, True)
+                fetch_times(upper[chunk]["second"], upper[chunk]["rest"], 1, t, p2, chunk * Y_COLS, Y_COLS)
+            join(upper[chunk])
+            weave(upper[chunk])
+            quantize_z(upper[chunk])
+            if chunk + 2 < chunks:
+                first_inputs(chunk + 2)
+            risk_scores(upper[chunk], chunk * Y_COLS, Y_COLS, chunk == chunks - 1)
 
         for q in range(4):
             (nc.sync if q < 2 else nc.scalar).dma_start(

@@ -53,22 +53,26 @@ def tile_list_fault_tree_risk_kernel(
         def load_table(a):
             nc.sync.dma_start(table[a][:].bitcast(I32), tab_words[a].rearrange("p n i -> p (n i)").bitcast(I32))
 
-        nc.vector.memset(w2_scales_raw[:].rearrange("p a c -> p (a c)").bitcast(I32), 0)
-        nc.vector.memset(table_scales[:].bitcast(I32), 0)
+        def load_table_scales(a, r):
+            nc.sync.dma_start(table_scales[4 * a + r : P : 32, :].bitcast(I32), tab_scales[a, r:16:4, :].bitcast(I32))
 
+        nc.vector.memset(table_scales[:].bitcast(I32), 0)
+        nc.vector.memset(w2_scales_raw[:].rearrange("p a c -> p (a c)").bitcast(I32), 0)
+
+        scale_rows = [(a, q) for q in range(4) for a in range(2)]
         nc.sync.dma_start(idx[:], offs)
         nc.sync.dma_start(severity[:], g.rearrange("(b p t) -> p b t", b=2, t=PACK))
         nc.sync.dma_start(w2_raw[:].bitcast(I32), w2_words.rearrange("a p c -> p a c").bitcast(I32))
+        for a, q in scale_rows[:3]:
+            load_table_scales(a, q)
         load_table(0)
-        for q in range(4):
-            nc.sync.dma_start(
-                table_scales[32 * q : 32 * q + 8, :].bitcast(I32), tab_scales[:, 4 * q : 4 * q + 4, :].bitcast(I32)
-            )
+        for a, q in scale_rows[3:]:
+            load_table_scales(a, q)
         load_w1(0, 0)
         for q in range(4):
             nc.sync.dma_start(
-                w2_scales_raw[32 * q : 32 * q + 4, :, :].bitcast(I32),
-                w2_scales[:, 4 * q : 4 * q + 4, :].rearrange("a r c -> r a c").bitcast(I32),
+                w2_scales_raw[q:P:32, :, :].bitcast(I32),
+                w2_scales[:, q:16:4, :].rearrange("a r c -> r a c").bitcast(I32),
             )
         load_table(1)
         nc.sync.dma_start(p1[:], pos1)
@@ -77,10 +81,8 @@ def tile_list_fault_tree_risk_kernel(
         load_w1(0, 1)
         load_w1(1, 1)
 
-        severity_rows = [held("severity_lower", [P, PACK, G], F32), held("severity_upper", [P, PACK, Y_COLS], F32)]
-        for b in range(2):
-            rows = severity_rows[b]
-            nc.vector.tensor_copy(rows[:], severity[:, b, :].unsqueeze(2).to_broadcast(list(rows.shape)))
+        severity_rows = held("severity_rows", [P, 2, PACK, G], F32)
+        nc.scalar.copy(severity_rows[:], severity[:].unsqueeze(3).to_broadcast([P, 2, PACK, G]))
 
         w2_dealt = held("w2_dealt", [P, 4, PACK, 2 * P], U8)
         nc.vector.tensor_copy(
@@ -152,44 +154,59 @@ def tile_list_fault_tree_risk_kernel(
                     )
                 nc.scalar.activation(h[b, t][:, half * BANK : (half + 1) * BANK], bank[:], ACT.Sigmoid)
 
-        def gate_tiles(pool, name, width):
+        def fetch_times(dst, factor, b, t, places, gates):
+            entries = places[:, gates.start // LANES : gates.stop // LANES]
+            nc.vector.tensor_tensor(out=dst, in0=h[b, t][:].indirect(entries), in1=factor, op=ALU.mult)
+
+        def first_tiles(pool, first_tag, rest_tag, b, gates):
+            shape = [P, PACK, gates.stop - gates.start]
+            first = pool.tile(shape, F32, name=first_tag, align_bytes=64)
+            return {"b": b, "gates": gates, "first": first, "rest": held(rest_tag, shape, F32)}
+
+        def first_input(firsts, t):
+            b, gates = firsts["b"], firsts["gates"]
+            fetch_times(firsts["first"][:, t, :], severity_rows[:, b, t, gates], b, t, p1, gates)
+
+        def remainder(firsts, t):
+            weight = severity[:, firsts["b"], t : t + 1]
+            nc.scalar.activation(firsts["rest"][:, t, :], firsts["first"][:, t, :], ACT.Identity, bias=weight, scale=-1.0)
+
+        def remainder_on_vector(firsts, t):
+            weight = severity[:, firsts["b"], t : t + 1]
+            nc.vector.tensor_scalar(firsts["rest"][:, t, :], firsts["first"][:, t, :], -1.0, weight, ALU.mult, ALU.add)
+
+        def gate_tiles(pool, firsts, gates):
+            b = firsts["b"]
+            width = gates.stop - gates.start
+            local = slice(gates.start - firsts["gates"].start, gates.stop - firsts["gates"].start)
+            name = f"{b}_{gates.start}"
             return {
-                "first": pool.tile([P, PACK, width], F32, name=f"first{width}"),
-                "rest": pool.tile([P, PACK, width], F32, name=f"rest{width}"),
-                "second": pool.tile([P, PACK, width], F32, name=f"second{width}"),
-                "pairs": pool.tile([P, 2, width, 2], BF16, name="w2_raw", align_bytes=64),
+                "b": b,
+                "gates": gates,
+                "first": firsts["first"][:, :, local],
+                "rest": firsts["rest"][:, :, local],
+                "second": pool.tile([P, PACK, width], F32, name=f"gathered{b}", align_bytes=64),
                 "z": held(f"z{name}", [P, width * PACK], BF16),
                 "codes": held(f"z_codes{name}", [P, width], U32),
                 "scales": held(f"z_scales{name}", [P, width], U8),
             }
 
-        def fetch_times(dst, factor, b, t, places, m0, width):
-            entries = places[:, m0 // LANES : (m0 + width) // LANES]
-            nc.vector.tensor_tensor(out=dst[:, t, :], in0=h[b, t][:].indirect(entries), in1=factor[:, t, :], op=ALU.mult)
-
-        def remainder(tiles, b, t):
-            nc.scalar.activation(
-                tiles["rest"][:, t, :], tiles["first"][:, t, :], ACT.Identity, bias=severity[:, b, t : t + 1], scale=-1.0
-            )
+        def second_input(tiles, t):
+            fetch_times(tiles["second"][:, t, :], tiles["rest"][:, t, :], tiles["b"], t, p2, tiles["gates"])
 
         def join(tiles):
             nc.vector.tensor_tensor(
-                out=tiles["pairs"][:],
-                in0=tiles["first"][:].rearrange("p (u e) m -> p u m e", e=2),
-                in1=tiles["second"][:].rearrange("p (u e) m -> p u m e", e=2),
+                out=tiles["z"][:].rearrange("p (c i t) -> p c t i", i=2, t=PACK),
+                in0=tiles["first"].rearrange("p t (c i) -> p c t i", i=2),
+                in1=tiles["second"][:].rearrange("p t (c i) -> p c t i", i=2),
                 op=ALU.add,
-            )
-
-        def weave(tiles):
-            words = tiles["pairs"][:].rearrange("p u m e -> p u (m e)").bitcast(F32)
-            nc.vector.tensor_copy(
-                tiles["z"][:].bitcast(F32).rearrange("p (m u) -> p m u", u=2), words.rearrange("p u m -> p m u")
             )
 
         def quantize_z(tiles):
             nc.vector.quantize_mx(out=tiles["codes"][:].bitcast(FP8X4), scales=tiles["scales"][:], in_=tiles["z"][:])
 
-        lower = gate_tiles(keep, "lower", G)
+        lower_firsts = first_tiles(keep, "first_lower", "rest", 0, slice(0, G))
+        lower = gate_tiles(keep, lower_firsts, slice(0, G))
         w1_upper = [held(f"w1_upper{a}", [P, PACK * PASS], BF16) for a in range(2)]
 
         def round_upper(copy, a, ms, pair):
@@ -199,26 +216,32 @@ def tile_list_fault_tree_risk_kernel(
         round_upper(nc.vector.tensor_copy, 0, every_m, 0)
         round_upper(nc.vector.tensor_copy, 0, m_halves[0], 1)
         for t in range(PACK):
-            fetch_times(lower["first"], severity_rows[0], 0, t, p1, 0, G)
+            first_input(lower_firsts, t)
             if t + 1 < PACK:
                 failure_probabilities(0, t + 1)
             else:
                 round_upper(nc.scalar.copy, 0, m_halves[1], 1)
                 for ms in m_halves:
                     round_upper(nc.scalar.copy, 1, ms, 0)
-            remainder(lower, 0, t)
+            remainder(lower_firsts, t)
             if t > 0:
-                fetch_times(lower["second"], lower["rest"], 0, t - 1, p2, 0, G)
+                second_input(lower, t - 1)
         for ms in m_halves:
             round_upper(nc.scalar.copy, 1, ms, 1)
-        fetch_times(lower["second"], lower["rest"], 0, PACK - 1, p2, 0, G)
         for a in range(2):
             quantize_w1(w1_upper[a], a, 1, every_t)
+        second_input(lower, PACK - 1)
         for t in range(PACK):
             failure_probabilities(1, t)
+        upper_firsts = first_tiles(keep, "w1_raw00", "rest", 1, slice(0, G - Y_COLS))
+        first_input(upper_firsts, 0)
         join(lower)
-        weave(lower)
+        first_input(upper_firsts, 1)
         quantize_z(lower)
+        for t in range(2, PACK):
+            first_input(upper_firsts, t)
+        for t in range(PACK):
+            remainder(upper_firsts, t)
 
         y_codes = held("y_codes", [P, 2, G], U32)
         y_scales = held("y_scales", [P, 2, G], U8)
@@ -235,58 +258,75 @@ def tile_list_fault_tree_risk_kernel(
                     stop=(a == 1 and t == PACK - 1),
                 )
 
-        def risk_scores(upper, m0, width, last):
-            for n in range(2):
-                y = held(f"y{m0}_{n}", [P, PACK, width], F32)
-                y_bf = held(f"y_bf{m0}_{n}", [P, width, PACK], BF16)
-                for c0 in range(0, width, Y_COLS):
-                    local = slice(c0, c0 + Y_COLS)
-                    whole = slice(m0 + c0, m0 + c0 + Y_COLS)
-                    bank = psum.tile([P, PACK, Y_COLS], F32, name="bank")
-                    risk_passes(bank, n, 0, lower["codes"][:, whole], lower["scales"][:, whole])
-                    risk_passes(bank, n, 1, upper["codes"][:, local], upper["scales"][:, local])
-                    if last and n == 1:
-                        nc.vector.tensor_copy(y[:, :, local], bank[:])
-                        nc.vector.tensor_copy(
-                            y_bf[:, local, :].rearrange("p (c i) t -> p c t i", i=PACK),
-                            y[:, :, local].rearrange("p t (c i) -> p c t i", i=PACK),
-                        )
-                    else:
-                        nc.scalar.copy(y_bf[:, local, :], bank[:].rearrange("p t m -> p m t"))
-                        nc.scalar.copy(y[:, :, local], bank[:])
-                rows = out_0[n * PASS : (n + 1) * PASS, m0 : m0 + width]
-                nc.sync.dma_start(rows.rearrange("(p t) m -> p t m", t=PACK), y[:])
-                nc.vector.quantize_mx(
-                    out=y_codes[:, n, m0 : m0 + width].bitcast(FP8X4),
-                    scales=y_scales[:, n, m0 : m0 + width],
-                    in_=y_bf[:].rearrange("p m t -> p (m t)"),
-                )
+        def risk_bank(upper, n):
+            gates = upper["gates"]
+            bank = psum.tile([P, PACK, Y_COLS], F32, name="bank")
+            risk_passes(bank, n, 0, lower["codes"][:, gates], lower["scales"][:, gates])
+            risk_passes(bank, n, 1, upper["codes"][:], upper["scales"][:])
+            return {"bank": bank, "gates": gates, "n": n}
+
+        def planes_of(scores, copy):
+            gates, n = scores["gates"], scores["n"]
+            y_bf = held(f"y_bf{gates.start}_{n}", [P, Y_COLS, PACK], BF16)
+            copy(y_bf[:], scores["bank"][:].rearrange("p t m -> p m t"))
+            nc.vector.quantize_mx(
+                out=y_codes[:, n, gates].bitcast(FP8X4),
+                scales=y_scales[:, n, gates],
+                in_=y_bf[:].rearrange("p m t -> p (m t)"),
+            )
+
+        def store_scores(scores):
+            gates, n = scores["gates"], scores["n"]
+            y = held(f"y{gates.start}_{n}", [P, PACK, Y_COLS], F32)
+            nc.scalar.copy(y[:], scores["bank"][:])
+            rows = out_0[n * PASS : (n + 1) * PASS, gates]
+            nc.sync.dma_start(rows.rearrange("(p t) m -> p t m", t=PACK), y[:])
+
+        def store_codes(gates):
             words = out_1.rearrange("n p m t -> p n (m t)").bitcast(I32)
-            nc.sync.dma_start(words[:, :, m0 : m0 + width], y_codes[:, :, m0 : m0 + width].bitcast(I32))
+            nc.sync.dma_start(words[:, :, gates], y_codes[:, :, gates].bitcast(I32))
 
-        chunks = G // Y_COLS
-        upper = {}
+        def risk_scores(upper, round_second_bank):
+            for n, copy in enumerate((nc.scalar.copy, round_second_bank)):
+                scores = risk_bank(upper, n)
+                planes_of(scores, copy)
+                store_scores(scores)
+            store_codes(upper["gates"])
 
-        def first_inputs(chunk):
-            upper[chunk] = gate_tiles(ring, f"upper{chunk}", Y_COLS)
-            for t in range(PACK):
-                fetch_times(upper[chunk]["first"], severity_rows[1], 1, t, p1, chunk * Y_COLS, Y_COLS)
-                remainder(upper[chunk], 1, t)
+        chunk_gates = [slice(m0, m0 + Y_COLS) for m0 in range(0, G, Y_COLS)]
+        upper = [gate_tiles(ring, upper_firsts, chunk_gates[0])]
+        for t in range(PACK):
+            second_input(upper[0], t)
+        for chunk in (1, 2):
+            upper.append(gate_tiles(ring, upper_firsts, chunk_gates[chunk]))
+            second_input(upper[chunk], 0)
+            join(upper[chunk - 1])
+            second_input(upper[chunk], 1)
+            quantize_z(upper[chunk - 1])
+            for t in range(2, PACK):
+                second_input(upper[chunk], t)
+            risk_scores(upper[chunk - 1], nc.scalar.copy)
 
-        first_inputs(0)
-        first_inputs(1)
-        for chunk in range(chunks):
-            for t in range(PACK):
-                fetch_times(upper[chunk]["second"], upper[chunk]["rest"], 1, t, p2, chunk * Y_COLS, Y_COLS)
-            join(upper[chunk])
-            weave(upper[chunk])
-            quantize_z(upper[chunk])
-            if chunk + 2 < chunks:
-                first_inputs(chunk + 2)
-            risk_scores(upper[chunk], chunk * Y_COLS, Y_COLS, chunk == chunks - 1)
+        last_firsts = first_tiles(ring, "gathered1", "rest_last", 1, chunk_gates[3])
+        first_input(last_firsts, 0)
+        join(upper[2])
+        first_input(last_firsts, 1)
+        quantize_z(upper[2])
+        upper.append(gate_tiles(ring, last_firsts, chunk_gates[3]))
+        for t in range(PACK):
+            if t + 2 < PACK:
+                first_input(last_firsts, t + 2)
+            remainder_on_vector(last_firsts, t)
+            if t > 0:
+                second_input(upper[3], t - 1)
+        second_input(upper[3], PACK - 1)
+        join(upper[3])
+        quantize_z(upper[3])
+        risk_scores(upper[2], nc.vector.tensor_copy)
+        risk_scores(upper[3], nc.vector.tensor_copy)
 
         for q in range(4):
             (nc.sync if q < 2 else nc.scalar).dma_start(
-                out_2[:, 4 * q : 4 * q + 4, :].rearrange("n r m -> r n m").bitcast(I32),
-                y_scales[32 * q : 32 * q + 4, :, :].bitcast(I32),
+                out_2[:, q:16:4, :].rearrange("n r m -> r n m").bitcast(I32),
+                y_scales[q:P:32, :, :].bitcast(I32),
             )

@@ -54,7 +54,7 @@ def tile_list_fault_tree_risk_kernel(
             nc.sync.dma_start(table[a][:].bitcast(I32), tab_words[a].rearrange("p n i -> p (n i)").bitcast(I32))
 
         def load_table_scales(a, r):
-            nc.sync.dma_start(table_scales[4 * a + r : P : 32, :].bitcast(I32), tab_scales[a, r:16:4, :].bitcast(I32))
+            nc.sync.dma_start(table_scales[4 + 4 * a + r : P : 32, :].bitcast(I32), tab_scales[a, r:16:4, :].bitcast(I32))
 
         nc.vector.memset(table_scales[:].bitcast(I32), 0)
         nc.vector.memset(w2_scales_raw[:].rearrange("p a c -> p (a c)").bitcast(I32), 0)
@@ -148,7 +148,7 @@ def tile_list_fault_tree_risk_kernel(
                         lhsT=w1_codes[a, b][:, cols].bitcast(FP8X4),
                         lhsT_scale=w1_scales[a, b][:, cols],
                         rhs=picked[a, half][:].bitcast(FP8X4),
-                        rhs_scale=picked_scales[4 * a : P, half * BANK : (half + 1) * BANK],
+                        rhs_scale=picked_scales[4 + 4 * a : P, half * BANK : (half + 1) * BANK],
                         start=(a == 0),
                         stop=(a == 1),
                     )
@@ -170,10 +170,6 @@ def tile_list_fault_tree_risk_kernel(
         def remainder(firsts, t):
             weight = severity[:, firsts["b"], t : t + 1]
             nc.scalar.activation(firsts["rest"][:, t, :], firsts["first"][:, t, :], ACT.Identity, bias=weight, scale=-1.0)
-
-        def remainder_on_vector(firsts, t):
-            weight = severity[:, firsts["b"], t : t + 1]
-            nc.vector.tensor_scalar(firsts["rest"][:, t, :], firsts["first"][:, t, :], -1.0, weight, ALU.mult, ALU.add)
 
         def gate_tiles(pool, firsts, gates):
             b = firsts["b"]
@@ -233,7 +229,7 @@ def tile_list_fault_tree_risk_kernel(
         second_input(lower, PACK - 1)
         for t in range(PACK):
             failure_probabilities(1, t)
-        upper_firsts = first_tiles(keep, "w1_raw00", "rest", 1, slice(0, G - Y_COLS))
+        upper_firsts = first_tiles(keep, "w1_raw00", "rest", 1, slice(0, G))
         first_input(upper_firsts, 0)
         join(lower)
         first_input(upper_firsts, 1)
@@ -286,18 +282,11 @@ def tile_list_fault_tree_risk_kernel(
             words = out_1.rearrange("n p m t -> p n (m t)").bitcast(I32)
             nc.sync.dma_start(words[:, :, gates], y_codes[:, :, gates].bitcast(I32))
 
-        def risk_scores(upper, round_second_bank):
-            for n, copy in enumerate((nc.scalar.copy, round_second_bank)):
-                scores = risk_bank(upper, n)
-                planes_of(scores, copy)
-                store_scores(scores)
-            store_codes(upper["gates"])
-
         chunk_gates = [slice(m0, m0 + Y_COLS) for m0 in range(0, G, Y_COLS)]
         upper = [gate_tiles(ring, upper_firsts, chunk_gates[0])]
         for t in range(PACK):
             second_input(upper[0], t)
-        for chunk in (1, 2):
+        for chunk in range(1, len(chunk_gates)):
             upper.append(gate_tiles(ring, upper_firsts, chunk_gates[chunk]))
             second_input(upper[chunk], 0)
             join(upper[chunk - 1])
@@ -305,25 +294,27 @@ def tile_list_fault_tree_risk_kernel(
             quantize_z(upper[chunk - 1])
             for t in range(2, PACK):
                 second_input(upper[chunk], t)
-            risk_scores(upper[chunk - 1], nc.scalar.copy)
+            if chunk + 1 < len(chunk_gates):
+                for n in range(2):
+                    scores = risk_bank(upper[chunk - 1], n)
+                    planes_of(scores, nc.scalar.copy)
+                    store_scores(scores)
+                store_codes(chunk_gates[chunk - 1])
 
-        last_firsts = first_tiles(ring, "gathered1", "rest_last", 1, chunk_gates[3])
-        first_input(last_firsts, 0)
-        join(upper[2])
-        first_input(last_firsts, 1)
-        quantize_z(upper[2])
-        upper.append(gate_tiles(ring, last_firsts, chunk_gates[3]))
-        for t in range(PACK):
-            if t + 2 < PACK:
-                first_input(last_firsts, t + 2)
-            remainder_on_vector(last_firsts, t)
-            if t > 0:
-                second_input(upper[3], t - 1)
-        second_input(upper[3], PACK - 1)
-        join(upper[3])
-        quantize_z(upper[3])
-        risk_scores(upper[2], nc.vector.tensor_copy)
-        risk_scores(upper[3], nc.vector.tensor_copy)
+        before_last = [risk_bank(upper[-2], n) for n in range(2)]
+        store_scores(before_last[0])
+        join(upper[-1])
+        quantize_z(upper[-1])
+        planes_of(before_last[1], nc.vector.tensor_copy)
+        store_scores(before_last[1])
+        planes_of(before_last[0], nc.vector.tensor_copy)
+        store_codes(chunk_gates[-2])
+        last = [risk_bank(upper[-1], n) for n in range(2)]
+        store_scores(last[0])
+        planes_of(last[1], nc.vector.tensor_copy)
+        planes_of(last[0], nc.scalar.copy)
+        store_scores(last[1])
+        store_codes(chunk_gates[-1])
 
         for q in range(4):
             (nc.sync if q < 2 else nc.scalar).dma_start(

@@ -30,8 +30,7 @@ def tile_list_fault_tree_risk_kernel(
     nc = tc.nc
     with ExitStack() as ctx:
         keep = ctx.enter_context(tc.tile_pool(name="keep", bufs=1))
-        ring = ctx.enter_context(tc.tile_pool(name="ring", bufs=2))
-        psum = ctx.enter_context(tc.psum_pool(name="psum", bufs=8))
+        psum = ctx.enter_context(tc.psum_pool(name="psum", bufs=1))
 
         def held(name, shape, dtype):
             return keep.tile(shape, dtype, name=name, align_bytes=64)
@@ -41,7 +40,7 @@ def tile_list_fault_tree_risk_kernel(
         p2 = keep.tile([P, G // LANES], U16, name="p2")
         table = [held(f"table{a}", [P, T], U32) for a in range(2)]
         table_scales = held("table_scales", [P, T], U8)
-        w1_raw = {(a, b): held(f"w1_raw{a}{b}", [P, PACK, PASS], F32) for a in range(2) for b in range(2)}
+        w1_raw = {(a, b): held(f"w1_raw{a}{b}", [P, PACK, PASS], F32) for a, b in ((0, 0), (0, 1), (1, 1))}
         w2_raw = held("w2_raw", [P, 2, 2 * N], U8)
         w2_scales_raw = held("w2_scales_raw", [P, 2, N], U8)
         severity = held("severity", [P, 2, PACK], F32)
@@ -50,56 +49,67 @@ def tile_list_fault_tree_risk_kernel(
             rows = w1[a * PASS : (a + 1) * PASS, b * PASS : (b + 1) * PASS]
             nc.sync.dma_start(w1_raw[a, b][:], rows.rearrange("(p j) c -> p j c", j=PACK))
 
+        w1_late = [held(f"w1_late{half}", [P, PACK, PASS // 2], F32) for half in range(2)]
+
+        def load_w1_late(half):
+            rows = w1[PASS : 2 * PASS, half * PASS // 2 : (half + 1) * PASS // 2]
+            nc.sync.dma_start(w1_late[half][:], rows.rearrange("(p j) c -> p j c", j=PACK))
+
         def load_table(a):
             nc.sync.dma_start(table[a][:].bitcast(I32), tab_words[a].rearrange("p n i -> p (n i)").bitcast(I32))
 
         def load_table_scales(a, r):
             nc.sync.dma_start(table_scales[4 + 4 * a + r : P : 32, :].bitcast(I32), tab_scales[a, r:16:4, :].bitcast(I32))
 
+        warm = held("warm", [P, 2], F32)
+        nc.gpsimd.memset(warm[:, 0:1], 0.0)
+        nc.scalar.activation(warm[:, 1:2], warm[:, 0:1], ACT.Sigmoid)
+
         nc.vector.memset(table_scales[:].bitcast(I32), 0)
         nc.vector.memset(w2_scales_raw[:].rearrange("p a c -> p (a c)").bitcast(I32), 0)
 
-        scale_rows = [(a, q) for q in range(4) for a in range(2)]
-        nc.sync.dma_start(idx[:], offs)
-        nc.sync.dma_start(severity[:], g.rearrange("(b p t) -> p b t", b=2, t=PACK))
-        nc.sync.dma_start(w2_raw[:].bitcast(I32), w2_words.rearrange("a p c -> p a c").bitcast(I32))
-        for a, q in scale_rows[:3]:
-            load_table_scales(a, q)
-        load_table(0)
-        for a, q in scale_rows[3:]:
-            load_table_scales(a, q)
-        load_w1(0, 0)
-        for q in range(4):
+        def load_w2_scales(r):
             nc.sync.dma_start(
-                w2_scales_raw[q:P:32, :, :].bitcast(I32),
-                w2_scales[:, q:16:4, :].rearrange("a r c -> r a c").bitcast(I32),
+                w2_scales_raw[r:P:32, :, :].bitcast(I32),
+                w2_scales[:, r:16:4, :].rearrange("a q c -> q a c").bitcast(I32),
             )
+
+        scale_rows = [(a, r) for r in range(4) for a in range(2)]
+        nc.sync.dma_start(severity[:], g.rearrange("(b p t) -> p b t", b=2, t=PACK))
+        load_table(0)
+        nc.sync.dma_start(idx[:], offs)
+        for a, r in scale_rows[:4]:
+            load_table_scales(a, r)
+        load_w1(0, 0)
+        for a, r in scale_rows[4:]:
+            load_table_scales(a, r)
         load_table(1)
+        load_w1_late(0)
+        load_w1_late(1)
         nc.sync.dma_start(p1[:], pos1)
+        nc.sync.dma_start(w2_raw[:].bitcast(I32), w2_words.rearrange("a p c -> p a c").bitcast(I32))
+        for r in range(4):
+            load_w2_scales(r)
         nc.sync.dma_start(p2[:], pos2)
-        load_w1(1, 0)
         load_w1(0, 1)
         load_w1(1, 1)
 
         severity_rows = held("severity_rows", [P, 2, PACK, G], F32)
         nc.scalar.copy(severity_rows[:], severity[:].unsqueeze(3).to_broadcast([P, 2, PACK, G]))
 
-        w2_dealt = held("w2_dealt", [P, 4, PACK, 2 * P], U8)
-        nc.vector.tensor_copy(
-            w2_dealt[:].bitcast(U16),
-            w2_raw[:].bitcast(U16).rearrange("p a (n m t) -> p (a n) t m", n=2, t=PACK),
-        )
-
         picked_scales = held("picked_scales", [P, S], U8)
-        picked = {(a, half): held(f"picked{a}{half}", [P, BANK], U32) for a in range(2) for half in range(2)}
+        picked = {}
 
-        def pick_words(a):
+        def pick_words(a, tag):
+            both = held(tag, [P, S], U32)
             for half in range(2):
+                picked[a, half] = both[:, half * BANK : (half + 1) * BANK]
                 entries = idx[:, half * BANK // LANES : (half + 1) * BANK // LANES]
-                nc.vector.tensor_copy(picked[a, half][:], table[a][:].indirect(entries))
+                nc.vector.tensor_copy(picked[a, half], table[a][:].indirect(entries))
 
-        w1_codes = {key: held(f"w1_codes{key[0]}{key[1]}", [P, PASS], U32) for key in w1_raw}
-        w1_scales = {key: held(f"w1_scales{key[0]}{key[1]}", [P, PASS], U8) for key in w1_raw}
+        blocks = [(a, b) for a in range(2) for b in range(2)]
+        w1_codes = {key: held(f"w1_codes{key[0]}{key[1]}", [P, PASS], U32) for key in blocks[1:]}
+        w1_scales = {key: held(f"w1_scales{key[0]}{key[1]}", [P, PASS], U8) for key in blocks}
 
         def round_w1(copy, rounded, into, a, b, ms, ts):
             dealt = rounded[:].rearrange("p (t m j) -> p m j t", m=P, j=PACK)
@@ -117,37 +127,53 @@ def tile_list_fault_tree_risk_kernel(
         m_halves = (slice(0, P // 2), slice(P // 2, P))
         t_pairs = (slice(0, 2), slice(2, 4))
 
-        pick_words(0)
+        pick_words(0, "picked0")
         nc.vector.tensor_copy(picked_scales[:], table_scales[:].indirect(idx[:]))
-        w1_first = held("w1_upper0", [P, PACK * PASS], BF16)
+        w1_codes[0, 0] = held("table_scales", [P, PASS], U32)
+        w1_first = held("w1_first", [P, PACK * PASS], BF16)
         for ts in t_pairs:
             round_w1(nc.scalar.copy, w1_first, ts, 0, 0, every_m, ts)
         quantize_w1(w1_first, 0, 0, every_t)
+
+        pick_words(1, "w1_first")
+        w1_low = held("w1_low", [P, 2 * PASS], BF16)
+        w1_high = held("w1_high", [P, 2 * PASS], BF16)
+
+        def round_late(copy, rounded, half, pair):
+            dealt = rounded[:].rearrange("p (t m j) -> p m j t", m=P, j=PACK)
+            raw = w1_late[half][:].rearrange("p j (m t) -> p m j t", t=PACK)
+            copy(dealt[:, m_halves[half], :, :], raw[:, :, :, t_pairs[pair]])
+
+        round_late(nc.scalar.copy, w1_low, 0, 0)
+        round_late(nc.scalar.copy, w1_high, 0, 1)
+        round_late(nc.vector.tensor_copy, w1_low, 1, 0)
+        round_late(nc.scalar.copy, w1_high, 1, 1)
+        quantize_w1(w1_low, 1, 0, t_pairs[0])
+        quantize_w1(w1_high, 1, 0, t_pairs[1])
+
+        w2_dealt = held("w2_dealt", [P, 4, PACK, 2 * P], U8)
+        nc.vector.tensor_copy(
+            w2_dealt[:].bitcast(U16),
+            w2_raw[:].bitcast(U16).rearrange("p a (n m t) -> p (a n) t m", n=2, t=PACK),
+        )
+
         w2_scales_dealt = held("w2_scales_dealt", [P, 4, PACK, P], U8)
         nc.vector.tensor_copy(
             w2_scales_dealt[:], w2_scales_raw[:].rearrange("p a (n m t) -> p (a n) t m", n=2, t=PACK)
         )
-
-        pick_words(1)
-        w1_low = held("w1_low", [P, 2 * PASS], BF16)
-        w1_high = held("w1_high", [P, 2 * PASS], BF16)
-        round_w1(nc.vector.tensor_copy, w1_low, t_pairs[0], 1, 0, every_m, t_pairs[0])
-        round_w1(nc.scalar.copy, w1_high, t_pairs[0], 1, 0, every_m, t_pairs[1])
-        quantize_w1(w1_low, 1, 0, t_pairs[0])
-        quantize_w1(w1_high, 1, 0, t_pairs[1])
 
         h = {(b, t): held(f"h{b}{t}", [P, S], F32) for b in range(2) for t in range(PACK)}
 
         def failure_probabilities(b, t):
             cols = slice(t * P, (t + 1) * P)
             for half in range(2):
-                bank = psum.tile([P, BANK], F32, name="bank")
+                bank = psum.tile([P, BANK], F32, name=f"bank{(2 * (PACK * b + t) + half) % 6}")
                 for a in range(2):
                     nc.tensor.matmul_mx(
                         out=bank[:],
                         lhsT=w1_codes[a, b][:, cols].bitcast(FP8X4),
                         lhsT_scale=w1_scales[a, b][:, cols],
-                        rhs=picked[a, half][:].bitcast(FP8X4),
+                        rhs=picked[a, half].bitcast(FP8X4),
                         rhs_scale=picked_scales[4 + 4 * a : P, half * BANK : (half + 1) * BANK],
                         start=(a == 0),
                         stop=(a == 1),
@@ -171,7 +197,7 @@ def tile_list_fault_tree_risk_kernel(
             weight = severity[:, firsts["b"], t : t + 1]
             nc.scalar.activation(firsts["rest"][:, t, :], firsts["first"][:, t, :], ACT.Identity, bias=weight, scale=-1.0)
 
-        def gate_tiles(pool, firsts, gates):
+        def gate_tiles(second, firsts, gates):
             b = firsts["b"]
             width = gates.stop - gates.start
             local = slice(gates.start - firsts["gates"].start, gates.stop - firsts["gates"].start)
@@ -181,66 +207,74 @@ def tile_list_fault_tree_risk_kernel(
                 "gates": gates,
                 "first": firsts["first"][:, :, local],
                 "rest": firsts["rest"][:, :, local],
-                "second": pool.tile([P, PACK, width], F32, name=f"gathered{b}", align_bytes=64),
-                "z": held(f"z{name}", [P, width * PACK], BF16),
-                "codes": held(f"z_codes{name}", [P, width], U32),
+                "second": second,
+                                "codes": held(f"z_codes{name}", [P, width], U32),
                 "scales": held(f"z_scales{name}", [P, width], U8),
             }
 
         def second_input(tiles, t):
             fetch_times(tiles["second"][:, t, :], tiles["rest"][:, t, :], tiles["b"], t, p2, tiles["gates"])
 
-        def join(tiles):
+        def join(tiles, tag, cols=slice(0, Y_COLS)):
+            tiles["z", cols.start] = held(tag, [P, PACK * (cols.stop - cols.start)], BF16)
             nc.vector.tensor_tensor(
-                out=tiles["z"][:].rearrange("p (c i t) -> p c t i", i=2, t=PACK),
-                in0=tiles["first"].rearrange("p t (c i) -> p c t i", i=2),
-                in1=tiles["second"][:].rearrange("p t (c i) -> p c t i", i=2),
+                out=tiles["z", cols.start][:].rearrange("p (c i t) -> p c t i", i=2, t=PACK),
+                in0=tiles["first"][:, :, cols].rearrange("p t (c i) -> p c t i", i=2),
+                in1=tiles["second"][:, :, cols].rearrange("p t (c i) -> p c t i", i=2),
                 op=ALU.add,
             )
 
-        def quantize_z(tiles):
-            nc.vector.quantize_mx(out=tiles["codes"][:].bitcast(FP8X4), scales=tiles["scales"][:], in_=tiles["z"][:])
+        def quantize_z(tiles, cols=slice(0, Y_COLS)):
+            nc.vector.quantize_mx(
+                out=tiles["codes"][:, cols].bitcast(FP8X4), scales=tiles["scales"][:, cols], in_=tiles["z", cols.start][:]
+            )
 
         lower_firsts = first_tiles(keep, "first_lower", "rest", 0, slice(0, G))
-        lower = gate_tiles(keep, lower_firsts, slice(0, G))
+        lower = gate_tiles(held("second_lower", [P, PACK, G], F32)[:], lower_firsts, slice(0, G))
         w1_upper = [held(f"w1_upper{a}", [P, PACK * PASS], BF16) for a in range(2)]
 
         def round_upper(copy, a, ms, pair):
             round_w1(copy, w1_upper[a], t_pairs[pair], a, 1, ms, t_pairs[pair])
 
         failure_probabilities(0, 0)
-        round_upper(nc.vector.tensor_copy, 0, every_m, 0)
-        round_upper(nc.vector.tensor_copy, 0, m_halves[0], 1)
         for t in range(PACK):
             first_input(lower_firsts, t)
             if t + 1 < PACK:
                 failure_probabilities(0, t + 1)
             else:
-                round_upper(nc.scalar.copy, 0, m_halves[1], 1)
-                for ms in m_halves:
-                    round_upper(nc.scalar.copy, 1, ms, 0)
+                for pair in range(2):
+                    round_upper(nc.scalar.copy, 0, every_m, pair)
             remainder(lower_firsts, t)
             if t > 0:
                 second_input(lower, t - 1)
-        for ms in m_halves:
-            round_upper(nc.scalar.copy, 1, ms, 1)
-        for a in range(2):
-            quantize_w1(w1_upper[a], a, 1, every_t)
+        for pair in range(2):
+            round_upper(nc.scalar.copy, 1, every_m, pair)
         second_input(lower, PACK - 1)
+        gate_halves = (slice(0, G // 2), slice(G // 2, G))
+        quantize_w1(w1_upper[0], 0, 1, every_t)
+        join(lower, "w1_upper0", gate_halves[0])
+        quantize_w1(w1_upper[1], 1, 1, every_t)
         for t in range(PACK):
             failure_probabilities(1, t)
         upper_firsts = first_tiles(keep, "w1_raw00", "rest", 1, slice(0, G))
+        join(lower, "w1_upper1", gate_halves[1])
+        quantize_z(lower, gate_halves[0])
         first_input(upper_firsts, 0)
-        join(lower)
-        first_input(upper_firsts, 1)
-        quantize_z(lower)
-        for t in range(2, PACK):
+        quantize_z(lower, gate_halves[1])
+        for t in range(1, PACK):
             first_input(upper_firsts, t)
         for t in range(PACK):
             remainder(upper_firsts, t)
 
+        chunks = G // Y_COLS
         y_codes = held("y_codes", [P, 2, G], U32)
         y_scales = held("y_scales", [P, 2, G], U8)
+        y_bf = {}
+        y = {}
+        banks = {}
+
+        def chunk_gates(c):
+            return slice(c * Y_COLS, (c + 1) * Y_COLS)
 
         def risk_passes(bank, n, a, codes, scales):
             for t in range(PACK):
@@ -254,70 +288,71 @@ def tile_list_fault_tree_risk_kernel(
                     stop=(a == 1 and t == PACK - 1),
                 )
 
-        def risk_bank(upper, n):
-            gates = upper["gates"]
-            bank = psum.tile([P, PACK, Y_COLS], F32, name="bank")
-            risk_passes(bank, n, 0, lower["codes"][:, gates], lower["scales"][:, gates])
-            risk_passes(bank, n, 1, upper["codes"][:], upper["scales"][:])
-            return {"bank": bank, "gates": gates, "n": n}
+        def risk_scores(c):
+            y_bf[c] = held(f"y_bf{c}", [P, 2, Y_COLS, PACK], BF16)
+            for n in range(2):
+                banks[c, n] = psum.tile([P, PACK, Y_COLS], F32, name=f"bank{6 - 2 * (c % 2) + n}")
+                y[c, n] = held(f"y{c}{n}", [P, PACK, Y_COLS], F32)
+                risk_passes(banks[c, n], n, 0, lower["codes"][:, chunk_gates(c)], lower["scales"][:, chunk_gates(c)])
+            for n in range(2):
+                risk_passes(banks[c, n], n, 1, upper[c]["codes"][:], upper[c]["scales"][:])
 
-        def planes_of(scores, copy):
-            gates, n = scores["gates"], scores["n"]
-            y_bf = held(f"y_bf{gates.start}_{n}", [P, Y_COLS, PACK], BF16)
-            copy(y_bf[:], scores["bank"][:].rearrange("p t m -> p m t"))
-            nc.vector.quantize_mx(
-                out=y_codes[:, n, gates].bitcast(FP8X4),
-                scales=y_scales[:, n, gates],
-                in_=y_bf[:].rearrange("p m t -> p (m t)"),
-            )
+        def round_scores(copy, c, n):
+            copy(y_bf[c][:, n, :, :], banks[c, n][:].rearrange("p t m -> p m t"))
 
-        def store_scores(scores):
-            gates, n = scores["gates"], scores["n"]
-            y = held(f"y{gates.start}_{n}", [P, PACK, Y_COLS], F32)
-            nc.scalar.copy(y[:], scores["bank"][:])
-            rows = out_0[n * PASS : (n + 1) * PASS, gates]
-            nc.sync.dma_start(rows.rearrange("(p t) m -> p t m", t=PACK), y[:])
+        def store_scores(copy, c, n):
+            copy(y[c, n][:], banks[c, n][:])
+            rows = out_0[n * PASS : (n + 1) * PASS, chunk_gates(c)]
+            nc.sync.dma_start(rows.rearrange("(p t) m -> p t m", t=PACK), y[c, n][:])
 
-        def store_codes(gates):
+        def planes(c):
+            for n in range(2):
+                nc.vector.quantize_mx(
+                    out=y_codes[:, n, chunk_gates(c)].bitcast(FP8X4),
+                    scales=y_scales[:, n, chunk_gates(c)],
+                    in_=y_bf[c][:, n, :, :].rearrange("p m t -> p (m t)"),
+                )
             words = out_1.rearrange("n p m t -> p n (m t)").bitcast(I32)
-            nc.sync.dma_start(words[:, :, gates], y_codes[:, :, gates].bitcast(I32))
+            nc.sync.dma_start(words[:, :, chunk_gates(c)], y_codes[:, :, chunk_gates(c)].bitcast(I32))
 
-        chunk_gates = [slice(m0, m0 + Y_COLS) for m0 in range(0, G, Y_COLS)]
-        upper = [gate_tiles(ring, upper_firsts, chunk_gates[0])]
+        def empty_banks(c):
+            for n in range(2):
+                round_scores(nc.scalar.copy, c, n)
+            for n in range(2):
+                store_scores(nc.scalar.copy, c, n)
+
+        seconds = held("second_upper", [P, PACK + 1, Y_COLS], F32)
+        upper = [gate_tiles(seconds[:, 0:PACK, :], upper_firsts, chunk_gates(0))]
         for t in range(PACK):
             second_input(upper[0], t)
-        for chunk in range(1, len(chunk_gates)):
-            upper.append(gate_tiles(ring, upper_firsts, chunk_gates[chunk]))
-            second_input(upper[chunk], 0)
-            join(upper[chunk - 1])
-            second_input(upper[chunk], 1)
-            quantize_z(upper[chunk - 1])
-            for t in range(2, PACK):
-                second_input(upper[chunk], t)
-            if chunk + 1 < len(chunk_gates):
-                for n in range(2):
-                    scores = risk_bank(upper[chunk - 1], n)
-                    planes_of(scores, nc.scalar.copy)
-                    store_scores(scores)
-                store_codes(chunk_gates[chunk - 1])
+        for c in range(1, chunks):
+            shift = c % 2
+            upper.append(gate_tiles(seconds[:, shift : shift + PACK, :], upper_firsts, chunk_gates(c)))
+            order = list(reversed(range(PACK))) if shift else list(range(PACK))
+            second_input(upper[c], order[0])
+            join(upper[c - 1], f"y_bf{c - 3}" if c >= 3 else f"z{c - 1}")
+            second_input(upper[c], order[1])
+            quantize_z(upper[c - 1])
+            risk_scores(c - 1)
+            empty_banks(c - 1)
+            for t in order[2:]:
+                second_input(upper[c], t)
+            if 2 <= c < chunks - 1:
+                planes(c - 2)
+        last = chunks - 1
+        join(upper[last], "z_last")
+        planes(last - 2)
+        quantize_z(upper[last])
+        planes(last - 1)
+        risk_scores(last)
+        store_scores(nc.scalar.copy, last, 0)
+        store_scores(nc.vector.tensor_copy, last, 1)
+        round_scores(nc.scalar.copy, last, 0)
+        round_scores(nc.vector.tensor_copy, last, 1)
+        planes(last)
 
-        before_last = [risk_bank(upper[-2], n) for n in range(2)]
-        store_scores(before_last[0])
-        join(upper[-1])
-        quantize_z(upper[-1])
-        planes_of(before_last[1], nc.vector.tensor_copy)
-        store_scores(before_last[1])
-        planes_of(before_last[0], nc.vector.tensor_copy)
-        store_codes(chunk_gates[-2])
-        last = [risk_bank(upper[-1], n) for n in range(2)]
-        store_scores(last[0])
-        planes_of(last[1], nc.vector.tensor_copy)
-        planes_of(last[0], nc.scalar.copy)
-        store_scores(last[1])
-        store_codes(chunk_gates[-1])
-
-        for q in range(4):
-            (nc.sync if q < 2 else nc.scalar).dma_start(
-                out_2[:, q:16:4, :].rearrange("n r m -> r n m").bitcast(I32),
-                y_scales[q:P:32, :, :].bitcast(I32),
+        for r in range(4):
+            (nc.sync if r < 2 else nc.scalar).dma_start(
+                out_2[:, r:16:4, :].rearrange("n q m -> q n m").bitcast(I32),
+                y_scales[r:P:32, :, :].bitcast(I32),
             )

@@ -19,9 +19,13 @@ ACT = mybir.ActivationFunctionType
 P = 128
 PACK = 4
 PASS = P * PACK
+QUAD = 32
+ROWS = 4
 BANK = 512
 LANES = 16
-Y_COLS = 128
+LINE = 16
+CHUNK = 128
+H_BANKS = 6
 
 
 def tile_list_fault_tree_risk_kernel(
@@ -30,78 +34,61 @@ def tile_list_fault_tree_risk_kernel(
     nc = tc.nc
     with ExitStack() as ctx:
         keep = ctx.enter_context(tc.tile_pool(name="keep", bufs=1))
+        shared = ctx.enter_context(tc.tile_pool(name="shared", bufs=1))
         psum = ctx.enter_context(tc.psum_pool(name="psum", bufs=1))
 
         def held(name, shape, dtype):
             return keep.tile(shape, dtype, name=name, align_bytes=64)
 
+        def tenant(name, shape, dtype, offset):
+            return shared.tile(shape, dtype, name=name, align_bytes=64, offset=offset)
+
         idx = keep.tile([P, S // LANES], U16, name="idx")
         p1 = keep.tile([P, G // LANES], U16, name="p1")
         p2 = keep.tile([P, G // LANES], U16, name="p2")
         table = [held(f"table{a}", [P, T], U32) for a in range(2)]
-        table_scales = held("table_scales", [P, T], U8)
-        w1_raw = {(a, b): held(f"w1_raw{a}{b}", [P, PACK, PASS], F32) for a, b in ((0, 0), (0, 1), (1, 1))}
-        w2_raw = held("w2_raw", [P, 2, 2 * N], U8)
-        w2_scales_raw = held("w2_scales_raw", [P, 2, N], U8)
+        table_scales = tenant("table_scales", [P, T], U8, 0)
+        w1_raw = {(a, 0): held(f"w1_raw{a}0", [P, PACK, PASS], F32) for a in range(2)}
         severity = held("severity", [P, 2, PACK], F32)
 
         def load_w1(a, b):
             rows = w1[a * PASS : (a + 1) * PASS, b * PASS : (b + 1) * PASS]
             nc.sync.dma_start(w1_raw[a, b][:], rows.rearrange("(p j) c -> p j c", j=PACK))
 
-        w1_late = [held(f"w1_late{half}", [P, PACK, PASS // 2], F32) for half in range(2)]
-
-        def load_w1_late(half):
-            rows = w1[PASS : 2 * PASS, half * PASS // 2 : (half + 1) * PASS // 2]
-            nc.sync.dma_start(w1_late[half][:], rows.rearrange("(p j) c -> p j c", j=PACK))
-
-        def load_table(a):
-            nc.sync.dma_start(table[a][:].bitcast(I32), tab_words[a].rearrange("p n i -> p (n i)").bitcast(I32))
-
-        def load_table_scales(a, r):
-            nc.sync.dma_start(table_scales[4 + 4 * a + r : P : 32, :].bitcast(I32), tab_scales[a, r:16:4, :].bitcast(I32))
-
         warm = held("warm", [P, 2], F32)
         nc.gpsimd.memset(warm[:, 0:1], 0.0)
         nc.scalar.activation(warm[:, 1:2], warm[:, 0:1], ACT.Sigmoid)
 
         nc.vector.memset(table_scales[:].bitcast(I32), 0)
-        nc.vector.memset(w2_scales_raw[:].rearrange("p a c -> p (a c)").bitcast(I32), 0)
+        w2_planes = [held(f"w2_plane{a}", [P, N], U8) for a in range(2)]
+        nc.vector.memset(w2_planes[1][:].bitcast(I32), 0)
 
-        def load_w2_scales(r):
-            nc.sync.dma_start(
-                w2_scales_raw[r:P:32, :, :].bitcast(I32),
-                w2_scales[:, r:16:4, :].rearrange("a q c -> q a c").bitcast(I32),
-            )
-
-        scale_rows = [(a, r) for r in range(4) for a in range(2)]
-        nc.sync.dma_start(severity[:], g.rearrange("(b p t) -> p b t", b=2, t=PACK))
-        load_table(0)
-        nc.sync.dma_start(idx[:], offs)
-        for a, r in scale_rows[:4]:
-            load_table_scales(a, r)
         load_w1(0, 0)
-        for a, r in scale_rows[4:]:
-            load_table_scales(a, r)
-        load_table(1)
-        load_w1_late(0)
-        load_w1_late(1)
+        nc.sync.dma_start(severity[:], g.rearrange("(b p t) -> p b t", b=2, t=PACK))
+        nc.sync.dma_start(idx[:], offs)
+        for a in range(2):
+            nc.sync.dma_start(table_scales[ROWS * a : P : 2 * ROWS, :].bitcast(I32), tab_scales[a].bitcast(I32))
         nc.sync.dma_start(p1[:], pos1)
-        nc.sync.dma_start(w2_raw[:].bitcast(I32), w2_words.rearrange("a p c -> p a c").bitcast(I32))
-        for r in range(4):
-            load_w2_scales(r)
         nc.sync.dma_start(p2[:], pos2)
-        load_w1(0, 1)
-        load_w1(1, 1)
-
-        severity_rows = held("severity_rows", [P, 2, PACK, G], F32)
-        nc.scalar.copy(severity_rows[:], severity[:].unsqueeze(3).to_broadcast([P, 2, PACK, G]))
+        for a in range(2):
+            nc.sync.dma_start(table[a][:].bitcast(I32), tab_words[a].rearrange("p n i -> p (n i)").bitcast(I32))
+        load_w1(1, 0)
 
         picked_scales = held("picked_scales", [P, S], U8)
+        table_planes = held("table_planes", [P, S], U8)
+        nc.vector.tensor_copy(picked_scales[:], table_scales[:].indirect(idx[:]))
+        nc.vector.tensor_copy(table_planes[:].bitcast(I32), picked_scales[:].bitcast(I32))
+        for a in range(2):
+            for r in range(1, ROWS):
+                nc.scalar.dma_start(
+                    table_planes[ROWS * a + r : P : QUAD, :].bitcast(I32),
+                    picked_scales[ROWS * a + 2 * ROWS * r : P : QUAD, :].bitcast(I32),
+                )
+
         picked = {}
 
-        def pick_words(a, tag):
-            both = held(tag, [P, S], U32)
+        def pick_words(a, name):
+            both = held(name, [P, S], U32)
             for half in range(2):
                 picked[a, half] = both[:, half * BANK : (half + 1) * BANK]
                 entries = idx[:, half * BANK // LANES : (half + 1) * BANK // LANES]
@@ -111,70 +98,78 @@ def tile_list_fault_tree_risk_kernel(
         w1_codes = {key: held(f"w1_codes{key[0]}{key[1]}", [P, PASS], U32) for key in blocks[1:]}
         w1_scales = {key: held(f"w1_scales{key[0]}{key[1]}", [P, PASS], U8) for key in blocks}
 
-        def round_w1(copy, rounded, into, a, b, ms, ts):
-            dealt = rounded[:].rearrange("p (t m j) -> p m j t", m=P, j=PACK)
-            raw = w1_raw[a, b][:].rearrange("p j (m t) -> p m j t", t=PACK)
-            copy(dealt[:, ms, :, into], raw[:, ms, :, ts])
+        def round_columns(rounded, a, b, half):
+            ms = slice(half * P // 2, (half + 1) * P // 2)
+            dealt = rounded[:].rearrange("p (u e m j) -> p m u j e", u=2, e=2, j=PACK)
+            raw = w1_raw[a, b][:].rearrange("p j (m u e) -> p m u j e", u=2, e=2)
+            nc.scalar.copy(dealt[:, ms], raw[:, ms])
 
-        def quantize_w1(rounded, a, b, ts):
-            cols = slice(ts.start * P, ts.stop * P)
+        def round_pair(copy, rounded, a, b, u):
+            dealt = rounded[:].rearrange("p (e m j) -> p m j e", e=2, j=PACK)
+            raw = w1_raw[a, b][:].rearrange("p j (m u e) -> p u m j e", u=2, e=2)
+            copy(dealt, raw[:, u])
+
+        def quantize_w1(rounded, a, b, cols):
             nc.vector.quantize_mx(
                 out=w1_codes[a, b][:, cols].bitcast(FP8X4), scales=w1_scales[a, b][:, cols], in_=rounded[:]
             )
 
-        every_t = slice(0, PACK)
-        every_m = slice(0, P)
-        m_halves = (slice(0, P // 2), slice(P // 2, P))
-        t_pairs = (slice(0, 2), slice(2, 4))
+        w1_codes[0, 0] = tenant("w1_codes00", [P, PASS], U32, 0)
+        w1_first = held("w1_first", [P, PACK * PASS], BF16)
+        for half in range(2):
+            round_columns(w1_first, 0, 0, half)
+        quantize_w1(w1_first, 0, 0, slice(0, PASS))
+
+        w2_raw = held("w1_raw00", [P, 2, 2 * N], U8)
+        nc.sync.dma_start(w2_raw[:].bitcast(I32), w2_words.rearrange("a p c -> p a c").bitcast(I32))
+        w2_scales_raw = tenant("w2_scales_raw", [P, N], U8, T // 2)
+        nc.vector.memset(w2_scales_raw[:].bitcast(I32), 0)
+        for quad in range(P // QUAD):
+            nc.sync.dma_start(
+                w2_scales_raw[QUAD * quad : QUAD * quad + 2 * ROWS, :].bitcast(I32),
+                w2_scales[:, ROWS * quad : ROWS * (quad + 1), :].bitcast(I32),
+            )
+
+        severity_rows = held("severity_rows", [P, 2, PACK, G], F32)
+        nc.scalar.copy(severity_rows[:], severity[:].unsqueeze(3).to_broadcast([P, 2, PACK, G]))
 
         pick_words(0, "picked0")
-        nc.vector.tensor_copy(picked_scales[:], table_scales[:].indirect(idx[:]))
-        w1_codes[0, 0] = held("table_scales", [P, PASS], U32)
-        w1_first = held("w1_first", [P, PACK * PASS], BF16)
-        for ts in t_pairs:
-            round_w1(nc.scalar.copy, w1_first, ts, 0, 0, every_m, ts)
-        quantize_w1(w1_first, 0, 0, every_t)
-
         pick_words(1, "w1_first")
-        w1_low = held("w1_low", [P, 2 * PASS], BF16)
-        w1_high = held("w1_high", [P, 2 * PASS], BF16)
+        for a in range(2):
+            w1_raw[a, 1] = held(f"table{a}", [P, PACK, PASS], F32)
+            load_w1(a, 1)
 
-        def round_late(copy, rounded, half, pair):
-            dealt = rounded[:].rearrange("p (t m j) -> p m j t", m=P, j=PACK)
-            raw = w1_late[half][:].rearrange("p j (m t) -> p m j t", t=PACK)
-            copy(dealt[:, m_halves[half], :, :], raw[:, :, :, t_pairs[pair]])
-
-        round_late(nc.scalar.copy, w1_low, 0, 0)
-        round_late(nc.scalar.copy, w1_high, 0, 1)
-        round_late(nc.vector.tensor_copy, w1_low, 1, 0)
-        round_late(nc.scalar.copy, w1_high, 1, 1)
-        quantize_w1(w1_low, 1, 0, t_pairs[0])
-        quantize_w1(w1_high, 1, 0, t_pairs[1])
+        w1_pairs = [held(f"w1_pair{u}", [P, 2 * PASS], BF16) for u in range(2)]
+        round_pair(nc.vector.tensor_copy, w1_pairs[0], 1, 0, 0)
+        round_pair(nc.scalar.copy, w1_pairs[1], 1, 0, 1)
+        for u in range(2):
+            quantize_w1(w1_pairs[u], 1, 0, slice(2 * u * P, 2 * (u + 1) * P))
 
         w2_dealt = held("w2_dealt", [P, 4, PACK, 2 * P], U8)
         nc.vector.tensor_copy(
-            w2_dealt[:].bitcast(U16),
-            w2_raw[:].bitcast(U16).rearrange("p a (n m t) -> p (a n) t m", n=2, t=PACK),
+            w2_dealt[:].bitcast(U16).rearrange("p s t (c i) -> p s c t i", i=LINE // 2),
+            w2_raw[:].bitcast(U16).rearrange("p a (n c i t) -> p (a n) c t i", n=2, i=LINE // 2, t=PACK),
         )
-
-        w2_scales_dealt = held("w2_scales_dealt", [P, 4, PACK, P], U8)
         nc.vector.tensor_copy(
-            w2_scales_dealt[:], w2_scales_raw[:].rearrange("p a (n m t) -> p (a n) t m", n=2, t=PACK)
+            w2_planes[0][:].rearrange("p (n t c i) -> p n c t i", n=2, t=PACK, i=LINE),
+            w2_scales_raw[:].rearrange("p (n c i t) -> p n c t i", n=2, t=PACK, i=LINE),
         )
+        for r in range(ROWS):
+            nc.sync.dma_start(w2_planes[1][r:P:QUAD, :].bitcast(I32), w2_planes[0][ROWS + r : P : QUAD, :].bitcast(I32))
 
         h = {(b, t): held(f"h{b}{t}", [P, S], F32) for b in range(2) for t in range(PACK)}
 
         def failure_probabilities(b, t):
             cols = slice(t * P, (t + 1) * P)
             for half in range(2):
-                bank = psum.tile([P, BANK], F32, name=f"bank{(2 * (PACK * b + t) + half) % 6}")
+                bank = psum.tile([P, BANK], F32, name=f"bank{(2 * (PACK * b + t) + half) % H_BANKS}")
                 for a in range(2):
                     nc.tensor.matmul_mx(
                         out=bank[:],
                         lhsT=w1_codes[a, b][:, cols].bitcast(FP8X4),
                         lhsT_scale=w1_scales[a, b][:, cols],
                         rhs=picked[a, half].bitcast(FP8X4),
-                        rhs_scale=picked_scales[4 + 4 * a : P, half * BANK : (half + 1) * BANK],
+                        rhs_scale=table_planes[ROWS * a : P, half * BANK : (half + 1) * BANK],
                         start=(a == 0),
                         stop=(a == 1),
                     )
@@ -184,104 +179,102 @@ def tile_list_fault_tree_risk_kernel(
             entries = places[:, gates.start // LANES : gates.stop // LANES]
             nc.vector.tensor_tensor(out=dst, in0=h[b, t][:].indirect(entries), in1=factor, op=ALU.mult)
 
-        def first_tiles(pool, first_tag, rest_tag, b, gates):
-            shape = [P, PACK, gates.stop - gates.start]
-            first = pool.tile(shape, F32, name=first_tag, align_bytes=64)
-            return {"b": b, "gates": gates, "first": first, "rest": held(rest_tag, shape, F32)}
+        all_gates = slice(0, G)
+        first = {}
+        rest = {}
 
-        def first_input(firsts, t):
-            b, gates = firsts["b"], firsts["gates"]
-            fetch_times(firsts["first"][:, t, :], severity_rows[:, b, t, gates], b, t, p1, gates)
+        def first_input(b, t):
+            fetch_times(first[b][:, t, :], severity_rows[:, b, t, :], b, t, p1, all_gates)
 
-        def remainder(firsts, t):
-            weight = severity[:, firsts["b"], t : t + 1]
-            nc.scalar.activation(firsts["rest"][:, t, :], firsts["first"][:, t, :], ACT.Identity, bias=weight, scale=-1.0)
+        def remainder(b, t):
+            weight = severity[:, b, t : t + 1]
+            nc.scalar.activation(rest[b][:, t, :], first[b][:, t, :], ACT.Identity, bias=weight, scale=-1.0)
 
-        def gate_tiles(second, firsts, gates):
-            b = firsts["b"]
-            width = gates.stop - gates.start
-            local = slice(gates.start - firsts["gates"].start, gates.stop - firsts["gates"].start)
-            name = f"{b}_{gates.start}"
-            return {
-                "b": b,
-                "gates": gates,
-                "first": firsts["first"][:, :, local],
-                "rest": firsts["rest"][:, :, local],
-                "second": second,
-                                "codes": held(f"z_codes{name}", [P, width], U32),
-                "scales": held(f"z_scales{name}", [P, width], U8),
-            }
+        def second_input(second, b, t, gates):
+            fetch_times(second[:, t, :], rest[b][:, t, gates], b, t, p2, gates)
 
-        def second_input(tiles, t):
-            fetch_times(tiles["second"][:, t, :], tiles["rest"][:, t, :], tiles["b"], t, p2, tiles["gates"])
-
-        def join(tiles, tag, cols=slice(0, Y_COLS)):
-            tiles["z", cols.start] = held(tag, [P, PACK * (cols.stop - cols.start)], BF16)
+        def join(z, b, gates, second):
             nc.vector.tensor_tensor(
-                out=tiles["z", cols.start][:].rearrange("p (c i t) -> p c t i", i=2, t=PACK),
-                in0=tiles["first"][:, :, cols].rearrange("p t (c i) -> p c t i", i=2),
-                in1=tiles["second"][:, :, cols].rearrange("p t (c i) -> p c t i", i=2),
+                out=z[:].rearrange("p (c i t) -> p c t i", i=PACK, t=PACK),
+                in0=first[b][:, :, gates].rearrange("p t (c i) -> p c t i", i=PACK),
+                in1=second.rearrange("p t (c i) -> p c t i", i=PACK),
                 op=ALU.add,
             )
 
-        def quantize_z(tiles, cols=slice(0, Y_COLS)):
-            nc.vector.quantize_mx(
-                out=tiles["codes"][:, cols].bitcast(FP8X4), scales=tiles["scales"][:, cols], in_=tiles["z", cols.start][:]
-            )
+        def quantize_z(codes, scales, z):
+            nc.vector.quantize_mx(out=codes.bitcast(FP8X4), scales=scales, in_=z[:])
 
-        lower_firsts = first_tiles(keep, "first_lower", "rest", 0, slice(0, G))
-        lower = gate_tiles(held("second_lower", [P, PACK, G], F32)[:], lower_firsts, slice(0, G))
-        w1_upper = [held(f"w1_upper{a}", [P, PACK * PASS], BF16) for a in range(2)]
-
-        def round_upper(copy, a, ms, pair):
-            round_w1(copy, w1_upper[a], t_pairs[pair], a, 1, ms, t_pairs[pair])
+        first[0] = held("first_lower", [P, PACK, G], F32)
+        rest[0] = held("rest", [P, PACK, G], F32)
+        second_lower = held("second_lower", [P, PACK, G], F32)
+        lower_codes = held("lower_codes", [P, G], U32)
+        lower_scales = held("lower_scales", [P, G], U8)
 
         failure_probabilities(0, 0)
-        for t in range(PACK):
-            first_input(lower_firsts, t)
-            if t + 1 < PACK:
-                failure_probabilities(0, t + 1)
-            else:
-                for pair in range(2):
-                    round_upper(nc.scalar.copy, 0, every_m, pair)
-            remainder(lower_firsts, t)
+        for t in range(PACK - 1):
+            first_input(0, t)
+            failure_probabilities(0, t + 1)
+            remainder(0, t)
             if t > 0:
-                second_input(lower, t - 1)
-        for pair in range(2):
-            round_upper(nc.scalar.copy, 1, every_m, pair)
-        second_input(lower, PACK - 1)
+                second_input(second_lower, 0, t - 1, all_gates)
+        first_input(0, PACK - 1)
+        w1_upper = [tenant("w1_upper0", [P, PACK * PASS], BF16, 0)]
+        for half in range(2):
+            round_columns(w1_upper[0], 0, 1, half)
+        remainder(0, PACK - 1)
+        second_input(second_lower, 0, PACK - 2, all_gates)
+        w1_upper.append(held("w1_codes10", [P, PACK * PASS], BF16))
+        for half in range(2):
+            round_columns(w1_upper[1], 1, 1, half)
+        second_input(second_lower, 0, PACK - 1, all_gates)
+
         gate_halves = (slice(0, G // 2), slice(G // 2, G))
-        quantize_w1(w1_upper[0], 0, 1, every_t)
-        join(lower, "w1_upper0", gate_halves[0])
-        quantize_w1(w1_upper[1], 1, 1, every_t)
+        quantize_w1(w1_upper[0], 0, 1, slice(0, PASS))
+        z_lower = [tenant("z_first", [P, PACK * G // 2], BF16, 0)]
+        join(z_lower[0], 0, gate_halves[0], second_lower[:, :, gate_halves[0]])
+        quantize_w1(w1_upper[1], 1, 1, slice(0, PASS))
         for t in range(PACK):
             failure_probabilities(1, t)
-        upper_firsts = first_tiles(keep, "w1_raw00", "rest", 1, slice(0, G))
-        join(lower, "w1_upper1", gate_halves[1])
-        quantize_z(lower, gate_halves[0])
-        first_input(upper_firsts, 0)
-        quantize_z(lower, gate_halves[1])
-        for t in range(1, PACK):
-            first_input(upper_firsts, t)
+        first[1] = held("w1_raw10", [P, PACK, G], F32)
+        rest[1] = held("rest", [P, PACK, G], F32)
+        z_lower.append(held("w1_codes10", [P, PACK * G // 2], BF16))
+        join(z_lower[1], 0, gate_halves[1], second_lower[:, :, gate_halves[1]])
+        for z, gates in zip(z_lower, gate_halves):
+            quantize_z(lower_codes[:, gates], lower_scales[:, gates], z)
+
         for t in range(PACK):
-            remainder(upper_firsts, t)
+            first_input(1, t)
+        for t in range(PACK):
+            remainder(1, t)
 
-        chunks = G // Y_COLS
-        y_codes = held("y_codes", [P, 2, G], U32)
+        chunk_gates = [slice(m0, m0 + CHUNK) for m0 in range(0, G, CHUNK)]
+        last = len(chunk_gates) - 1
         y_scales = held("y_scales", [P, 2, G], U8)
-        y_bf = {}
-        y = {}
-        banks = {}
+        upper_codes, upper_scales, z_upper, banks, y, y_bf = {}, {}, {}, {}, {}, {}
 
-        def chunk_gates(c):
-            return slice(c * Y_COLS, (c + 1) * Y_COLS)
+        seconds = held("second_upper", [P, PACK + 1, CHUNK], F32)
 
-        def risk_passes(bank, n, a, codes, scales):
+        def second_rows(c):
+            return seconds[:, c % 2 : c % 2 + PACK, :]
+
+        def open_chunk(c):
+            upper_codes[c] = held(f"upper_codes{c}", [P, CHUNK], U32)
+            upper_scales[c] = held(f"upper_scales{c}", [P, CHUNK], U8)
+            return list(reversed(range(PACK))) if c % 2 else list(range(PACK))
+
+        def second_upper(c, t):
+            second_input(second_rows(c), 1, t, chunk_gates[c])
+
+        def join_upper(c):
+            z_upper[c] = held(f"z{c}", [P, PACK * CHUNK], BF16)
+            join(z_upper[c], 1, chunk_gates[c], second_rows(c))
+
+        def risk_passes(c, n, a, codes, scales):
             for t in range(PACK):
                 nc.tensor.matmul_mx(
-                    out=bank[:, t, :],
+                    out=banks[c, n][:, t, :],
                     lhsT=w2_dealt[:, 2 * a + n, t, :].bitcast(FP4X4),
-                    lhsT_scale=w2_scales_dealt[:, 2 * a + n, t, :],
+                    lhsT_scale=w2_planes[a][:, (PACK * n + t) * P : (PACK * n + t + 1) * P],
                     rhs=codes.bitcast(FP8X4),
                     rhs_scale=scales,
                     start=(a == 0 and t == 0),
@@ -289,70 +282,76 @@ def tile_list_fault_tree_risk_kernel(
                 )
 
         def risk_scores(c):
-            y_bf[c] = held(f"y_bf{c}", [P, 2, Y_COLS, PACK], BF16)
+            y_bf[c] = held(f"y_bf{c}", [P, 2, CHUNK, PACK], BF16)
             for n in range(2):
-                banks[c, n] = psum.tile([P, PACK, Y_COLS], F32, name=f"bank{6 - 2 * (c % 2) + n}")
-                y[c, n] = held(f"y{c}{n}", [P, PACK, Y_COLS], F32)
-                risk_passes(banks[c, n], n, 0, lower["codes"][:, chunk_gates(c)], lower["scales"][:, chunk_gates(c)])
+                banks[c, n] = psum.tile([P, PACK, CHUNK], F32, name=f"bank{H_BANKS - 2 * (c % 2) + n}")
+                y[c, n] = held(f"y{c}{n}", [P, PACK, CHUNK], F32)
+                risk_passes(c, n, 0, lower_codes[:, chunk_gates[c]], lower_scales[:, chunk_gates[c]])
             for n in range(2):
-                risk_passes(banks[c, n], n, 1, upper[c]["codes"][:], upper[c]["scales"][:])
-
-        def round_scores(copy, c, n):
-            copy(y_bf[c][:, n, :, :], banks[c, n][:].rearrange("p t m -> p m t"))
+                risk_passes(c, n, 1, upper_codes[c][:], upper_scales[c][:])
 
         def store_scores(copy, c, n):
             copy(y[c, n][:], banks[c, n][:])
-            rows = out_0[n * PASS : (n + 1) * PASS, chunk_gates(c)]
+            rows = out_0[n * PASS : (n + 1) * PASS, chunk_gates[c]]
             nc.sync.dma_start(rows.rearrange("(p t) m -> p t m", t=PACK), y[c, n][:])
 
-        def planes(c):
-            for n in range(2):
-                nc.vector.quantize_mx(
-                    out=y_codes[:, n, chunk_gates(c)].bitcast(FP8X4),
-                    scales=y_scales[:, n, chunk_gates(c)],
-                    in_=y_bf[c][:, n, :, :].rearrange("p m t -> p (m t)"),
-                )
-            words = out_1.rearrange("n p m t -> p n (m t)").bitcast(I32)
-            nc.sync.dma_start(words[:, :, chunk_gates(c)], y_codes[:, :, chunk_gates(c)].bitcast(I32))
+        def round_scores(copy, c, n):
+            copy(
+                y_bf[c][:, n, :, :].rearrange("p (c i) t -> p c t i", i=PACK),
+                banks[c, n][:].rearrange("p t (c i) -> p c t i", i=PACK),
+            )
 
-        def empty_banks(c):
-            for n in range(2):
-                round_scores(nc.scalar.copy, c, n)
-            for n in range(2):
-                store_scores(nc.scalar.copy, c, n)
-
-        seconds = held("second_upper", [P, PACK + 1, Y_COLS], F32)
-        upper = [gate_tiles(seconds[:, 0:PACK, :], upper_firsts, chunk_gates(0))]
-        for t in range(PACK):
-            second_input(upper[0], t)
-        for c in range(1, chunks):
-            shift = c % 2
-            upper.append(gate_tiles(seconds[:, shift : shift + PACK, :], upper_firsts, chunk_gates(c)))
-            order = list(reversed(range(PACK))) if shift else list(range(PACK))
-            second_input(upper[c], order[0])
-            join(upper[c - 1], f"y_bf{c - 3}" if c >= 3 else f"z{c - 1}")
-            second_input(upper[c], order[1])
-            quantize_z(upper[c - 1])
+        for t in open_chunk(0):
+            second_upper(0, t)
+        for c in range(1, last + 1):
+            order = open_chunk(c)
+            second_upper(c, order[0])
+            join_upper(c - 1)
+            second_upper(c, order[1])
+            quantize_z(upper_codes[c - 1][:], upper_scales[c - 1][:], z_upper[c - 1])
             risk_scores(c - 1)
-            empty_banks(c - 1)
+            for n in range(2):
+                store_scores(nc.scalar.copy, c - 1, n)
+            for n in range(2):
+                round_scores(nc.scalar.copy, c - 1, n)
             for t in order[2:]:
-                second_input(upper[c], t)
-            if 2 <= c < chunks - 1:
-                planes(c - 2)
-        last = chunks - 1
-        join(upper[last], "z_last")
-        planes(last - 2)
-        quantize_z(upper[last])
-        planes(last - 1)
-        risk_scores(last)
-        store_scores(nc.scalar.copy, last, 0)
-        store_scores(nc.vector.tensor_copy, last, 1)
-        round_scores(nc.scalar.copy, last, 0)
-        round_scores(nc.vector.tensor_copy, last, 1)
-        planes(last)
+                second_upper(c, t)
 
-        for r in range(4):
-            (nc.sync if r < 2 else nc.scalar).dma_start(
-                out_2[:, r:16:4, :].rearrange("n q m -> q n m").bitcast(I32),
-                y_scales[r:P:32, :, :].bitcast(I32),
+        y_codes = held(f"z{last - 1}", [P, 2, G], U32)
+
+        def quantize_y(c, n):
+            nc.vector.quantize_mx(
+                out=y_codes[:, n, chunk_gates[c]].bitcast(FP8X4),
+                scales=y_scales[:, n, chunk_gates[c]],
+                in_=y_bf[c][:, n, :, :].rearrange("p m t -> p (m t)"),
+            )
+
+        def store_codes(c):
+            words = out_1.rearrange("n p m t -> p n (m t)").bitcast(I32)
+            nc.sync.dma_start(words[:, :, chunk_gates[c]], y_codes[:, :, chunk_gates[c]].bitcast(I32))
+
+        quantize_y(0, 0)
+        join_upper(last)
+        quantize_y(0, 1)
+        store_codes(0)
+        quantize_z(upper_codes[last][:], upper_scales[last][:], z_upper[last])
+        for c in range(1, last):
+            for n in range(2):
+                quantize_y(c, n)
+            store_codes(c)
+
+        risk_scores(last)
+        copies = (nc.scalar.copy, nc.vector.tensor_copy)
+        for n in range(2):
+            store_scores(copies[n], last, n)
+        for n in range(2):
+            round_scores(copies[n], last, n)
+        for n in range(2):
+            quantize_y(last, n)
+        store_codes(last)
+
+        for r in range(ROWS):
+            (nc.sync if r < ROWS // 2 else nc.scalar).dma_start(
+                out_2[:, r : LANES : ROWS, :].rearrange("n q m -> q n m").bitcast(I32),
+                y_scales[r:P:QUAD, :, :].bitcast(I32),
             )

@@ -98,16 +98,13 @@ def tile_list_fault_tree_risk_kernel(
         w1_codes = {key: held(f"w1_codes{key[0]}{key[1]}", [P, PASS], U32) for key in blocks[1:]}
         w1_scales = {key: held(f"w1_scales{key[0]}{key[1]}", [P, PASS], U8) for key in blocks}
 
-        def round_columns(rounded, a, b, half):
-            ms = slice(half * P // 2, (half + 1) * P // 2)
-            dealt = rounded[:].rearrange("p (u e m j) -> p m u j e", u=2, e=2, j=PACK)
-            raw = w1_raw[a, b][:].rearrange("p j (m u e) -> p m u j e", u=2, e=2)
-            nc.scalar.copy(dealt[:, ms], raw[:, ms])
-
         def round_pair(copy, rounded, a, b, u):
-            dealt = rounded[:].rearrange("p (e m j) -> p m j e", e=2, j=PACK)
             raw = w1_raw[a, b][:].rearrange("p j (m u e) -> p u m j e", u=2, e=2)
-            copy(dealt, raw[:, u])
+            copy(rounded.rearrange("p (e m j) -> p m j e", e=2, j=PACK), raw[:, u])
+
+        def round_block(rounded, a, b):
+            for u in range(2):
+                round_pair(nc.scalar.copy, rounded[:, 2 * u * PASS : 2 * (u + 1) * PASS], a, b, u)
 
         def quantize_w1(rounded, a, b, cols):
             nc.vector.quantize_mx(
@@ -116,8 +113,7 @@ def tile_list_fault_tree_risk_kernel(
 
         w1_codes[0, 0] = tenant("w1_codes00", [P, PASS], U32, 0)
         w1_first = held("w1_first", [P, PACK * PASS], BF16)
-        for half in range(2):
-            round_columns(w1_first, 0, 0, half)
+        round_block(w1_first, 0, 0)
         quantize_w1(w1_first, 0, 0, slice(0, PASS))
 
         w2_raw = held("w1_raw00", [P, 2, 2 * N], U8)
@@ -140,8 +136,8 @@ def tile_list_fault_tree_risk_kernel(
             load_w1(a, 1)
 
         w1_pairs = [held(f"w1_pair{u}", [P, 2 * PASS], BF16) for u in range(2)]
-        round_pair(nc.vector.tensor_copy, w1_pairs[0], 1, 0, 0)
-        round_pair(nc.scalar.copy, w1_pairs[1], 1, 0, 1)
+        round_pair(nc.vector.tensor_copy, w1_pairs[0][:], 1, 0, 0)
+        round_pair(nc.scalar.copy, w1_pairs[1][:], 1, 0, 1)
         for u in range(2):
             quantize_w1(w1_pairs[u], 1, 0, slice(2 * u * P, 2 * (u + 1) * P))
 
@@ -218,26 +214,26 @@ def tile_list_fault_tree_risk_kernel(
             if t > 0:
                 second_input(second_lower, 0, t - 1, all_gates)
         first_input(0, PACK - 1)
-        w1_upper = [tenant("w1_upper0", [P, PACK * PASS], BF16, 0)]
-        for half in range(2):
-            round_columns(w1_upper[0], 0, 1, half)
+        w1_upper = tenant("w1_upper", [P, PACK * PASS], BF16, 0)
+        round_block(w1_upper, 0, 1)
         remainder(0, PACK - 1)
         second_input(second_lower, 0, PACK - 2, all_gates)
-        w1_upper.append(held("w1_codes10", [P, PACK * PASS], BF16))
-        for half in range(2):
-            round_columns(w1_upper[1], 1, 1, half)
+        last_pairs = [held(name, [P, 2 * PASS], BF16) for name in ("w1_codes10", "w1_pair1")]
+        for u in range(2):
+            round_pair(nc.scalar.copy, last_pairs[u][:], 1, 1, u)
         second_input(second_lower, 0, PACK - 1, all_gates)
 
         gate_halves = (slice(0, G // 2), slice(G // 2, G))
-        quantize_w1(w1_upper[0], 0, 1, slice(0, PASS))
-        z_lower = [tenant("z_first", [P, PACK * G // 2], BF16, 0)]
+        quantize_w1(w1_upper, 0, 1, slice(0, PASS))
+        quantize_w1(last_pairs[0], 1, 1, slice(0, 2 * P))
+        z_lower = [held("w1_codes10", [P, PACK * G // 2], BF16)]
         join(z_lower[0], 0, gate_halves[0], second_lower[:, :, gate_halves[0]])
-        quantize_w1(w1_upper[1], 1, 1, slice(0, PASS))
+        quantize_w1(last_pairs[1], 1, 1, slice(2 * P, PASS))
         for t in range(PACK):
             failure_probabilities(1, t)
         first[1] = held("w1_raw10", [P, PACK, G], F32)
         rest[1] = held("rest", [P, PACK, G], F32)
-        z_lower.append(held("w1_codes10", [P, PACK * G // 2], BF16))
+        z_lower.append(held("w1_pair1", [P, PACK * G // 2], BF16))
         join(z_lower[1], 0, gate_halves[1], second_lower[:, :, gate_halves[1]])
         for z, gates in zip(z_lower, gate_halves):
             quantize_z(lower_codes[:, gates], lower_scales[:, gates], z)
@@ -352,6 +348,6 @@ def tile_list_fault_tree_risk_kernel(
 
         for r in range(ROWS):
             (nc.sync if r < ROWS // 2 else nc.scalar).dma_start(
-                out_2[:, r : LANES : ROWS, :].rearrange("n q m -> q n m").bitcast(I32),
+                out_2[:, r::ROWS, :].rearrange("n q m -> q n m").bitcast(I32),
                 y_scales[r:P:QUAD, :, :].bitcast(I32),
             )

@@ -60,14 +60,16 @@ def tile_list_fault_tree_risk_kernel(
         nc.scalar.activation(warm[:, 1:2], warm[:, 0:1], ACT.Sigmoid)
 
         nc.vector.memset(table_scales[:].bitcast(I32), 0)
+        w2_scales_raw = held("w2_scales_raw", [P, N], U8)
+        nc.gpsimd.memset(w2_scales_raw[:].bitcast(I32), 0)
         w2_planes = [held(f"w2_plane{a}", [P, N], U8) for a in range(2)]
         nc.vector.memset(w2_planes[1][:].bitcast(I32), 0)
 
         load_w1(0, 0)
         nc.sync.dma_start(severity[:], g.rearrange("(b p t) -> p b t", b=2, t=PACK))
         nc.sync.dma_start(idx[:], offs)
-        for a in range(2):
-            nc.sync.dma_start(table_scales[ROWS * a : P : 2 * ROWS, :].bitcast(I32), tab_scales[a].bitcast(I32))
+        nc.sync.dma_start(table_scales[0:P:ROWS].bitcast(I32), tab_scales.rearrange("a q t -> q a t").bitcast(I32))
+        nc.sync.dma_start(w2_scales_raw[0:P:ROWS].bitcast(I32), w2_scales.rearrange("a q c -> q a c").bitcast(I32))
         nc.sync.dma_start(p1[:], pos1)
         nc.sync.dma_start(p2[:], pos2)
         for a in range(2):
@@ -83,6 +85,16 @@ def tile_list_fault_tree_risk_kernel(
                 nc.scalar.dma_start(
                     table_planes[ROWS * a + r : P : QUAD, :].bitcast(I32),
                     picked_scales[ROWS * a + 2 * ROWS * r : P : QUAD, :].bitcast(I32),
+                )
+
+        nc.vector.tensor_copy(
+            w2_planes[0][:].rearrange("p (n t c i) -> p n c t i", n=2, t=PACK, i=LINE),
+            w2_scales_raw[:].rearrange("p (n c i t) -> p n c t i", n=2, t=PACK, i=LINE),
+        )
+        for a in range(2):
+            for r in range(1 - a, ROWS):
+                nc.gpsimd.dma_start(
+                    w2_planes[a][r:P:QUAD].bitcast(I32), w2_planes[0][2 * ROWS * r + ROWS * a : P : QUAD].bitcast(I32)
                 )
 
         picked = {}
@@ -118,13 +130,6 @@ def tile_list_fault_tree_risk_kernel(
 
         w2_raw = held("w1_raw00", [P, 2, 2 * N], U8)
         nc.sync.dma_start(w2_raw[:].bitcast(I32), w2_words.rearrange("a p c -> p a c").bitcast(I32))
-        w2_scales_raw = tenant("w2_scales_raw", [P, N], U8, T // 2)
-        nc.vector.memset(w2_scales_raw[:].bitcast(I32), 0)
-        for quad in range(P // QUAD):
-            nc.sync.dma_start(
-                w2_scales_raw[QUAD * quad : QUAD * quad + 2 * ROWS, :].bitcast(I32),
-                w2_scales[:, ROWS * quad : ROWS * (quad + 1), :].bitcast(I32),
-            )
 
         severity_rows = held("severity_rows", [P, 2, PACK, G], F32)
         nc.scalar.copy(severity_rows[:], severity[:].unsqueeze(3).to_broadcast([P, 2, PACK, G]))
@@ -146,12 +151,6 @@ def tile_list_fault_tree_risk_kernel(
             w2_dealt[:].bitcast(U16).rearrange("p s t (c i) -> p s c t i", i=LINE // 2),
             w2_raw[:].bitcast(U16).rearrange("p a (n c i t) -> p (a n) c t i", n=2, i=LINE // 2, t=PACK),
         )
-        nc.vector.tensor_copy(
-            w2_planes[0][:].rearrange("p (n t c i) -> p n c t i", n=2, t=PACK, i=LINE),
-            w2_scales_raw[:].rearrange("p (n c i t) -> p n c t i", n=2, t=PACK, i=LINE),
-        )
-        for r in range(ROWS):
-            nc.sync.dma_start(w2_planes[1][r:P:QUAD, :].bitcast(I32), w2_planes[0][ROWS + r : P : QUAD, :].bitcast(I32))
 
         h = {(b, t): held(f"h{b}{t}", [P, S], F32) for b in range(2) for t in range(PACK)}
 

@@ -290,10 +290,10 @@ def tile_list_fault_tree_risk_kernel(
             rows = out_0[n * PASS : (n + 1) * PASS, chunk_gates[c]]
             nc.sync.dma_start(rows.rearrange("(p t) m -> p t m", t=PACK), y[c, n][:])
 
-        def round_scores(copy, c, n):
+        def round_scores(copy, c, n, source):
             copy(
                 y_bf[c][:, n, :, :].rearrange("p (c i) t -> p c t i", i=PACK),
-                banks[c, n][:].rearrange("p t (c i) -> p c t i", i=PACK),
+                source[c, n][:].rearrange("p t (c i) -> p c t i", i=PACK),
             )
 
         for t in open_chunk(0):
@@ -307,8 +307,8 @@ def tile_list_fault_tree_risk_kernel(
             risk_scores(c - 1)
             for n in range(2):
                 store_scores(nc.scalar.copy, c - 1, n)
-            for n in range(2):
-                round_scores(nc.scalar.copy, c - 1, n)
+            for n in range(1 if c == last else 2):
+                round_scores(nc.scalar.copy, c - 1, n, banks)
             for t in order[2:]:
                 second_upper(c, t)
 
@@ -330,6 +330,7 @@ def tile_list_fault_tree_risk_kernel(
         quantize_y(0, 1)
         store_codes(0)
         quantize_z(upper_codes[last][:], upper_scales[last][:], z_upper[last])
+        round_scores(nc.vector.tensor_copy, last - 1, 1, y)
         for c in range(1, last):
             for n in range(2):
                 quantize_y(c, n)
@@ -340,7 +341,7 @@ def tile_list_fault_tree_risk_kernel(
         for n in range(2):
             store_scores(copies[n], last, n)
         for n in range(2):
-            round_scores(copies[n], last, n)
+            round_scores(copies[n], last, n, banks if n == 0 else y)
         for n in range(2):
             quantize_y(last, n)
         store_codes(last)

@@ -101,18 +101,17 @@ def tile_list_fault_tree_risk_kernel(
 
         def pick_words(a, name):
             both = held(name, [P, S], U32)
+            nc.vector.tensor_copy(both[:], table[a][:].indirect(idx[:]))
             for half in range(2):
                 picked[a, half] = both[:, half * BANK : (half + 1) * BANK]
-                entries = idx[:, half * BANK // LANES : (half + 1) * BANK // LANES]
-                nc.vector.tensor_copy(picked[a, half], table[a][:].indirect(entries))
 
         blocks = [(a, b) for a in range(2) for b in range(2)]
         w1_codes = {key: held(f"w1_codes{key[0]}{key[1]}", [P, PASS], U32) for key in blocks[1:]}
         w1_scales = {key: held(f"w1_scales{key[0]}{key[1]}", [P, PASS], U8) for key in blocks}
 
-        def round_pair(copy, rounded, a, b, u):
+        def round_pair(copy, rounded, a, b, u, words=slice(0, P)):
             raw = w1_raw[a, b][:].rearrange("p j (m u e) -> p u m j e", u=2, e=2)
-            copy(rounded.rearrange("p (e m j) -> p m j e", e=2, j=PACK), raw[:, u])
+            copy(rounded.rearrange("p (e m j) -> p m j e", e=2, j=PACK)[:, words], raw[:, u, words])
 
         def round_block(rounded, a, b):
             for u in range(2):
@@ -141,7 +140,8 @@ def tile_list_fault_tree_risk_kernel(
             load_w1(a, 1)
 
         w1_pairs = [held(f"w1_pair{u}", [P, 2 * PASS], BF16) for u in range(2)]
-        round_pair(nc.vector.tensor_copy, w1_pairs[0][:], 1, 0, 0)
+        round_pair(nc.scalar.copy, w1_pairs[0][:], 1, 0, 0, slice(P - QUAD, P))
+        round_pair(nc.vector.tensor_copy, w1_pairs[0][:], 1, 0, 0, slice(0, P - QUAD))
         round_pair(nc.scalar.copy, w1_pairs[1][:], 1, 0, 1)
         for u in range(2):
             quantize_w1(w1_pairs[u], 1, 0, slice(2 * u * P, 2 * (u + 1) * P))
@@ -197,12 +197,12 @@ def tile_list_fault_tree_risk_kernel(
             )
 
         def quantize_z(codes, scales, z):
-            nc.vector.quantize_mx(out=codes.bitcast(FP8X4), scales=scales, in_=z[:])
+            nc.vector.quantize_mx(out=codes.bitcast(FP8X4), scales=scales, in_=z)
 
         first[0] = held("first_lower", [P, PACK, G], F32)
         rest[0] = held("rest", [P, PACK, G], F32)
         second_lower = held("second_lower", [P, PACK, G], F32)
-        lower_codes = held("lower_codes", [P, G], U32)
+        lower_codes = held("lower_codes", [P, G - CHUNK], U32)
         lower_scales = held("lower_scales", [P, G], U8)
 
         failure_probabilities(0, 0)
@@ -234,8 +234,9 @@ def tile_list_fault_tree_risk_kernel(
         rest[1] = held("rest", [P, PACK, G], F32)
         z_lower.append(held("w1_pair1", [P, PACK * G // 2], BF16))
         join(z_lower[1], 0, gate_halves[1], second_lower[:, :, gate_halves[1]])
-        for z, gates in zip(z_lower, gate_halves):
-            quantize_z(lower_codes[:, gates], lower_scales[:, gates], z)
+        quantize_z(lower_codes[:, gate_halves[0]], lower_scales[:, gate_halves[0]], z_lower[0][:])
+        third = slice(G // 2, G - CHUNK)
+        quantize_z(lower_codes[:, third], lower_scales[:, third], z_lower[1][:, : PACK * CHUNK])
 
         for t in range(PACK):
             first_input(1, t)
@@ -261,7 +262,7 @@ def tile_list_fault_tree_risk_kernel(
             second_input(second_rows(c), 1, t, chunk_gates[c])
 
         def join_upper(c):
-            z_upper[c] = held(f"z{c}", [P, PACK * CHUNK], BF16)
+            z_upper[c] = tenant(f"z{c}", [P, PACK * CHUNK], BF16, 2 * T - (last - 1 - c) * T // 4 + (c == last) * T)
             join(z_upper[c], 1, chunk_gates[c], second_rows(c))
 
         def risk_passes(c, n, a, codes, scales):
@@ -281,14 +282,14 @@ def tile_list_fault_tree_risk_kernel(
             for n in range(2):
                 banks[c, n] = psum.tile([P, PACK, CHUNK], F32, name=f"bank{H_BANKS - 2 * (c % 2) + n}")
                 y[c, n] = held(f"y{c}{n}", [P, PACK, CHUNK], F32)
-                risk_passes(c, n, 0, lower_codes[:, chunk_gates[c]], lower_scales[:, chunk_gates[c]])
+                risk_passes(c, n, 0, last_codes[:] if c == last else lower_codes[:, chunk_gates[c]], lower_scales[:, chunk_gates[c]])
             for n in range(2):
                 risk_passes(c, n, 1, upper_codes[c][:], upper_scales[c][:])
 
-        def store_scores(copy, c, n):
-            copy(y[c, n][:], banks[c, n][:])
+        def store_scores(copy, c, n, slices=slice(0, PACK)):
+            copy(y[c, n][:, slices], banks[c, n][:, slices])
             rows = out_0[n * PASS : (n + 1) * PASS, chunk_gates[c]]
-            nc.sync.dma_start(rows.rearrange("(p t) m -> p t m", t=PACK), y[c, n][:])
+            nc.sync.dma_start(rows.rearrange("(p t) m -> p t m", t=PACK)[:, slices], y[c, n][:, slices])
 
         def round_scores(copy, c, n, source):
             copy(
@@ -296,23 +297,7 @@ def tile_list_fault_tree_risk_kernel(
                 source[c, n][:].rearrange("p t (c i) -> p c t i", i=PACK),
             )
 
-        for t in open_chunk(0):
-            second_upper(0, t)
-        for c in range(1, last + 1):
-            order = open_chunk(c)
-            second_upper(c, order[0])
-            join_upper(c - 1)
-            second_upper(c, order[1])
-            quantize_z(upper_codes[c - 1][:], upper_scales[c - 1][:], z_upper[c - 1])
-            risk_scores(c - 1)
-            for n in range(2):
-                store_scores(nc.scalar.copy, c - 1, n)
-            for n in range(1 if c == last else 2):
-                round_scores(nc.scalar.copy, c - 1, n, banks)
-            for t in order[2:]:
-                second_upper(c, t)
-
-        y_codes = held(f"z{last - 1}", [P, 2, G], U32)
+        y_codes = tenant("y_codes", [P, 2, G], U32, 4 * T)
 
         def quantize_y(c, n):
             nc.vector.quantize_mx(
@@ -321,20 +306,43 @@ def tile_list_fault_tree_risk_kernel(
                 in_=y_bf[c][:, n, :, :].rearrange("p m t -> p (m t)"),
             )
 
-        def store_codes(c):
+        def store_codes(gates):
             words = out_1.rearrange("n p m t -> p n (m t)").bitcast(I32)
-            nc.sync.dma_start(words[:, :, chunk_gates[c]], y_codes[:, :, chunk_gates[c]].bitcast(I32))
+            nc.sync.dma_start(words[:, :, gates], y_codes[:, :, gates].bitcast(I32))
 
-        quantize_y(0, 0)
+        for t in open_chunk(0):
+            second_upper(0, t)
+        for c in range(1, last + 1):
+            order = open_chunk(c)
+            second_upper(c, order[0])
+            join_upper(c - 1)
+            second_upper(c, order[1])
+            quantize_z(upper_codes[c - 1][:], upper_scales[c - 1][:], z_upper[c - 1][:])
+            risk_scores(c - 1)
+            for n in range(2):
+                store_scores(nc.scalar.copy, c - 1, n)
+            for n in range(1 if c == last else 2):
+                round_scores(nc.scalar.copy, c - 1, n, banks)
+            if c == last:
+                for n in range(2):
+                    quantize_y(0, n)
+                store_codes(chunk_gates[0])
+            for t in order[2:]:
+                second_upper(c, t)
+
+                last_codes = tenant("last_codes", [P, CHUNK], U32, 2 * T)
+
+        quantize_z(last_codes[:], lower_scales[:, chunk_gates[last]], z_lower[1][:, PACK * CHUNK :])
         join_upper(last)
-        quantize_y(0, 1)
-        store_codes(0)
-        quantize_z(upper_codes[last][:], upper_scales[last][:], z_upper[last])
+        quantize_y(1, 0)
+        quantize_z(upper_codes[last][:], upper_scales[last][:], z_upper[last][:])
+        quantize_y(1, 1)
+        store_codes(chunk_gates[1])
         round_scores(nc.vector.tensor_copy, last - 1, 1, y)
-        for c in range(1, last):
+        for c in range(2, last):
             for n in range(2):
                 quantize_y(c, n)
-            store_codes(c)
+            store_codes(chunk_gates[c])
 
         risk_scores(last)
         copies = (nc.scalar.copy, nc.vector.tensor_copy)
@@ -344,7 +352,7 @@ def tile_list_fault_tree_risk_kernel(
             round_scores(copies[n], last, n, banks if n == 0 else y)
         for n in range(2):
             quantize_y(last, n)
-        store_codes(last)
+        store_codes(chunk_gates[last])
 
         for r in range(ROWS):
             (nc.sync if r < ROWS // 2 else nc.scalar).dma_start(

@@ -62,8 +62,7 @@ def tile_list_fault_tree_risk_kernel(
         nc.vector.memset(table_scales[:].bitcast(I32), 0)
         w2_scales_raw = held("w2_scales_raw", [P, N], U8)
         nc.gpsimd.memset(w2_scales_raw[:].bitcast(I32), 0)
-        w2_planes = [held(f"w2_plane{a}", [P, N], U8) for a in range(2)]
-        nc.vector.memset(w2_planes[1][:].bitcast(I32), 0)
+        w2_planes = [held("w2_plane0", [P, N], U8)]
 
         load_w1(0, 0)
         nc.sync.dma_start(severity[:], g.rearrange("(b p t) -> p b t", b=2, t=PACK))
@@ -91,12 +90,6 @@ def tile_list_fault_tree_risk_kernel(
             w2_planes[0][:].rearrange("p (n t c i) -> p n c t i", n=2, t=PACK, i=LINE),
             w2_scales_raw[:].rearrange("p (n c i t) -> p n c t i", n=2, t=PACK, i=LINE),
         )
-        for a in range(2):
-            for r in range(1 - a, ROWS):
-                nc.gpsimd.dma_start(
-                    w2_planes[a][r:P:QUAD].bitcast(I32), w2_planes[0][2 * ROWS * r + ROWS * a : P : QUAD].bitcast(I32)
-                )
-
         picked = {}
 
         def pick_words(a, name):
@@ -152,6 +145,13 @@ def tile_list_fault_tree_risk_kernel(
             w2_raw[:].bitcast(U16).rearrange("p a (n c i t) -> p (a n) c t i", n=2, i=LINE // 2, t=PACK),
         )
 
+        plane_tiles = [w2_planes[0], held("w1_pair0", [P, N], U8)]
+        nc.vector.tensor_copy(plane_tiles[1][:].bitcast(I32), w2_planes[0][:].bitcast(I32))
+        for a in (1, 0):
+            for r in range(1 - a, ROWS):
+                nc.sync.dma_start(
+                    plane_tiles[a][r:P:QUAD].bitcast(I32), plane_tiles[1 - a][2 * ROWS * r + ROWS * a : P : QUAD].bitcast(I32)
+                )
         h = {(b, t): held(f"h{b}{t}", [P, S], F32) for b in range(2) for t in range(PACK)}
 
         def failure_probabilities(b, t):
@@ -270,7 +270,7 @@ def tile_list_fault_tree_risk_kernel(
                 nc.tensor.matmul_mx(
                     out=banks[c, n][:, t, :],
                     lhsT=w2_dealt[:, 2 * a + n, t, :].bitcast(FP4X4),
-                    lhsT_scale=w2_planes[a][:, (PACK * n + t) * P : (PACK * n + t + 1) * P],
+                    lhsT_scale=plane_tiles[a][:, (PACK * n + t) * P : (PACK * n + t + 1) * P],
                     rhs=codes.bitcast(FP8X4),
                     rhs_scale=scales,
                     start=(a == 0 and t == 0),

@@ -59,10 +59,9 @@ def tile_list_fault_tree_risk_kernel(
         nc.gpsimd.memset(warm[:, 0:1], 0.0)
         nc.scalar.activation(warm[:, 1:2], warm[:, 0:1], ACT.Sigmoid)
 
-        nc.vector.memset(table_scales[:].bitcast(I32), 0)
         w2_scales_raw = held("w2_scales_raw", [P, N], U8)
+        nc.vector.memset(table_scales[:].bitcast(I32), 0)
         nc.gpsimd.memset(w2_scales_raw[:].bitcast(I32), 0)
-        w2_planes = [held("w2_plane0", [P, N], U8)]
 
         load_w1(0, 0)
         nc.sync.dma_start(severity[:], g.rearrange("(b p t) -> p b t", b=2, t=PACK))
@@ -86,10 +85,12 @@ def tile_list_fault_tree_risk_kernel(
                     picked_scales[ROWS * a + 2 * ROWS * r : P : QUAD, :].bitcast(I32),
                 )
 
+        w2_planes = [held("w2_plane0", [P, N], U8)]
         nc.vector.tensor_copy(
             w2_planes[0][:].rearrange("p (n t c i) -> p n c t i", n=2, t=PACK, i=LINE),
             w2_scales_raw[:].rearrange("p (n c i t) -> p n c t i", n=2, t=PACK, i=LINE),
         )
+
         picked = {}
 
         def pick_words(a, name):
@@ -133,8 +134,8 @@ def tile_list_fault_tree_risk_kernel(
             load_w1(a, 1)
 
         w1_pairs = [held(f"w1_pair{u}", [P, 2 * PASS], BF16) for u in range(2)]
-        round_pair(nc.scalar.copy, w1_pairs[0][:], 1, 0, 0, slice(P - QUAD, P))
-        round_pair(nc.vector.tensor_copy, w1_pairs[0][:], 1, 0, 0, slice(0, P - QUAD))
+        round_pair(nc.scalar.copy, w1_pairs[0][:], 1, 0, 0, slice(P - P // 4, P))
+        round_pair(nc.vector.tensor_copy, w1_pairs[0][:], 1, 0, 0, slice(0, P - P // 4))
         round_pair(nc.scalar.copy, w1_pairs[1][:], 1, 0, 1)
         for u in range(2):
             quantize_w1(w1_pairs[u], 1, 0, slice(2 * u * P, 2 * (u + 1) * P))
@@ -145,13 +146,13 @@ def tile_list_fault_tree_risk_kernel(
             w2_raw[:].bitcast(U16).rearrange("p a (n c i t) -> p (a n) c t i", n=2, i=LINE // 2, t=PACK),
         )
 
-        plane_tiles = [w2_planes[0], held("w1_pair0", [P, N], U8)]
-        nc.vector.tensor_copy(plane_tiles[1][:].bitcast(I32), w2_planes[0][:].bitcast(I32))
+        w2_planes.append(held("w1_pair0", [P, N], U8))
+        nc.sync.dma_start(w2_planes[1][:].bitcast(I32), w2_planes[0][:].bitcast(I32))
         for a in (1, 0):
             for r in range(1 - a, ROWS):
-                nc.sync.dma_start(
-                    plane_tiles[a][r:P:QUAD].bitcast(I32), plane_tiles[1 - a][2 * ROWS * r + ROWS * a : P : QUAD].bitcast(I32)
-                )
+                rows = w2_planes[1 - a][2 * ROWS * r + ROWS * a : P : QUAD]
+                nc.sync.dma_start(w2_planes[a][r:P:QUAD].bitcast(I32), rows.bitcast(I32))
+
         h = {(b, t): held(f"h{b}{t}", [P, S], F32) for b in range(2) for t in range(PACK)}
 
         def failure_probabilities(b, t):
@@ -181,9 +182,9 @@ def tile_list_fault_tree_risk_kernel(
         def first_input(b, t):
             fetch_times(first[b][:, t, :], severity_rows[:, b, t, :], b, t, p1, all_gates)
 
-        def remainder(b, t):
+        def remainder(b, t, gates=all_gates):
             weight = severity[:, b, t : t + 1]
-            nc.scalar.activation(rest[b][:, t, :], first[b][:, t, :], ACT.Identity, bias=weight, scale=-1.0)
+            nc.scalar.activation(rest[b][:, t, gates], first[b][:, t, gates], ACT.Identity, bias=weight, scale=-1.0)
 
         def second_input(second, b, t, gates):
             fetch_times(second[:, t, :], rest[b][:, t, gates], b, t, p2, gates)
@@ -235,16 +236,19 @@ def tile_list_fault_tree_risk_kernel(
         z_lower.append(held("w1_pair1", [P, PACK * G // 2], BF16))
         join(z_lower[1], 0, gate_halves[1], second_lower[:, :, gate_halves[1]])
         quantize_z(lower_codes[:, gate_halves[0]], lower_scales[:, gate_halves[0]], z_lower[0][:])
-        third = slice(G // 2, G - CHUNK)
-        quantize_z(lower_codes[:, third], lower_scales[:, third], z_lower[1][:, : PACK * CHUNK])
+        third_chunk = slice(G // 2, G - CHUNK)
+        quantize_z(lower_codes[:, third_chunk], lower_scales[:, third_chunk], z_lower[1][:, : PACK * CHUNK])
 
         for t in range(PACK):
             first_input(1, t)
         for t in range(PACK):
-            remainder(1, t)
+            remainder(1, t, slice(0, CHUNK))
+        for t in reversed(range(PACK)):
+            remainder(1, t, slice(CHUNK, G))
 
         chunk_gates = [slice(m0, m0 + CHUNK) for m0 in range(0, G, CHUNK)]
         last = len(chunk_gates) - 1
+        y_codes = held("y_codes", [P, 2, G], U32)
         y_scales = held("y_scales", [P, 2, G], U8)
         upper_codes, upper_scales, z_upper, banks, y, y_bf = {}, {}, {}, {}, {}, {}
 
@@ -262,7 +266,7 @@ def tile_list_fault_tree_risk_kernel(
             second_input(second_rows(c), 1, t, chunk_gates[c])
 
         def join_upper(c):
-            z_upper[c] = tenant(f"z{c}", [P, PACK * CHUNK], BF16, 2 * T - (last - 1 - c) * T // 4 + (c == last) * T)
+            z_upper[c] = held(f"z{c}", [P, PACK * CHUNK], BF16)
             join(z_upper[c], 1, chunk_gates[c], second_rows(c))
 
         def risk_passes(c, n, a, codes, scales):
@@ -270,34 +274,32 @@ def tile_list_fault_tree_risk_kernel(
                 nc.tensor.matmul_mx(
                     out=banks[c, n][:, t, :],
                     lhsT=w2_dealt[:, 2 * a + n, t, :].bitcast(FP4X4),
-                    lhsT_scale=plane_tiles[a][:, (PACK * n + t) * P : (PACK * n + t + 1) * P],
+                    lhsT_scale=w2_planes[a][:, (PACK * n + t) * P : (PACK * n + t + 1) * P],
                     rhs=codes.bitcast(FP8X4),
                     rhs_scale=scales,
                     start=(a == 0 and t == 0),
                     stop=(a == 1 and t == PACK - 1),
                 )
 
-        def risk_scores(c):
+        def risk_scores(c, lower):
             y_bf[c] = held(f"y_bf{c}", [P, 2, CHUNK, PACK], BF16)
             for n in range(2):
                 banks[c, n] = psum.tile([P, PACK, CHUNK], F32, name=f"bank{H_BANKS - 2 * (c % 2) + n}")
                 y[c, n] = held(f"y{c}{n}", [P, PACK, CHUNK], F32)
-                risk_passes(c, n, 0, last_codes[:] if c == last else lower_codes[:, chunk_gates[c]], lower_scales[:, chunk_gates[c]])
+                risk_passes(c, n, 0, lower, lower_scales[:, chunk_gates[c]])
             for n in range(2):
                 risk_passes(c, n, 1, upper_codes[c][:], upper_scales[c][:])
 
-        def store_scores(copy, c, n, slices=slice(0, PACK)):
-            copy(y[c, n][:, slices], banks[c, n][:, slices])
+        def store_scores(copy, c, n):
+            copy(y[c, n][:], banks[c, n][:])
             rows = out_0[n * PASS : (n + 1) * PASS, chunk_gates[c]]
-            nc.sync.dma_start(rows.rearrange("(p t) m -> p t m", t=PACK)[:, slices], y[c, n][:, slices])
+            nc.sync.dma_start(rows.rearrange("(p t) m -> p t m", t=PACK), y[c, n][:])
 
         def round_scores(copy, c, n, source):
             copy(
                 y_bf[c][:, n, :, :].rearrange("p (c i) t -> p c t i", i=PACK),
                 source[c, n][:].rearrange("p t (c i) -> p c t i", i=PACK),
             )
-
-        y_codes = tenant("y_codes", [P, 2, G], U32, 4 * T)
 
         def quantize_y(c, n):
             nc.vector.quantize_mx(
@@ -306,9 +308,9 @@ def tile_list_fault_tree_risk_kernel(
                 in_=y_bf[c][:, n, :, :].rearrange("p m t -> p (m t)"),
             )
 
-        def store_codes(gates):
+        def store_codes(c):
             words = out_1.rearrange("n p m t -> p n (m t)").bitcast(I32)
-            nc.sync.dma_start(words[:, :, gates], y_codes[:, :, gates].bitcast(I32))
+            nc.sync.dma_start(words[:, :, chunk_gates[c]], y_codes[:, :, chunk_gates[c]].bitcast(I32))
 
         for t in open_chunk(0):
             second_upper(0, t)
@@ -318,41 +320,40 @@ def tile_list_fault_tree_risk_kernel(
             join_upper(c - 1)
             second_upper(c, order[1])
             quantize_z(upper_codes[c - 1][:], upper_scales[c - 1][:], z_upper[c - 1][:])
-            risk_scores(c - 1)
+            risk_scores(c - 1, lower_codes[:, chunk_gates[c - 1]])
             for n in range(2):
                 store_scores(nc.scalar.copy, c - 1, n)
-            for n in range(1 if c == last else 2):
-                round_scores(nc.scalar.copy, c - 1, n, banks)
-            if c == last:
+            round_scores(nc.scalar.copy, c - 1, 0, banks)
+            if c < last:
+                round_scores(nc.scalar.copy, c - 1, 1, banks)
+            else:
                 for n in range(2):
                     quantize_y(0, n)
-                store_codes(chunk_gates[0])
+                store_codes(0)
             for t in order[2:]:
                 second_upper(c, t)
 
-                last_codes = tenant("last_codes", [P, CHUNK], U32, 2 * T)
-
+        last_codes = held(f"z{last - 1}", [P, CHUNK], U32)
         quantize_z(last_codes[:], lower_scales[:, chunk_gates[last]], z_lower[1][:, PACK * CHUNK :])
         join_upper(last)
         quantize_y(1, 0)
         quantize_z(upper_codes[last][:], upper_scales[last][:], z_upper[last][:])
         quantize_y(1, 1)
-        store_codes(chunk_gates[1])
+        store_codes(1)
         round_scores(nc.vector.tensor_copy, last - 1, 1, y)
-        for c in range(2, last):
-            for n in range(2):
-                quantize_y(c, n)
-            store_codes(chunk_gates[c])
+        for n in range(2):
+            quantize_y(last - 1, n)
+        store_codes(last - 1)
 
-        risk_scores(last)
+        risk_scores(last, last_codes[:])
         copies = (nc.scalar.copy, nc.vector.tensor_copy)
         for n in range(2):
             store_scores(copies[n], last, n)
         for n in range(2):
-            round_scores(copies[n], last, n, banks if n == 0 else y)
+            round_scores(copies[n], last, n, (banks, y)[n])
         for n in range(2):
             quantize_y(last, n)
-        store_codes(chunk_gates[last])
+        store_codes(last)
 
         for r in range(ROWS):
             (nc.sync if r < ROWS // 2 else nc.scalar).dma_start(

@@ -25,7 +25,8 @@ BANK = 512
 LANES = 16
 LINE = 16
 CHUNK = 128
-H_BANKS = 6
+H_BANKS = (6, 4)
+PSUM_BANKS = 8
 
 
 def tile_list_fault_tree_risk_kernel(
@@ -158,7 +159,7 @@ def tile_list_fault_tree_risk_kernel(
         def failure_probabilities(b, t):
             cols = slice(t * P, (t + 1) * P)
             for half in range(2):
-                bank = psum.tile([P, BANK], F32, name=f"bank{(2 * (PACK * b + t) + half) % H_BANKS}")
+                bank = psum.tile([P, BANK], F32, name=f"bank{(2 * (PACK * b + t) + half) % H_BANKS[b]}")
                 for a in range(2):
                     nc.tensor.matmul_mx(
                         out=bank[:],
@@ -284,16 +285,16 @@ def tile_list_fault_tree_risk_kernel(
         def risk_scores(c, lower):
             y_bf[c] = held(f"y_bf{c}", [P, 2, CHUNK, PACK], BF16)
             for n in range(2):
-                banks[c, n] = psum.tile([P, PACK, CHUNK], F32, name=f"bank{H_BANKS - 2 * (c % 2) + n}")
+                banks[c, n] = psum.tile([P, PACK, CHUNK], F32, name=f"bank{PSUM_BANKS - 2 - 2 * (c % 2) + n}")
                 y[c, n] = held(f"y{c}{n}", [P, PACK, CHUNK], F32)
                 risk_passes(c, n, 0, lower, lower_scales[:, chunk_gates[c]])
             for n in range(2):
                 risk_passes(c, n, 1, upper_codes[c][:], upper_scales[c][:])
 
-        def store_scores(copy, c, n):
+        def store_scores(copy, c, n, queue=nc.sync):
             copy(y[c, n][:], banks[c, n][:])
             rows = out_0[n * PASS : (n + 1) * PASS, chunk_gates[c]]
-            nc.sync.dma_start(rows.rearrange("(p t) m -> p t m", t=PACK), y[c, n][:])
+            queue.dma_start(rows.rearrange("(p t) m -> p t m", t=PACK), y[c, n][:])
 
         def round_scores(copy, c, n, source):
             copy(
@@ -323,10 +324,9 @@ def tile_list_fault_tree_risk_kernel(
             risk_scores(c - 1, lower_codes[:, chunk_gates[c - 1]])
             for n in range(2):
                 store_scores(nc.scalar.copy, c - 1, n)
-            round_scores(nc.scalar.copy, c - 1, 0, banks)
-            if c < last:
-                round_scores(nc.scalar.copy, c - 1, 1, banks)
-            else:
+            for n in range(2):
+                round_scores(nc.scalar.copy, c - 1, n, banks)
+            if c == last:
                 for n in range(2):
                     quantize_y(0, n)
                 store_codes(0)
@@ -340,7 +340,6 @@ def tile_list_fault_tree_risk_kernel(
         quantize_z(upper_codes[last][:], upper_scales[last][:], z_upper[last][:])
         quantize_y(1, 1)
         store_codes(1)
-        round_scores(nc.vector.tensor_copy, last - 1, 1, y)
         for n in range(2):
             quantize_y(last - 1, n)
         store_codes(last - 1)
@@ -348,7 +347,7 @@ def tile_list_fault_tree_risk_kernel(
         risk_scores(last, last_codes[:])
         copies = (nc.scalar.copy, nc.vector.tensor_copy)
         for n in range(2):
-            store_scores(copies[n], last, n)
+            store_scores(copies[n], last, n, (nc.scalar, nc.sync)[n])
         for n in range(2):
             round_scores(copies[n], last, n, (banks, y)[n])
         for n in range(2):
@@ -356,7 +355,7 @@ def tile_list_fault_tree_risk_kernel(
         store_codes(last)
 
         for r in range(ROWS):
-            (nc.sync if r < ROWS // 2 else nc.scalar).dma_start(
+            (nc.scalar if r else nc.sync).dma_start(
                 out_2[:, r::ROWS, :].rearrange("n q m -> q n m").bitcast(I32),
                 y_scales[r:P:QUAD, :, :].bitcast(I32),
             )

@@ -25,7 +25,7 @@ BANK = 512
 LANES = 16
 LINE = 16
 CHUNK = 128
-H_BANKS = (6, 4)
+H_BANKS = (6, 8)
 PSUM_BANKS = 8
 
 
@@ -204,48 +204,52 @@ def tile_list_fault_tree_risk_kernel(
         first[0] = held("first_lower", [P, PACK, G], F32)
         rest[0] = held("rest", [P, PACK, G], F32)
         second_lower = held("second_lower", [P, PACK, G], F32)
-        lower_codes = held("lower_codes", [P, G - CHUNK], U32)
+        lower_codes = held("lower_codes", [P, G // 2], U32)
         lower_scales = held("lower_scales", [P, G], U8)
 
-        failure_probabilities(0, 0)
-        for t in range(PACK - 1):
-            first_input(0, t)
-            failure_probabilities(0, t + 1)
-            remainder(0, t)
-            if t > 0:
-                second_input(second_lower, 0, t - 1, all_gates)
-        first_input(0, PACK - 1)
-        w1_upper = tenant("w1_upper", [P, PACK * PASS], BF16, 0)
-        round_block(w1_upper, 0, 1)
-        remainder(0, PACK - 1)
-        second_input(second_lower, 0, PACK - 2, all_gates)
-        last_pairs = [held(name, [P, 2 * PASS], BF16) for name in ("w1_codes10", "w1_pair1")]
-        for u in range(2):
-            round_pair(nc.scalar.copy, last_pairs[u][:], 1, 1, u)
-        second_input(second_lower, 0, PACK - 1, all_gates)
+        def round_upper(a, u, name):
+            shape = [P, 2 * PASS]
+            upper_pairs[a, u] = tenant("w1_upper", shape, BF16, 0) if (a, u) == (0, 0) else held(name, shape, BF16)
+            round_pair(nc.scalar.copy, upper_pairs[a, u][:], a, 1, u)
 
+        def quantize_upper(a, u):
+            quantize_w1(upper_pairs[a, u], a, 1, slice(2 * u * P, 2 * (u + 1) * P))
+
+        upper_pairs = {}
         gate_halves = (slice(0, G // 2), slice(G // 2, G))
-        quantize_w1(w1_upper, 0, 1, slice(0, PASS))
-        quantize_w1(last_pairs[0], 1, 1, slice(0, 2 * P))
-        z_lower = [held("w1_codes10", [P, PACK * G // 2], BF16)]
-        join(z_lower[0], 0, gate_halves[0], second_lower[:, :, gate_halves[0]])
-        quantize_w1(last_pairs[1], 1, 1, slice(2 * P, PASS))
+        for t in range(PACK - 1):
+            failure_probabilities(0, t)
+            first_input(0, t)
+        remainder(0, 0)
+        second_input(second_lower, 0, 0, all_gates)
+        failure_probabilities(0, PACK - 1)
+        first_input(0, PACK - 1)
+        remainder(0, 1)
+        second_input(second_lower, 0, 1, all_gates)
+        for a in range(2):
+            round_upper(a, 0, f"w1_codes{a}0")
+            quantize_upper(a, 0)
+            remainder(0, 2 + a)
+            if a == 0:
+                second_input(second_lower, 0, 2, all_gates)
+        for gates in gate_halves:
+            second_input(second_lower[:, :, gates], 0, PACK - 1, gates)
+        z_lower = [held(f"z_lower{i}", [P, PACK * G // 2], BF16) for i in range(2)]
+        for a in range(2):
+            round_upper(a, 1, f"w1_scales{a}0")
+            quantize_upper(a, 1)
+        for i in range(2):
+            join(z_lower[i], 0, gate_halves[i], second_lower[:, :, gate_halves[i]])
         for t in range(PACK):
             failure_probabilities(1, t)
         first[1] = held("w1_raw10", [P, PACK, G], F32)
         rest[1] = held("rest", [P, PACK, G], F32)
-        z_lower.append(held("w1_pair1", [P, PACK * G // 2], BF16))
-        join(z_lower[1], 0, gate_halves[1], second_lower[:, :, gate_halves[1]])
         quantize_z(lower_codes[:, gate_halves[0]], lower_scales[:, gate_halves[0]], z_lower[0][:])
-        third_chunk = slice(G // 2, G - CHUNK)
-        quantize_z(lower_codes[:, third_chunk], lower_scales[:, third_chunk], z_lower[1][:, : PACK * CHUNK])
 
         for t in range(PACK):
             first_input(1, t)
         for t in range(PACK):
-            remainder(1, t, slice(0, CHUNK))
-        for t in reversed(range(PACK)):
-            remainder(1, t, slice(CHUNK, G))
+            remainder(1, t)
 
         chunk_gates = [slice(m0, m0 + CHUNK) for m0 in range(0, G, CHUNK)]
         last = len(chunk_gates) - 1
@@ -253,18 +257,20 @@ def tile_list_fault_tree_risk_kernel(
         y_scales = held("y_scales", [P, 2, G], U8)
         upper_codes, upper_scales, z_upper, banks, y, y_bf = {}, {}, {}, {}, {}, {}
 
-        seconds = held("second_upper", [P, PACK + 1, CHUNK], F32)
+        seconds = held("second_upper", [P, PACK, 2 * CHUNK], F32)
 
         def second_rows(c):
-            return seconds[:, c % 2 : c % 2 + PACK, :]
-
-        def open_chunk(c):
-            upper_codes[c] = held(f"upper_codes{c}", [P, CHUNK], U32)
-            upper_scales[c] = held(f"upper_scales{c}", [P, CHUNK], U8)
-            return list(reversed(range(PACK))) if c % 2 else list(range(PACK))
+            return seconds[:, :, (c % 2) * CHUNK : (c % 2 + 1) * CHUNK]
 
         def second_upper(c, t):
             second_input(second_rows(c), 1, t, chunk_gates[c])
+
+        def second_upper_pair(c, t):
+            second_input(seconds, 1, t, slice(chunk_gates[c].start, chunk_gates[c + 1].stop))
+
+        for c in range(last + 1):
+            upper_codes[c] = held(f"upper_codes{c}", [P, CHUNK], U32)
+            upper_scales[c] = held(f"upper_scales{c}", [P, CHUNK], U8)
 
         def join_upper(c):
             z_upper[c] = held(f"z{c}", [P, PACK * CHUNK], BF16)
@@ -285,7 +291,7 @@ def tile_list_fault_tree_risk_kernel(
         def risk_scores(c, lower):
             y_bf[c] = held(f"y_bf{c}", [P, 2, CHUNK, PACK], BF16)
             for n in range(2):
-                banks[c, n] = psum.tile([P, PACK, CHUNK], F32, name=f"bank{PSUM_BANKS - 2 - 2 * (c % 2) + n}")
+                banks[c, n] = psum.tile([P, PACK, CHUNK], F32, name=f"bank{(PSUM_BANKS - 2 - 2 * c) % PSUM_BANKS + n}")
                 y[c, n] = held(f"y{c}{n}", [P, PACK, CHUNK], F32)
                 risk_passes(c, n, 0, lower, lower_scales[:, chunk_gates[c]])
             for n in range(2):
@@ -309,50 +315,72 @@ def tile_list_fault_tree_risk_kernel(
                 in_=y_bf[c][:, n, :, :].rearrange("p m t -> p (m t)"),
             )
 
-        def store_codes(c):
+        def store_codes(gates):
             words = out_1.rearrange("n p m t -> p n (m t)").bitcast(I32)
-            nc.sync.dma_start(words[:, :, chunk_gates[c]], y_codes[:, :, chunk_gates[c]].bitcast(I32))
+            nc.sync.dma_start(words[:, :, gates], y_codes[:, :, gates].bitcast(I32))
 
-        for t in open_chunk(0):
-            second_upper(0, t)
-        for c in range(1, last + 1):
-            order = open_chunk(c)
-            second_upper(c, order[0])
-            join_upper(c - 1)
-            second_upper(c, order[1])
-            quantize_z(upper_codes[c - 1][:], upper_scales[c - 1][:], z_upper[c - 1][:])
-            risk_scores(c - 1, lower_codes[:, chunk_gates[c - 1]])
-            for n in range(2):
-                store_scores(nc.scalar.copy, c - 1, n)
-            for n in range(2):
-                round_scores(nc.scalar.copy, c - 1, n, banks)
-            if c == last:
-                for n in range(2):
-                    quantize_y(0, n)
-                store_codes(0)
-            for t in order[2:]:
-                second_upper(c, t)
+        def finish(c, lower):
+            quantize_z(upper_codes[c][:], upper_scales[c][:], z_upper[c][:])
+            risk_scores(c, lower)
 
-        last_codes = held(f"z{last - 1}", [P, CHUNK], U32)
-        quantize_z(last_codes[:], lower_scales[:, chunk_gates[last]], z_lower[1][:, PACK * CHUNK :])
-        join_upper(last)
-        quantize_y(1, 0)
-        quantize_z(upper_codes[last][:], upper_scales[last][:], z_upper[last][:])
-        quantize_y(1, 1)
-        store_codes(1)
+        def late_lower_codes(c):
+            codes = held(f"z{c - 2}", [P, CHUNK], U32)
+            z = z_lower[1][:, (c - 2) * PACK * CHUNK : (c - 1) * PACK * CHUNK]
+            quantize_z(codes[:], lower_scales[:, chunk_gates[c]], z)
+            return codes[:]
+
+        def store_both(c):
+            for n in range(2):
+                store_scores(nc.scalar.copy, c, n)
+
+        second_upper_pair(0, 0)
+        second_upper_pair(0, 1)
+        second_upper(0, 2)
+        second_upper(0, 3)
+        second_upper(1, 2)
+        join_upper(0)
+        second_upper(1, 3)
+        finish(0, lower_codes[:, chunk_gates[0]])
+        store_both(0)
+        second_upper(2, 2)
+        join_upper(1)
+        second_upper(2, 3)
+        finish(1, lower_codes[:, chunk_gates[1]])
+        store_both(1)
         for n in range(2):
-            quantize_y(last - 1, n)
-        store_codes(last - 1)
+            round_scores(nc.scalar.copy, 0, n, banks)
+        second_upper_pair(2, 0)
+        second_upper_pair(2, 1)
+        lower = late_lower_codes(2)
+        join_upper(2)
+        second_upper(3, 2)
+        finish(2, lower)
+        store_both(2)
+        second_upper(3, 3)
+        lower = late_lower_codes(3)
+        join_upper(last)
+        quantize_y(0, 0)
+        finish(last, lower)
+        quantize_y(0, 1)
+        store_codes(chunk_gates[0])
+        for n in range(2):
+            round_scores(nc.vector.tensor_copy, 1, n, y)
+        for n in range(2):
+            quantize_y(1, n)
+        store_codes(chunk_gates[1])
 
-        risk_scores(last, last_codes[:])
         copies = (nc.scalar.copy, nc.vector.tensor_copy)
         for n in range(2):
             store_scores(copies[n], last, n, (nc.scalar, nc.sync)[n])
+        round_scores(nc.vector.tensor_copy, 2, 0, y)
         for n in range(2):
             round_scores(copies[n], last, n, (banks, y)[n])
-        for n in range(2):
+        round_scores(nc.scalar.copy, 2, 1, banks)
+        quantize_y(2, 0)
+        for n in (1, 0):
             quantize_y(last, n)
-        store_codes(last)
+        quantize_y(2, 1)
+        store_codes(gate_halves[1])
 
         for r in range(ROWS):
             (nc.scalar if r else nc.sync).dma_start(

@@ -204,7 +204,6 @@ def tile_list_fault_tree_risk_kernel(
         first[0] = held("first_lower", [P, PACK, G], F32)
         rest[0] = held("rest", [P, PACK, G], F32)
         second_lower = held("second_lower", [P, PACK, G], F32)
-        lower_codes = held("lower_codes", [P, G // 2], U32)
         lower_scales = held("lower_scales", [P, G], U8)
 
         def round_upper(a, u, name):
@@ -234,17 +233,17 @@ def tile_list_fault_tree_risk_kernel(
                 second_input(second_lower, 0, 2, all_gates)
         for gates in gate_halves:
             second_input(second_lower[:, :, gates], 0, PACK - 1, gates)
-        z_lower = [held(f"z_lower{i}", [P, PACK * G // 2], BF16) for i in range(2)]
+        z_lower = held("z_lower", [P, PACK * G // 2], BF16)
         for a in range(2):
             round_upper(a, 1, f"w1_scales{a}0")
             quantize_upper(a, 1)
-        for i in range(2):
-            join(z_lower[i], 0, gate_halves[i], second_lower[:, :, gate_halves[i]])
+        join(z_lower, 0, gate_halves[0], second_lower[:, :, gate_halves[0]])
         for t in range(PACK):
             failure_probabilities(1, t)
         first[1] = held("w1_raw10", [P, PACK, G], F32)
         rest[1] = held("rest", [P, PACK, G], F32)
-        quantize_z(lower_codes[:, gate_halves[0]], lower_scales[:, gate_halves[0]], z_lower[0][:])
+        lower_codes = held("lower_codes", [P, G // 2], U32)
+        quantize_z(lower_codes[:], lower_scales[:, gate_halves[0]], z_lower[:])
 
         for t in range(PACK):
             first_input(1, t)
@@ -323,10 +322,15 @@ def tile_list_fault_tree_risk_kernel(
             quantize_z(upper_codes[c][:], upper_scales[c][:], z_upper[c][:])
             risk_scores(c, lower)
 
+        z_late = {}
+
+        def late_lower_join(c):
+            z_late[c] = held(f"z{c - 2}", [P, PACK * CHUNK], BF16)
+            join(z_late[c], 0, chunk_gates[c], second_lower[:, :, chunk_gates[c]])
+
         def late_lower_codes(c):
-            codes = held(f"z{c - 2}", [P, CHUNK], U32)
-            z = z_lower[1][:, (c - 2) * PACK * CHUNK : (c - 1) * PACK * CHUNK]
-            quantize_z(codes[:], lower_scales[:, chunk_gates[c]], z)
+            codes = held(f"lower_codes{c}", [P, CHUNK], U32)
+            quantize_z(codes[:], lower_scales[:, chunk_gates[c]], z_late[c][:])
             return codes[:]
 
         def store_both(c):
@@ -344,42 +348,43 @@ def tile_list_fault_tree_risk_kernel(
         store_both(0)
         second_upper(2, 2)
         join_upper(1)
-        second_upper(2, 3)
+        late_lower_join(2)
         finish(1, lower_codes[:, chunk_gates[1]])
         store_both(1)
-        for n in range(2):
-            round_scores(nc.scalar.copy, 0, n, banks)
+        for c in range(2):
+            for n in range(2):
+                round_scores(nc.scalar.copy, c, n, banks)
+        third_lower = late_lower_codes(2)
+        second_upper(2, 3)
         second_upper_pair(2, 0)
         second_upper_pair(2, 1)
-        lower = late_lower_codes(2)
+        late_lower_join(3)
         join_upper(2)
-        second_upper(3, 2)
-        finish(2, lower)
-        store_both(2)
-        second_upper(3, 3)
-        lower = late_lower_codes(3)
-        join_upper(last)
+        last_lower = late_lower_codes(3)
         quantize_y(0, 0)
-        finish(last, lower)
+        finish(2, third_lower)
+        store_both(2)
+        round_scores(nc.scalar.copy, 2, 0, banks)
+        second_upper(3, 2)
+        second_upper(3, 3)
         quantize_y(0, 1)
         store_codes(chunk_gates[0])
-        for n in range(2):
-            round_scores(nc.vector.tensor_copy, 1, n, y)
-        for n in range(2):
-            quantize_y(1, n)
+        join_upper(last)
+        quantize_y(1, 0)
+        finish(last, last_lower)
+        quantize_y(1, 1)
         store_codes(chunk_gates[1])
 
+        round_scores(nc.vector.tensor_copy, 2, 1, y)
         copies = (nc.scalar.copy, nc.vector.tensor_copy)
         for n in range(2):
             store_scores(copies[n], last, n, (nc.scalar, nc.sync)[n])
-        round_scores(nc.vector.tensor_copy, 2, 0, y)
+        quantize_y(2, 0)
         for n in range(2):
             round_scores(copies[n], last, n, (banks, y)[n])
-        round_scores(nc.scalar.copy, 2, 1, banks)
-        quantize_y(2, 0)
-        for n in (1, 0):
-            quantize_y(last, n)
         quantize_y(2, 1)
+        for n in range(2):
+            quantize_y(last, n)
         store_codes(gate_halves[1])
 
         for r in range(ROWS):

@@ -69,11 +69,11 @@ def tile_list_fault_tree_risk_kernel(
         nc.sync.dma_start(idx[:], offs)
         nc.sync.dma_start(table_scales[0:P:ROWS].bitcast(I32), tab_scales.rearrange("a q t -> q a t").bitcast(I32))
         nc.sync.dma_start(w2_scales_raw[0:P:ROWS].bitcast(I32), w2_scales.rearrange("a q c -> q a c").bitcast(I32))
-        nc.sync.dma_start(p1[:], pos1)
-        nc.sync.dma_start(p2[:], pos2)
         for a in range(2):
             nc.sync.dma_start(table[a][:].bitcast(I32), tab_words[a].rearrange("p n i -> p (n i)").bitcast(I32))
         load_w1(1, 0)
+        nc.sync.dma_start(p1[:], pos1)
+        nc.sync.dma_start(p2[:], pos2)
 
         picked_scales = held("picked_scales", [P, S], U8)
         table_planes = held("table_planes", [P, S], U8)
@@ -122,7 +122,7 @@ def tile_list_fault_tree_risk_kernel(
         round_block(w1_first, 0, 0)
         quantize_w1(w1_first, 0, 0, slice(0, PASS))
 
-        w2_raw = held("w1_raw00", [P, 2, 2 * N], U8)
+        w2_raw = held("picked_scales", [P, 2, 2 * N], U8)
         nc.sync.dma_start(w2_raw[:].bitcast(I32), w2_words.rearrange("a p c -> p a c").bitcast(I32))
 
         severity_rows = held("severity_rows", [P, 2, PACK, G], F32)
@@ -138,8 +138,9 @@ def tile_list_fault_tree_risk_kernel(
         round_pair(nc.scalar.copy, w1_pairs[0][:], 1, 0, 0, slice(P - P // 4, P))
         round_pair(nc.vector.tensor_copy, w1_pairs[0][:], 1, 0, 0, slice(0, P - P // 4))
         round_pair(nc.scalar.copy, w1_pairs[1][:], 1, 0, 1)
-        for u in range(2):
-            quantize_w1(w1_pairs[u], 1, 0, slice(2 * u * P, 2 * (u + 1) * P))
+        for t in range(2):
+            quantize_w1(w1_pairs[0][:, t * PASS : (t + 1) * PASS], 1, 0, slice(t * P, (t + 1) * P))
+        quantize_w1(w1_pairs[1], 1, 0, slice(2 * P, PASS))
 
         w2_dealt = held("w2_dealt", [P, 4, PACK, 2 * P], U8)
         nc.vector.tensor_copy(
@@ -247,8 +248,11 @@ def tile_list_fault_tree_risk_kernel(
 
         for t in range(PACK):
             first_input(1, t)
-        for t in range(PACK):
+        for t in range(2):
             remainder(1, t)
+        for gates in (slice(0, CHUNK), slice(CHUNK, G)):
+            for t in range(2, PACK):
+                remainder(1, t, gates)
 
         chunk_gates = [slice(m0, m0 + CHUNK) for m0 in range(0, G, CHUNK)]
         last = len(chunk_gates) - 1
@@ -291,12 +295,12 @@ def tile_list_fault_tree_risk_kernel(
             y_bf[c] = held(f"y_bf{c}", [P, 2, CHUNK, PACK], BF16)
             for n in range(2):
                 banks[c, n] = psum.tile([P, PACK, CHUNK], F32, name=f"bank{(PSUM_BANKS - 2 - 2 * c) % PSUM_BANKS + n}")
-                y[c, n] = held(f"y{c}{n}", [P, PACK, CHUNK], F32)
                 risk_passes(c, n, 0, lower, lower_scales[:, chunk_gates[c]])
             for n in range(2):
                 risk_passes(c, n, 1, upper_codes[c][:], upper_scales[c][:])
 
         def store_scores(copy, c, n, queue=nc.sync):
+            y[c, n] = held(f"y_bf{c - 1}" if (c, n) == (last, 1) else f"y{c}{n}", [P, PACK, CHUNK], F32)
             copy(y[c, n][:], banks[c, n][:])
             rows = out_0[n * PASS : (n + 1) * PASS, chunk_gates[c]]
             queue.dma_start(rows.rearrange("(p t) m -> p t m", t=PACK), y[c, n][:])
@@ -364,7 +368,7 @@ def tile_list_fault_tree_risk_kernel(
         quantize_y(0, 0)
         finish(2, third_lower)
         store_both(2)
-        round_scores(nc.scalar.copy, 2, 0, banks)
+        round_scores(nc.scalar.copy, 2, 1, banks)
         second_upper(3, 2)
         second_upper(3, 3)
         quantize_y(0, 1)
@@ -373,19 +377,19 @@ def tile_list_fault_tree_risk_kernel(
         quantize_y(1, 0)
         finish(last, last_lower)
         quantize_y(1, 1)
-        store_codes(chunk_gates[1])
 
-        round_scores(nc.vector.tensor_copy, 2, 1, y)
+        round_scores(nc.vector.tensor_copy, 2, 0, y)
+        for n in range(2):
+            quantize_y(2, n)
+        store_codes(slice(CHUNK, G - CHUNK))
         copies = (nc.scalar.copy, nc.vector.tensor_copy)
         for n in range(2):
             store_scores(copies[n], last, n, (nc.scalar, nc.sync)[n])
-        quantize_y(2, 0)
         for n in range(2):
             round_scores(copies[n], last, n, (banks, y)[n])
-        quantize_y(2, 1)
         for n in range(2):
             quantize_y(last, n)
-        store_codes(gate_halves[1])
+        store_codes(chunk_gates[last])
 
         for r in range(ROWS):
             (nc.scalar if r else nc.sync).dma_start(

@@ -1,6 +1,7 @@
 from contextlib import ExitStack
 
 import concourse.mybir as mybir
+from concourse.masks import make_identity
 
 K, T, S, G, H, N = 1024, 4096, 1024, 512, 1024, 1024
 FLOPS = 2 * K * H * S + 2 * H * N * G
@@ -63,10 +64,14 @@ def tile_list_fault_tree_risk_kernel(
         w2_scales_raw = held("w2_scales_raw", [P, N], U8)
         nc.vector.memset(table_scales[:].bitcast(I32), 0)
         nc.gpsimd.memset(w2_scales_raw[:].bitcast(I32), 0)
+        severity_flat = held("severity_flat", [P, PASS], F32)
+        nc.gpsimd.memset(severity_flat[:], 0.0)
+        identity = held("identity", [P, P], F32)
+        make_identity(nc, identity[:])
 
         load_w1(0, 0)
-        nc.sync.dma_start(severity[:], g.rearrange("(b p t) -> p b t", b=2, t=PACK))
         nc.sync.dma_start(idx[:], offs)
+        nc.sync.dma_start(severity_flat[0:2], g.rearrange("(b c) -> b c", b=2))
         nc.sync.dma_start(table_scales[0:P:ROWS].bitcast(I32), tab_scales.rearrange("a q t -> q a t").bitcast(I32))
         nc.sync.dma_start(w2_scales_raw[0:P:ROWS].bitcast(I32), w2_scales.rearrange("a q c -> q a c").bitcast(I32))
         for a in range(2):
@@ -125,6 +130,10 @@ def tile_list_fault_tree_risk_kernel(
         w2_raw = held("picked_scales", [P, 2, 2 * N], U8)
         nc.sync.dma_start(w2_raw[:].bitcast(I32), w2_words.rearrange("a p c -> p a c").bitcast(I32))
 
+        turned = psum.tile([P, PACK, P], F32, name=f"bank{PSUM_BANKS - 1}")
+        for t in range(PACK):
+            nc.tensor.transpose(turned[:, t, :], severity_flat[:, t:PASS:PACK], identity[:])
+        nc.scalar.copy(severity[:], turned[:, :, 0:2].rearrange("p t b -> p b t"))
         severity_rows = held("severity_rows", [P, 2, PACK, G], F32)
         nc.scalar.copy(severity_rows[:], severity[:].unsqueeze(3).to_broadcast([P, 2, PACK, G]))
 
@@ -232,13 +241,13 @@ def tile_list_fault_tree_risk_kernel(
             remainder(0, 2 + a)
             if a == 0:
                 second_input(second_lower, 0, 2, all_gates)
-        for gates in gate_halves:
-            second_input(second_lower[:, :, gates], 0, PACK - 1, gates)
-        z_lower = held("z_lower", [P, PACK * G // 2], BF16)
-        for a in range(2):
-            round_upper(a, 1, f"w1_scales{a}0")
-            quantize_upper(a, 1)
+        second_input(second_lower, 0, PACK - 1, all_gates)
+        round_upper(0, 1, "w1_scales00")
+        quantize_upper(0, 1)
+        z_lower = held("table0", [P, PACK * G // 2], BF16)
         join(z_lower, 0, gate_halves[0], second_lower[:, :, gate_halves[0]])
+        round_upper(1, 1, "w1_scales10")
+        quantize_upper(1, 1)
         for t in range(PACK):
             failure_probabilities(1, t)
         first[1] = held("w1_raw10", [P, PACK, G], F32)

@@ -28,6 +28,8 @@ LINE = 16
 CHUNK = 128
 H_BANKS = (6, 8)
 PSUM_BANKS = 8
+CODES_AT = 4 * PACK * PASS
+PLANE_AT = CODES_AT + 4 * PASS
 
 
 def tile_list_fault_tree_risk_kernel(
@@ -48,8 +50,8 @@ def tile_list_fault_tree_risk_kernel(
         idx = keep.tile([P, S // LANES], U16, name="idx")
         p1 = keep.tile([P, G // LANES], U16, name="p1")
         p2 = keep.tile([P, G // LANES], U16, name="p2")
-        table = [held(f"table{a}", [P, T], U32) for a in range(2)]
-        table_scales = tenant("table_scales", [P, T], U8, 0)
+        table = [tenant("table0", [P, T], U32, 0), held("table1", [P, T], U32)]
+        table_scales = held("table_scales", [P, T], U8)
         w1_raw = {(a, 0): held(f"w1_raw{a}0", [P, PACK, PASS], F32) for a in range(2)}
         severity = held("severity", [P, 2, PACK], F32)
 
@@ -91,12 +93,6 @@ def tile_list_fault_tree_risk_kernel(
                     picked_scales[ROWS * a + 2 * ROWS * r : P : QUAD, :].bitcast(I32),
                 )
 
-        w2_planes = [held("w2_plane0", [P, N], U8)]
-        nc.vector.tensor_copy(
-            w2_planes[0][:].rearrange("p (n t c i) -> p n c t i", n=2, t=PACK, i=LINE),
-            w2_scales_raw[:].rearrange("p (n c i t) -> p n c t i", n=2, t=PACK, i=LINE),
-        )
-
         picked = {}
 
         def pick_words(a, name):
@@ -122,10 +118,8 @@ def tile_list_fault_tree_risk_kernel(
                 out=w1_codes[a, b][:, cols].bitcast(FP8X4), scales=w1_scales[a, b][:, cols], in_=rounded[:]
             )
 
-        w1_codes[0, 0] = tenant("w1_codes00", [P, PASS], U32, 0)
         w1_first = held("w1_first", [P, PACK * PASS], BF16)
         round_block(w1_first, 0, 0)
-        quantize_w1(w1_first, 0, 0, slice(0, PASS))
 
         w2_raw = held("picked_scales", [P, 2, 2 * N], U8)
         nc.sync.dma_start(w2_raw[:].bitcast(I32), w2_words.rearrange("a p c -> p a c").bitcast(I32))
@@ -138,9 +132,18 @@ def tile_list_fault_tree_risk_kernel(
         nc.scalar.copy(severity_rows[:], severity[:].unsqueeze(3).to_broadcast([P, 2, PACK, G]))
 
         pick_words(0, "picked0")
+
+        w2_planes = [tenant("w2_plane0", [P, N], U8, PLANE_AT)]
+        nc.vector.tensor_copy(
+            w2_planes[0][:].rearrange("p (n t c i) -> p n c t i", n=2, t=PACK, i=LINE),
+            w2_scales_raw[:].rearrange("p (n c i t) -> p n c t i", n=2, t=PACK, i=LINE),
+        )
+        w1_codes[0, 0] = tenant("w1_codes00", [P, PASS], U32, CODES_AT)
+        quantize_w1(w1_first, 0, 0, slice(0, PASS))
         pick_words(1, "w1_first")
+        w1_raw[0, 1] = tenant("w1_raw01", [P, PACK, PASS], F32, 0)
+        w1_raw[1, 1] = held("table1", [P, PACK, PASS], F32)
         for a in range(2):
-            w1_raw[a, 1] = held(f"table{a}", [P, PACK, PASS], F32)
             load_w1(a, 1)
 
         w1_pairs = [held(f"w1_pair{u}", [P, 2 * PASS], BF16) for u in range(2)]
@@ -151,11 +154,16 @@ def tile_list_fault_tree_risk_kernel(
             quantize_w1(w1_pairs[0][:, t * PASS : (t + 1) * PASS], 1, 0, slice(t * P, (t + 1) * P))
         quantize_w1(w1_pairs[1], 1, 0, slice(2 * P, PASS))
 
-        w2_dealt = held("w2_dealt", [P, 4, PACK, 2 * P], U8)
-        nc.vector.tensor_copy(
-            w2_dealt[:].bitcast(U16).rearrange("p s t (c i) -> p s c t i", i=LINE // 2),
-            w2_raw[:].bitcast(U16).rearrange("p a (n c i t) -> p (a n) c t i", n=2, i=LINE // 2, t=PACK),
-        )
+        w2_dealt = {}
+
+        def deal_w2(copy, a, name):
+            w2_dealt[a] = held(name, [P, 2, PACK, 2 * P], U8)
+            copy(
+                w2_dealt[a][:].bitcast(U16).rearrange("p n t (c i) -> p n c t i", i=LINE // 2),
+                w2_raw[:, a].bitcast(U16).rearrange("p (n c i t) -> p n c t i", n=2, i=LINE // 2, t=PACK),
+            )
+
+        deal_w2(nc.vector.tensor_copy, 0, "w2_dealt0")
 
         w2_planes.append(held("w1_pair0", [P, N], U8))
         nc.sync.dma_start(w2_planes[1][:].bitcast(I32), w2_planes[0][:].bitcast(I32))
@@ -218,7 +226,7 @@ def tile_list_fault_tree_risk_kernel(
 
         def round_upper(a, u, name):
             shape = [P, 2 * PASS]
-            upper_pairs[a, u] = tenant("w1_upper", shape, BF16, 0) if (a, u) == (0, 0) else held(name, shape, BF16)
+            upper_pairs[a, u] = tenant("w1_upper", shape, BF16, CODES_AT) if (a, u) == (0, 0) else held(name, shape, BF16)
             round_pair(nc.scalar.copy, upper_pairs[a, u][:], a, 1, u)
 
         def quantize_upper(a, u):
@@ -244,7 +252,7 @@ def tile_list_fault_tree_risk_kernel(
         second_input(second_lower, 0, PACK - 1, all_gates)
         round_upper(0, 1, "w1_scales00")
         quantize_upper(0, 1)
-        z_lower = held("table0", [P, PACK * G // 2], BF16)
+        z_lower = tenant("z_lower", [P, PACK * G // 2], BF16, 0)
         join(z_lower, 0, gate_halves[0], second_lower[:, :, gate_halves[0]])
         round_upper(1, 1, "w1_scales10")
         quantize_upper(1, 1)
@@ -262,6 +270,8 @@ def tile_list_fault_tree_risk_kernel(
         for gates in (slice(0, CHUNK), slice(CHUNK, G)):
             for t in range(2, PACK):
                 remainder(1, t, gates)
+
+        deal_w2(nc.scalar.copy, 1, "severity_rows")
 
         chunk_gates = [slice(m0, m0 + CHUNK) for m0 in range(0, G, CHUNK)]
         last = len(chunk_gates) - 1
@@ -292,7 +302,7 @@ def tile_list_fault_tree_risk_kernel(
             for t in range(PACK):
                 nc.tensor.matmul_mx(
                     out=banks[c, n][:, t, :],
-                    lhsT=w2_dealt[:, 2 * a + n, t, :].bitcast(FP4X4),
+                    lhsT=w2_dealt[a][:, n, t, :].bitcast(FP4X4),
                     lhsT_scale=w2_planes[a][:, (PACK * n + t) * P : (PACK * n + t + 1) * P],
                     rhs=codes.bitcast(FP8X4),
                     rhs_scale=scales,

@@ -96,10 +96,8 @@ def tile_list_fault_tree_risk_kernel(
         picked = {}
 
         def pick_words(a, name):
-            both = held(name, [P, S], U32)
-            nc.vector.tensor_copy(both[:], table[a][:].indirect(idx[:]))
-            for half in range(2):
-                picked[a, half] = both[:, half * BANK : (half + 1) * BANK]
+            picked[a] = held(name, [P, S], U32)
+            nc.vector.tensor_copy(picked[a][:], table[a][:].indirect(idx[:]))
 
         blocks = [(a, b) for a in range(2) for b in range(2)]
         w1_codes = {key: held(f"w1_codes{key[0]}{key[1]}", [P, PASS], U32) for key in blocks[1:]}
@@ -176,19 +174,24 @@ def tile_list_fault_tree_risk_kernel(
 
         def failure_probabilities(b, t):
             cols = slice(t * P, (t + 1) * P)
-            for half in range(2):
-                bank = psum.tile([P, BANK], F32, name=f"bank{(2 * (PACK * b + t) + half) % H_BANKS[b]}")
+            if (b, t) == (0, 0):
+                width, numbers = BANK // 2, (0, 1, PSUM_BANKS - 2, PSUM_BANKS - 1)
+            else:
+                width, numbers = BANK, [(2 * (PACK * b + t) + half) % H_BANKS[b] for half in range(2)]
+            for part, number in enumerate(numbers):
+                entries = slice(part * width, (part + 1) * width)
+                bank = psum.tile([P, width], F32, name=f"bank{number}")
                 for a in range(2):
                     nc.tensor.matmul_mx(
                         out=bank[:],
                         lhsT=w1_codes[a, b][:, cols].bitcast(FP8X4),
                         lhsT_scale=w1_scales[a, b][:, cols],
-                        rhs=picked[a, half].bitcast(FP8X4),
-                        rhs_scale=table_planes[ROWS * a : P, half * BANK : (half + 1) * BANK],
+                        rhs=picked[a][:, entries].bitcast(FP8X4),
+                        rhs_scale=table_planes[ROWS * a : P, entries],
                         start=(a == 0),
                         stop=(a == 1),
                     )
-                nc.scalar.activation(h[b, t][:, half * BANK : (half + 1) * BANK], bank[:], ACT.Sigmoid)
+                nc.scalar.activation(h[b, t][:, entries], bank[:], ACT.Sigmoid)
 
         def fetch_times(dst, factor, b, t, places, gates):
             entries = places[:, gates.start // LANES : gates.stop // LANES]

@@ -175,9 +175,11 @@ def tile_list_fault_tree_risk_kernel(
         def failure_probabilities(b, t):
             cols = slice(t * P, (t + 1) * P)
             if (b, t) == (0, 0):
-                width, numbers = BANK // 2, (0, 1, PSUM_BANKS - 2, PSUM_BANKS - 1)
+                width, numbers = BANK // 2, range(4)
+            elif b == 0:
+                width, numbers = BANK, [(2 * (t + 1) + half) % H_BANKS[b] for half in range(2)]
             else:
-                width, numbers = BANK, [(2 * (PACK * b + t) + half) % H_BANKS[b] for half in range(2)]
+                width, numbers = BANK, [2 * t + half for half in range(2)]
             for part, number in enumerate(numbers):
                 entries = slice(part * width, (part + 1) * width)
                 bank = psum.tile([P, width], F32, name=f"bank{number}")

from contextlib import ExitStack

import concourse.mybir as mybir
from concourse.masks import make_identity

K, T, S, G, H, N = 1024, 4096, 1024, 512, 1024, 1024
FLOPS = 2 * K * H * S + 2 * H * N * G

F32 = mybir.dt.float32
BF16 = mybir.dt.bfloat16
I32 = mybir.dt.int32
U32 = mybir.dt.uint32
U16 = mybir.dt.uint16
U8 = mybir.dt.uint8
FP8X4 = mybir.dt.float8_e4m3fn_x4
FP4X4 = mybir.dt.float4_e2m1fn_x4
ALU = mybir.AluOpType
ACT = mybir.ActivationFunctionType

P = 128
PACK = 4
PASS = P * PACK
QUAD = 32
ROWS = 4
BANK = 512
LANES = 16
LINE = 16
CHUNK = 128
H_BANKS = (6, 8)
PSUM_BANKS = 8
CODES_AT = 4 * PACK * PASS
PLANE_AT = CODES_AT + 4 * PASS


def tile_list_fault_tree_risk_kernel(
    tc, tab_words, tab_scales, offs, w1, pos1, pos2, g, w2_words, w2_scales, out_0, out_1, out_2
):
    nc = tc.nc
    with ExitStack() as ctx:
        keep = ctx.enter_context(tc.tile_pool(name="keep", bufs=1))
        shared = ctx.enter_context(tc.tile_pool(name="shared", bufs=1))
        psum = ctx.enter_context(tc.psum_pool(name="psum", bufs=1))

        def held(name, shape, dtype):
            return keep.tile(shape, dtype, name=name, align_bytes=64)

        def tenant(name, shape, dtype, offset):
            return shared.tile(shape, dtype, name=name, align_bytes=64, offset=offset)

        idx = keep.tile([P, S // LANES], U16, name="idx")
        p1 = keep.tile([P, G // LANES], U16, name="p1")
        p2 = keep.tile([P, G // LANES], U16, name="p2")
        table = [tenant("table0", [P, T], U32, 0), held("table1", [P, T], U32)]
        table_scales = held("table_scales", [P, T], U8)
        w1_raw = {(a, 0): held(f"w1_raw{a}0", [P, PACK, PASS], F32) for a in range(2)}
        severity = held("severity", [P, 2, PACK], F32)

        def load_w1(a, b):
            rows = w1[a * PASS : (a + 1) * PASS, b * PASS : (b + 1) * PASS]
            nc.sync.dma_start(w1_raw[a, b][:], rows.rearrange("(p j) c -> p j c", j=PACK))

        warm = held("warm", [P, 2], F32)
        nc.gpsimd.memset(warm[:, 0:1], 0.0)
        nc.scalar.activation(warm[:, 1:2], warm[:, 0:1], ACT.Sigmoid)

        w2_scales_raw = held("w2_scales_raw", [P, N], U8)
        nc.vector.memset(table_scales[:].bitcast(I32), 0)
        nc.gpsimd.memset(w2_scales_raw[:].bitcast(I32), 0)
        severity_flat = held("severity_flat", [P, PASS], F32)
        nc.gpsimd.memset(severity_flat[:], 0.0)
        identity = held("identity", [P, P], F32)
        make_identity(nc, identity[:])

        load_w1(0, 0)
        nc.sync.dma_start(idx[:], offs)
        nc.sync.dma_start(severity_flat[0:2], g.rearrange("(b c) -> b c", b=2))
        nc.sync.dma_start(table_scales[0:P:ROWS].bitcast(I32), tab_scales.rearrange("a q t -> q a t").bitcast(I32))
        nc.sync.dma_start(w2_scales_raw[0:P:ROWS].bitcast(I32), w2_scales.rearrange("a q c -> q a c").bitcast(I32))
        for a in range(2):
            nc.sync.dma_start(table[a][:].bitcast(I32), tab_words[a].rearrange("p n i -> p (n i)").bitcast(I32))
        load_w1(1, 0)
        nc.sync.dma_start(p1[:], pos1)
        nc.sync.dma_start(p2[:], pos2)

        picked_scales = held("picked_scales", [P, S], U8)
        table_planes = held("table_planes", [P, S], U8)
        nc.vector.tensor_copy(picked_scales[:], table_scales[:].indirect(idx[:]))
        nc.vector.tensor_copy(table_planes[:].bitcast(I32), picked_scales[:].bitcast(I32))
        for a in range(2):
            for r in range(1, ROWS):
                nc.scalar.dma_start(
                    table_planes[ROWS * a + r : P : QUAD, :].bitcast(I32),
                    picked_scales[ROWS * a + 2 * ROWS * r : P : QUAD, :].bitcast(I32),
                )

        picked = {}

        def pick_words(a, name):
            picked[a] = held(name, [P, S], U32)
            nc.vector.tensor_copy(picked[a][:], table[a][:].indirect(idx[:]))

        blocks = [(a, b) for a in range(2) for b in range(2)]
        w1_codes = {key: held(f"w1_codes{key[0]}{key[1]}", [P, PASS], U32) for key in blocks[1:]}
        w1_scales = {key: held(f"w1_scales{key[0]}{key[1]}", [P, PASS], U8) for key in blocks}

        def round_pair(copy, rounded, a, b, u, words=slice(0, P)):
            raw = w1_raw[a, b][:].rearrange("p j (m u e) -> p u m j e", u=2, e=2)
            copy(rounded.rearrange("p (e m j) -> p m j e", e=2, j=PACK)[:, words], raw[:, u, words])

        def round_block(rounded, a, b):
            for u in range(2):
                round_pair(nc.scalar.copy, rounded[:, 2 * u * PASS : 2 * (u + 1) * PASS], a, b, u)

        def quantize_w1(rounded, a, b, cols):
            nc.vector.quantize_mx(
                out=w1_codes[a, b][:, cols].bitcast(FP8X4), scales=w1_scales[a, b][:, cols], in_=rounded[:]
            )

        w1_first = held("w1_first", [P, PACK * PASS], BF16)
        round_block(w1_first, 0, 0)

        w2_raw = held("picked_scales", [P, 2, 2 * N], U8)
        nc.sync.dma_start(w2_raw[:].bitcast(I32), w2_words.rearrange("a p c -> p a c").bitcast(I32))

        turned = psum.tile([P, PACK, P], F32, name=f"bank{PSUM_BANKS - 1}")
        for t in range(PACK):
            nc.tensor.transpose(turned[:, t, :], severity_flat[:, t:PASS:PACK], identity[:])
        nc.scalar.copy(severity[:], turned[:, :, 0:2].rearrange("p t b -> p b t"))
        severity_rows = held("severity_rows", [P, 2, PACK, G], F32)
        nc.scalar.copy(severity_rows[:], severity[:].unsqueeze(3).to_broadcast([P, 2, PACK, G]))

        pick_words(0, "picked0")

        w2_planes = [tenant("w2_plane0", [P, N], U8, PLANE_AT)]
        nc.vector.tensor_copy(
            w2_planes[0][:].rearrange("p (n t c i) -> p n c t i", n=2, t=PACK, i=LINE),
            w2_scales_raw[:].rearrange("p (n c i t) -> p n c t i", n=2, t=PACK, i=LINE),
        )
        w1_codes[0, 0] = tenant("w1_codes00", [P, PASS], U32, CODES_AT)
        quantize_w1(w1_first, 0, 0, slice(0, PASS))
        pick_words(1, "w1_first")
        w1_raw[0, 1] = tenant("w1_raw01", [P, PACK, PASS], F32, 0)
        w1_raw[1, 1] = held("table1", [P, PACK, PASS], F32)
        for a in range(2):
            load_w1(a, 1)

        w1_pairs = [held(f"w1_pair{u}", [P, 2 * PASS], BF16) for u in range(2)]
        round_pair(nc.scalar.copy, w1_pairs[0][:], 1, 0, 0, slice(P - P // 4, P))
        round_pair(nc.vector.tensor_copy, w1_pairs[0][:], 1, 0, 0, slice(0, P - P // 4))
        round_pair(nc.scalar.copy, w1_pairs[1][:], 1, 0, 1)
        for t in range(2):
            quantize_w1(w1_pairs[0][:, t * PASS : (t + 1) * PASS], 1, 0, slice(t * P, (t + 1) * P))
        quantize_w1(w1_pairs[1], 1, 0, slice(2 * P, PASS))

        w2_dealt = {}

        def deal_w2(copy, a, name):
            w2_dealt[a] = held(name, [P, 2, PACK, 2 * P], U8)
            copy(
                w2_dealt[a][:].bitcast(U16).rearrange("p n t (c i) -> p n c t i", i=LINE // 2),
                w2_raw[:, a].bitcast(U16).rearrange("p (n c i t) -> p n c t i", n=2, i=LINE // 2, t=PACK),
            )

        deal_w2(nc.vector.tensor_copy, 0, "w2_dealt0")

        w2_planes.append(held("w1_pair0", [P, N], U8))
        nc.sync.dma_start(w2_planes[1][:].bitcast(I32), w2_planes[0][:].bitcast(I32))
        for a in (1, 0):
            for r in range(1 - a, ROWS):
                rows = w2_planes[1 - a][2 * ROWS * r + ROWS * a : P : QUAD]
                nc.sync.dma_start(w2_planes[a][r:P:QUAD].bitcast(I32), rows.bitcast(I32))

        h = {(b, t): held(f"h{b}{t}", [P, S], F32) for b in range(2) for t in range(PACK)}

        def failure_probabilities(b, t):
            cols = slice(t * P, (t + 1) * P)
            if (b, t) == (0, 0):
                width, numbers = BANK // 2, range(4)
            elif b == 0:
                width, numbers = BANK, [(2 * (t + 1) + half) % H_BANKS[b] for half in range(2)]
            else:
                width, numbers = BANK, [2 * t + half for half in range(2)]
            for part, number in enumerate(numbers):
                entries = slice(part * width, (part + 1) * width)
                bank = psum.tile([P, width], F32, name=f"bank{number}")
                for a in range(2):
                    nc.tensor.matmul_mx(
                        out=bank[:],
                        lhsT=w1_codes[a, b][:, cols].bitcast(FP8X4),
                        lhsT_scale=w1_scales[a, b][:, cols],
                        rhs=picked[a][:, entries].bitcast(FP8X4),
                        rhs_scale=table_planes[ROWS * a : P, entries],
                        start=(a == 0),
                        stop=(a == 1),
                    )
                nc.scalar.activation(h[b, t][:, entries], bank[:], ACT.Sigmoid)

        def fetch_times(dst, factor, b, t, places, gates):
            entries = places[:, gates.start // LANES : gates.stop // LANES]
            nc.vector.tensor_tensor(out=dst, in0=h[b, t][:].indirect(entries), in1=factor, op=ALU.mult)

        all_gates = slice(0, G)
        first = {}
        rest = {}

        def first_input(b, t):
            fetch_times(first[b][:, t, :], severity_rows[:, b, t, :], b, t, p1, all_gates)

        def remainder(b, t, gates=all_gates):
            weight = severity[:, b, t : t + 1]
            nc.scalar.activation(rest[b][:, t, gates], first[b][:, t, gates], ACT.Identity, bias=weight, scale=-1.0)

        def second_input(second, b, t, gates):
            fetch_times(second[:, t, :], rest[b][:, t, gates], b, t, p2, gates)

        def join(z, b, gates, second):
            nc.vector.tensor_tensor(
                out=z[:].rearrange("p (c i t) -> p c t i", i=PACK, t=PACK),
                in0=first[b][:, :, gates].rearrange("p t (c i) -> p c t i", i=PACK),
                in1=second.rearrange("p t (c i) -> p c t i", i=PACK),
                op=ALU.add,
            )

        def quantize_z(codes, scales, z):
            nc.vector.quantize_mx(out=codes.bitcast(FP8X4), scales=scales, in_=z)

        first[0] = held("first_lower", [P, PACK, G], F32)
        rest[0] = held("rest", [P, PACK, G], F32)
        second_lower = held("second_lower", [P, PACK, G], F32)
        lower_scales = held("lower_scales", [P, G], U8)

        def round_upper(a, u, name):
            shape = [P, 2 * PASS]
            upper_pairs[a, u] = tenant("w1_upper", shape, BF16, CODES_AT) if (a, u) == (0, 0) else held(name, shape, BF16)
            round_pair(nc.scalar.copy, upper_pairs[a, u][:], a, 1, u)

        def quantize_upper(a, u):
            quantize_w1(upper_pairs[a, u], a, 1, slice(2 * u * P, 2 * (u + 1) * P))

        upper_pairs = {}
        gate_halves = (slice(0, G // 2), slice(G // 2, G))
        for t in range(PACK - 1):
            failure_probabilities(0, t)
            first_input(0, t)
        remainder(0, 0)
        second_input(second_lower, 0, 0, all_gates)
        failure_probabilities(0, PACK - 1)
        first_input(0, PACK - 1)
        remainder(0, 1)
        second_input(second_lower, 0, 1, all_gates)
        for a in range(2):
            round_upper(a, 0, f"w1_codes{a}0")
            quantize_upper(a, 0)
            remainder(0, 2 + a)
            if a == 0:
                second_input(second_lower, 0, 2, all_gates)
        second_input(second_lower, 0, PACK - 1, all_gates)
        round_upper(0, 1, "w1_scales00")
        quantize_upper(0, 1)
        z_lower = tenant("z_lower", [P, PACK * G // 2], BF16, 0)
        join(z_lower, 0, gate_halves[0], second_lower[:, :, gate_halves[0]])
        round_upper(1, 1, "w1_scales10")
        quantize_upper(1, 1)
        for t in range(PACK):
            failure_probabilities(1, t)
        first[1] = held("w1_raw10", [P, PACK, G], F32)
        rest[1] = held("rest", [P, PACK, G], F32)
        lower_codes = held("lower_codes", [P, G // 2], U32)
        quantize_z(lower_codes[:], lower_scales[:, gate_halves[0]], z_lower[:])

        for t in range(PACK):
            first_input(1, t)
        for t in range(2):
            remainder(1, t)
        for gates in (slice(0, CHUNK), slice(CHUNK, G)):
            for t in range(2, PACK):
                remainder(1, t, gates)

        deal_w2(nc.scalar.copy, 1, "severity_rows")

        chunk_gates = [slice(m0, m0 + CHUNK) for m0 in range(0, G, CHUNK)]
        last = len(chunk_gates) - 1
        y_codes = held("y_codes", [P, 2, G], U32)
        y_scales = held("y_scales", [P, 2, G], U8)
        upper_codes, upper_scales, z_upper, banks, y, y_bf = {}, {}, {}, {}, {}, {}

        seconds = held("second_upper", [P, PACK, 2 * CHUNK], F32)

        def second_rows(c):
            return seconds[:, :, (c % 2) * CHUNK : (c % 2 + 1) * CHUNK]

        def second_upper(c, t):
            second_input(second_rows(c), 1, t, chunk_gates[c])

        def second_upper_pair(c, t):
            second_input(seconds, 1, t, slice(chunk_gates[c].start, chunk_gates[c + 1].stop))

        for c in range(last + 1):
            upper_codes[c] = held(f"upper_codes{c}", [P, CHUNK], U32)
            upper_scales[c] = held(f"upper_scales{c}", [P, CHUNK], U8)

        def join_upper(c):
            z_upper[c] = held(f"z{c}", [P, PACK * CHUNK], BF16)
            join(z_upper[c], 1, chunk_gates[c], second_rows(c))

        def risk_passes(c, n, a, codes, scales):
            for t in range(PACK):
                nc.tensor.matmul_mx(
                    out=banks[c, n][:, t, :],
                    lhsT=w2_dealt[a][:, n, t, :].bitcast(FP4X4),
                    lhsT_scale=w2_planes[a][:, (PACK * n + t) * P : (PACK * n + t + 1) * P],
                    rhs=codes.bitcast(FP8X4),
                    rhs_scale=scales,
                    start=(a == 0 and t == 0),
                    stop=(a == 1 and t == PACK - 1),
                )

        def risk_scores(c, lower):
            y_bf[c] = held(f"y_bf{c}", [P, 2, CHUNK, PACK], BF16)
            for n in range(2):
                banks[c, n] = psum.tile([P, PACK, CHUNK], F32, name=f"bank{(PSUM_BANKS - 2 - 2 * c) % PSUM_BANKS + n}")
                risk_passes(c, n, 0, lower, lower_scales[:, chunk_gates[c]])
            for n in range(2):
                risk_passes(c, n, 1, upper_codes[c][:], upper_scales[c][:])

        def store_scores(copy, c, n, queue=nc.sync):
            y[c, n] = held(f"y_bf{c - 1}" if (c, n) == (last, 1) else f"y{c}{n}", [P, PACK, CHUNK], F32)
            copy(y[c, n][:], banks[c, n][:])
            rows = out_0[n * PASS : (n + 1) * PASS, chunk_gates[c]]
            queue.dma_start(rows.rearrange("(p t) m -> p t m", t=PACK), y[c, n][:])

        def round_scores(copy, c, n, source):
            copy(
                y_bf[c][:, n, :, :].rearrange("p (c i) t -> p c t i", i=PACK),
                source[c, n][:].rearrange("p t (c i) -> p c t i", i=PACK),
            )

        def quantize_y(c, n):
            nc.vector.quantize_mx(
                out=y_codes[:, n, chunk_gates[c]].bitcast(FP8X4),
                scales=y_scales[:, n, chunk_gates[c]],
                in_=y_bf[c][:, n, :, :].rearrange("p m t -> p (m t)"),
            )

        def store_codes(gates):
            words = out_1.rearrange("n p m t -> p n (m t)").bitcast(I32)
            nc.sync.dma_start(words[:, :, gates], y_codes[:, :, gates].bitcast(I32))

        def finish(c, lower):
            quantize_z(upper_codes[c][:], upper_scales[c][:], z_upper[c][:])
            risk_scores(c, lower)

        z_late = {}

        def late_lower_join(c):
            z_late[c] = held(f"z{c - 2}", [P, PACK * CHUNK], BF16)
            join(z_late[c], 0, chunk_gates[c], second_lower[:, :, chunk_gates[c]])

        def late_lower_codes(c):
            codes = held(f"lower_codes{c}", [P, CHUNK], U32)
            quantize_z(codes[:], lower_scales[:, chunk_gates[c]], z_late[c][:])
            return codes[:]

        def store_both(c):
            for n in range(2):
                store_scores(nc.scalar.copy, c, n)

        second_upper_pair(0, 0)
        second_upper_pair(0, 1)
        second_upper(0, 2)
        second_upper(0, 3)
        second_upper(1, 2)
        join_upper(0)
        second_upper(1, 3)
        finish(0, lower_codes[:, chunk_gates[0]])
        store_both(0)
        second_upper(2, 2)
        join_upper(1)
        late_lower_join(2)
        finish(1, lower_codes[:, chunk_gates[1]])
        store_both(1)
        for c in range(2):
            for n in range(2):
                round_scores(nc.scalar.copy, c, n, banks)
        third_lower = late_lower_codes(2)
        second_upper(2, 3)
        second_upper_pair(2, 0)
        second_upper_pair(2, 1)
        late_lower_join(3)
        join_upper(2)
        last_lower = late_lower_codes(3)
        quantize_y(0, 0)
        finish(2, third_lower)
        store_both(2)
        round_scores(nc.scalar.copy, 2, 1, banks)
        second_upper(3, 2)
        second_upper(3, 3)
        quantize_y(0, 1)
        store_codes(chunk_gates[0])
        join_upper(last)
        quantize_y(1, 0)
        finish(last, last_lower)
        quantize_y(1, 1)

        round_scores(nc.vector.tensor_copy, 2, 0, y)
        for n in range(2):
            quantize_y(2, n)
        store_codes(slice(CHUNK, G - CHUNK))
        copies = (nc.scalar.copy, nc.vector.tensor_copy)
        for n in range(2):
            store_scores(copies[n], last, n, (nc.scalar, nc.sync)[n])
        for n in range(2):
            round_scores(copies[n], last, n, (banks, y)[n])
        for n in range(2):
            quantize_y(last, n)
        store_codes(chunk_gates[last])

        for r in range(ROWS):
            (nc.scalar if r else nc.sync).dma_start(
                out_2[:, r::ROWS, :].rearrange("n q m -> q n m").bitcast(I32),
                y_scales[r:P:QUAD, :, :].bitcast(I32),
            )
